import numpy as np
import ml_dtypes


def mxq(x, axis, fmt="e4m3"):
    dtype, down = {"e4m3": (ml_dtypes.float8_e4m3fn, 7), "e5m2": (ml_dtypes.float8_e5m2, 14)}[fmt]
    v = np.moveaxis(np.asarray(x, np.float32).astype(ml_dtypes.bfloat16).astype(np.float64), axis, -1)
    blocks = v.reshape(v.shape[:-1] + (-1, 32))
    amax = np.abs(blocks).max(-1, keepdims=True)
    byte = np.maximum(np.where(amax > 0, np.frexp(amax)[1] - 1 + 127, 0) - down, 1)
    scale = np.exp2(byte - 127.0)
    codes = (blocks / scale).astype(np.float32).astype(dtype).astype(np.float64)
    return np.moveaxis((codes * scale).reshape(v.shape), -1, axis)


WIDE = False


def mx_kscale(k):
    if not WIDE:
        return np.ones(k)
    levels = np.array([10, -10, 5, -5, 0])
    if k % 512:
        return np.exp2(np.random.permutation(np.resize(levels, k // 32))).repeat(32)
    a = np.empty((k // 512, 16))
    for p in range(k // 512):
        a[p, :8] = np.random.permutation(np.resize(levels, 8))
        for g in range(8):
            far = levels[np.abs(levels - a[p, g]) >= 10]
            a[p, g + 8] = far[np.random.randint(len(far))]
    return np.exp2(a.ravel()).repeat(32)


def f64(x):
    return np.asarray(x).astype(np.float64)


def striped(idx):
    return np.tile(idx.reshape(-1, 16).T, (8, 1)).astype(np.uint16)


def unstriped(offs):
    return offs[:16].T.reshape(-1).astype(np.int64)


def striped8(idx):
    return np.concatenate([x.reshape(-1, 16).T for x in idx]).astype(np.uint16)


def runs(offs, k):
    lists = np.stack([offs[16 * r : 16 * r + 16].T.reshape(-1) for r in range(8)]).astype(np.int64)
    return lists[np.arange(k) % 512 // 64]


def pack_weight(w):
    k, n = w.shape
    w = f64(np.asarray(w, np.float32).astype(ml_dtypes.bfloat16)).reshape(k // 32, 32, n)
    amax = np.abs(w).max(1)
    byte = np.clip(np.where(amax > 0, np.frexp(amax)[1] - 1 + 127 - 7, 1), 1, 254)
    scaled = (w * np.exp2(127.0 - byte)[:, None, :]).reshape(k, n).astype(np.float32)
    words = np.ascontiguousarray(scaled.reshape(k // 512, 128, 4, n).transpose(0, 1, 3, 2)).astype(ml_dtypes.float8_e4m3fn).view(np.uint8)
    return words, np.ascontiguousarray(byte.astype(np.uint8).reshape(k // 512, 16, n))


def unpack_weight(words, scales):
    g, p, n, _ = words.shape
    vals = np.ascontiguousarray(words).view(ml_dtypes.float8_e4m3fn).astype(np.float64) * np.repeat(np.exp2(scales.astype(np.float64) - 127.0), 8, axis=1)[..., None]
    return vals.transpose(0, 1, 3, 2).reshape(g * 512, n)


E2M1 = np.array([0.0, 0.5, 1.0, 1.5, 2.0, 3.0, 4.0, 6.0, -0.0, -0.5, -1.0, -1.5, -2.0, -3.0, -4.0, -6.0])


def pack_fp4(w):
    k, n = w.shape
    w = f64(np.asarray(w, np.float32).astype(ml_dtypes.bfloat16)).reshape(k // 32, 32, n)
    amax = np.abs(w).max(1)
    mant, ex = np.frexp(amax / 6.0)
    byte = np.clip(np.where(amax > 0, np.where(mant > 0.5, ex, ex - 1) + 127, 1), 1, 254)
    scaled = (w * np.exp2(127.0 - byte)[:, None, :]).reshape(k, n).astype(np.float32)
    c = np.ascontiguousarray(scaled.reshape(k // 512, 128, 4, n).transpose(0, 1, 3, 2)).astype(ml_dtypes.float4_e2m1fn).view(np.uint8) & 0xF
    words = (c[..., 0::2] | (c[..., 1::2] << 4)).reshape(k // 512, 128, 2 * n)
    return np.ascontiguousarray(words), np.ascontiguousarray(byte.astype(np.uint8).reshape(k // 512, 16, n))


def unpack_fp4(words, scales):
    g, _, n = scales.shape
    words = np.ascontiguousarray(words).reshape(g, 128, n, 2)
    nib = np.empty((g, 128, n, 4), np.uint8)
    nib[..., 0::2] = words & 0xF
    nib[..., 1::2] = words >> 4
    vals = E2M1[nib] * np.repeat(np.exp2(scales.astype(np.float64) - 127.0), 8, axis=1)[..., None]
    return vals.transpose(0, 1, 3, 2).reshape(g * 512, n)


def relu(v):
    return np.maximum(v, 0.0)

def planes(y):
    n, m = y.shape
    v = y.astype(np.float32).astype(ml_dtypes.bfloat16).astype(np.float64).reshape(n // 32, 32, m)
    top = np.abs(v).max(1)
    byte = np.clip(np.where(top > 0, np.frexp(top)[1] - 1 + 127 - 7, 1), 1, 254)
    codes = (v * np.exp2(127.0 - byte)[:, None, :]).reshape(n, m).astype(np.float32).astype(ml_dtypes.float8_e4m3fn).view(np.uint8)
    words = codes.reshape(n // 512, 128, 4, m).transpose(0, 1, 3, 2)
    return np.ascontiguousarray(words), np.ascontiguousarray(byte.astype(np.uint8).reshape(n // 512, 16, m))


K, T, S, N, H = 1024, 2048, 512, 512, 512


def setup_inputs():
    n = np.random.standard_normal
    s = mx_kscale(K)[:, None]
    u = mx_kscale(H)
    packed_xT = pack_weight(n((K, T)) * s)
    packed_w2 = pack_fp4(n((H, N)) / np.sqrt(H) / u[:, None])
    return {
        "x_words": packed_xT[0],
        "x_scales": packed_xT[1],
        "w1": (n((K, H)) / np.sqrt(K) / s * u).astype(np.float32),
        "w2_words": packed_w2[0],
        "w2_scales": packed_w2[1],
        "offs": striped(np.random.permutation(T)[:S]),
        "p1": striped8(np.stack([np.random.permutation(S) for _ in range(8)])),
        "p2": striped8(np.stack([np.random.permutation(S) for _ in range(8)])),
        "q1": striped8(np.stack([np.random.permutation(S) for _ in range(8)])),
        "q2": striped8(np.stack([np.random.permutation(S) for _ in range(8)])),
    }


def reference(x_words, x_scales, w1, w2_words, w2_scales, offs, p1, p2, q1, q2):
    xq = unpack_weight(x_words, x_scales)[:, unstriped(offs)]
    y = mxq(f64(w1), 0, "e4m3").T @ xq
    h = np.minimum(np.minimum(y, y[np.arange(H)[:, None], runs(p1, H)]), y[np.arange(H)[:, None], runs(p2, H)])
    z = relu(np.maximum(np.maximum(h, h[np.arange(H)[:, None], runs(q1, H)]), h[np.arange(H)[:, None], runs(q2, H)]))
    out_0 = unpack_fp4(w2_words, w2_scales).T @ mxq(z, 0, "e4m3")
    return (out_0,) + planes(out_0)

@@ -1,0 +1,245 @@
+from contextlib import ExitStack
+
+import concourse.mybir as mybir
+
+F32 = mybir.dt.float32
+BF16 = mybir.dt.bfloat16
+I32 = mybir.dt.int32
+U32 = mybir.dt.uint32
+U16 = mybir.dt.uint16
+U8 = mybir.dt.uint8
+FP8X4 = mybir.dt.float8_e4m3fn_x4
+FP4X4 = mybir.dt.float4_e2m1fn_x4
+MIN = mybir.AluOpType.min
+MAX = mybir.AluOpType.max
+RELU = mybir.ActivationFunctionType.Relu
+
+K, T, S, H, N = 1024, 2048, 512, 512, 512
+FLOPS = 2 * K * H * S + 2 * H * N * S
+P = 128
+PACK = 4
+PASSES = K // (P * PACK)
+QUADS = 4
+HALF = S // 2
+CHUNK = 128
+CHUNKS = S // CHUNK
+STRIPE = 16
+
+
+def tile_picked_opening_relu_po_kernel(
+    tc, x_words, x_scales, w1, w2_words, w2_scales, offs, p1, p2, q1, q2, out_0, out_1, out_2
+):
+    nc = tc.nc
+    with ExitStack() as ctx:
+        sb = ctx.enter_context(tc.tile_pool(name="sb", bufs=1))
+        ps = ctx.enter_context(tc.psum_pool(name="ps", bufs=1))
+
+        def tile(shape, dtype, name):
+            return sb.tile(shape, dtype, name=name, align_bytes=64)
+
+        w1_raw = [tile([P, PACK, H], F32, "w1_raw%d" % g) for g in range(PASSES)]
+        x_tab = [tile([P, T], I32, "x_tab%d" % g) for g in range(PASSES)]
+        xs_tab = tile([P, T], U8, "xs_tab")
+        w2_raw = tile([P, 2 * N], U8, "w2_raw")
+        w2s_raw = tile([P, N], U8, "w2s_raw")
+        lists = {}
+        for name in ("offs", "p1", "p2", "q1", "q2"):
+            lists[name] = tile([P, S // STRIPE], U16, "list_" + name)
+
+        nc.gpsimd.memset(xs_tab[:].bitcast(I32), 0)
+        nc.vector.memset(w2s_raw[:].bitcast(I32), 0)
+
+        def load_w1(g):
+            nc.sync.dma_start(
+                out=w1_raw[g][:], in_=w1[512 * g : 512 * (g + 1), :].rearrange("(p j) c -> p j c", j=PACK)
+            )
+
+        load_w1(0)
+        for quad in range(QUADS):
+            nc.sync.dma_start(
+                out=xs_tab[32 * quad : 32 * quad + 4 * PASSES, :].bitcast(I32),
+                in_=x_scales[:, 4 * quad : 4 * quad + 4, :].bitcast(I32),
+            )
+        load_w1(1)
+        nc.sync.dma_start(out=lists["offs"][:], in_=offs)
+        for g in range(PASSES):
+            nc.sync.dma_start(out=x_tab[g][:], in_=x_words[g].rearrange("p c r -> p (c r)").bitcast(I32))
+        nc.sync.dma_start(out=lists["p1"][:], in_=p1)
+        nc.sync.dma_start(out=lists["p2"][:], in_=p2)
+        nc.sync.dma_start(out=w2_raw[:].bitcast(I32), in_=w2_words[0].bitcast(I32))
+        for quad in range(QUADS):
+            nc.sync.dma_start(
+                out=w2s_raw[32 * quad : 32 * quad + 4, :].bitcast(I32),
+                in_=w2_scales[0, 4 * quad : 4 * quad + 4, :].bitcast(I32),
+            )
+        nc.sync.dma_start(out=lists["q1"][:], in_=q1)
+        nc.sync.dma_start(out=lists["q2"][:], in_=q2)
+
+        w1_bf = [tile([P, PACK * H], BF16, "w1_bf%d" % g) for g in range(PASSES)]
+        w1_codes = [tile([P, H], U32, "w1_codes%d" % g) for g in range(PASSES)]
+        w1_sc = [tile([P, H], U8, "w1_sc%d" % g) for g in range(PASSES)]
+
+        def dealt(g):
+            return dict(
+                out=w1_bf[g][:].rearrange("p (t m j) -> p m j t", t=PACK, j=PACK),
+                in_=w1_raw[g][:].rearrange("p j (m t) -> p m j t", t=PACK),
+            )
+
+        def quantise_w1(g):
+            nc.vector.quantize_mx(out=w1_codes[g][:].bitcast(FP8X4), scales=w1_sc[g][:], in_=w1_bf[g][:])
+
+        x_codes = [tile([P, S], U32, "x_codes%d" % g) for g in range(PASSES)]
+        x_sc = tile([P, S], U8, "x_sc")
+
+        def gather_words(g, first, count):
+            picks = lists["offs"][:, first // STRIPE : (first + count) // STRIPE]
+            nc.vector.tensor_copy(x_codes[g][:, first : first + count], x_tab[g][:].bitcast(U32).indirect(picks))
+
+        nc.scalar.copy(**dealt(0))
+        nc.vector.tensor_copy(x_sc[:], xs_tab[:].indirect(lists["offs"][:]))
+        nc.vector.tensor_copy(**dealt(1))
+        quantise_w1(0)
+        quantise_w1(1)
+        gather_words(0, 0, S)
+        gather_words(1, 0, HALF)
+        gather_words(1, HALF, HALF)
+
+        pieces = [(0, 0, HALF), (0, HALF, HALF)] + [(t, 0, S) for t in range(1, PACK)]
+        y_ps = [ps.tile([P, count], F32, name="y_ps%d" % i, tag="bank%d" % i) for i, (t, first, count) in enumerate(pieces)]
+        for g in range(PASSES):
+            for i, (t, first, count) in enumerate(pieces):
+                cols = slice(P * t, P * (t + 1))
+                nc.tensor.matmul_mx(
+                    out=y_ps[i][:],
+                    lhsT=w1_codes[g][:, cols].bitcast(FP8X4),
+                    lhsT_scale=w1_sc[g][:, cols],
+                    rhs=x_codes[g][:, first : first + count].bitcast(FP8X4),
+                    rhs_scale=x_sc[4 * g : P, first : first + count],
+                    start=(g == 0),
+                    stop=(g == PASSES - 1),
+                )
+
+        w2_dealt = tile([P, 2 * N], U8, "w2_dealt")
+        w2s_dealt = tile([P, N], U8, "w2s_dealt")
+        nc.vector.tensor_copy(
+            out=w2_dealt[:].rearrange("p (t m b) -> p m t b", t=PACK, b=2),
+            in_=w2_raw[:].rearrange("p (m t b) -> p m t b", t=PACK, b=2),
+        )
+        nc.vector.tensor_copy(
+            out=w2s_dealt[:].rearrange("p (t m) -> p m t", t=PACK),
+            in_=w2s_raw[:].rearrange("p (m t) -> p m t", t=PACK),
+        )
+
+        y = [tile([P, S], F32, "y%d" % t) for t in range(PACK)]
+        h = [tile([P, S], F32, "h%d" % t) for t in range(PACK)]
+        near1 = [tile([P, S], F32, "near1_%d" % t) for t in range(PACK)]
+        near2 = [tile([P, S], F32, "near2_%d" % t) for t in range(PACK)]
+        low = [tile([P, S], F32, "low%d" % t) for t in range(PACK)]
+        h_bf = tile([P, PACK, S], BF16, "h_bf")
+        for i, (t, first, count) in enumerate(pieces):
+            nc.scalar.activation(y[t][:, first : first + count], y_ps[i][:], RELU)
+
+        def fetch(dst, window, name, first, count):
+            nc.vector.tensor_copy(
+                dst, window[:].indirect(lists[name][:, first // STRIPE : (first + count) // STRIPE])
+            )
+
+        def fetch_row(dst, window, name):
+            for first in range(0, S, HALF):
+                fetch(dst[:, first : first + HALF], window, name, first, HALF)
+
+        def finish_h(t):
+            nc.vector.tensor_tensor(h[t][:], low[t][:], near2[t][:], MIN)
+            nc.scalar.copy(out=h_bf[:, t, :], in_=h[t][:])
+
+        for t in range(PACK):
+            fetch_row(near1[t], y[t], "p1")
+            if t > 0:
+                finish_h(t - 1)
+            fetch_row(near2[t], y[t], "p2")
+            nc.vector.tensor_tensor(low[t][:], near1[t][:], y[t][:], MIN)
+
+        spans = [(0, 2 * CHUNK), (2 * CHUNK, CHUNK), (3 * CHUNK, CHUNK)]
+        far1 = [tile([P, PACK, n], BF16, "far1_%d" % c) for c, n in spans]
+        far2 = [tile([P, PACK, n], BF16, "far2_%d" % c) for c, n in spans]
+        high = [tile([P, PACK, n], BF16, "high%d" % c) for c, n in spans]
+        mid = [tile([P, PACK * n], BF16, "mid%d" % c) for c, n in spans]
+        z_bf = [tile([P, PACK * n], BF16, "z_bf%d" % c) for c, n in spans]
+        z_codes = [tile([P, n], U32, "z_codes%d" % c) for c, n in spans]
+        z_sc = [tile([P, n], U8, "z_sc%d" % c) for c, n in spans]
+        o_f32 = [tile([P, PACK, CHUNK], F32, "o_f32_%d" % c) for c in range(CHUNKS)]
+        o_bf = [tile([P, PACK * n], BF16, "o_bf%d" % c) for c, n in spans]
+        o_codes = [tile([P, n], U32, "o_codes%d" % c) for c, n in spans]
+        o_sc = tile([P, S], U8, "o_sc")
+        out_rows = out_0.rearrange("(p t) j -> p t j", t=PACK)
+        out_words = out_1[0].rearrange("p c r -> p (c r)").bitcast(I32)
+        last = len(spans) - 1
+
+        def woven(ap):
+            return ap.rearrange("p (n i t) -> p n t i", i=4, t=PACK)
+
+        def planar(ap):
+            return ap.rearrange("p t (n i) -> p n t i", i=4)
+
+        def second_product(c):
+            first, count = spans[c]
+            nc.vector.quantize_mx(out=z_codes[c][:].bitcast(FP8X4), scales=z_sc[c][:], in_=z_bf[c][:])
+            for lo in range(0, count, CHUNK):
+                unit = (first + lo) // CHUNK
+                o_ps = ps.tile([P, PACK, CHUNK], F32, name="o_ps%d" % unit, tag="bank%d" % (5 + unit % 3))
+                for t in range(PACK):
+                    nc.tensor.matmul_mx(
+                        out=o_ps[:, t, :],
+                        lhsT=w2_dealt[:, 2 * P * t : 2 * P * (t + 1)].bitcast(FP4X4),
+                        lhsT_scale=w2s_dealt[:, P * t : P * (t + 1)],
+                        rhs=z_codes[c][:, lo : lo + CHUNK].bitcast(FP8X4),
+                        rhs_scale=z_sc[c][:, lo : lo + CHUNK],
+                        start=True,
+                        stop=True,
+                    )
+                rounded = woven(o_bf[c][:, PACK * lo : PACK * (lo + CHUNK)])
+                if c == last:
+                    nc.vector.tensor_copy(out=rounded, in_=planar(o_ps[:]))
+                else:
+                    nc.scalar.copy(out=rounded, in_=planar(o_ps[:]))
+                nc.scalar.copy(out=o_f32[unit][:], in_=o_ps[:])
+                nc.sync.dma_start(out=out_rows[:, :, first + lo : first + lo + CHUNK], in_=o_f32[unit][:])
+
+        def planes(c):
+            first, count = spans[c]
+            cols = slice(first, first + count)
+            nc.vector.quantize_mx(out=o_codes[c][:].bitcast(FP8X4), scales=o_sc[:, cols], in_=o_bf[c][:])
+            nc.sync.dma_start(out=out_words[:, cols], in_=o_codes[c][:].bitcast(I32))
+
+        for c, (first, count) in enumerate(spans):
+            for t in range(PACK):
+                if c == 0 and t == 1:
+                    finish_h(PACK - 1)
+                fetch(far1[c][:, t, :], h[t], "q1", first, count)
+            fetch(far2[c][:, 0, :], h[0], "q2", first, count)
+            nc.vector.tensor_tensor(high[c][:], far1[c][:], h_bf[:, :, first : first + count], MAX)
+            if c == last:
+                nc.scalar.copy(out=woven(mid[c][:]), in_=planar(high[c][:]))
+            fetch(far2[c][:, 1, :], h[1], "q2", first, count)
+            if c > 0:
+                second_product(c - 1)
+            for t in range(2, PACK):
+                fetch(far2[c][:, t, :], h[t], "q2", first, count)
+            if c > 1:
+                planes(c - 2)
+            if c == last:
+                nc.vector.tensor_tensor(woven(z_bf[c][:]), planar(far2[c][:]), woven(mid[c][:]), MAX)
+            else:
+                nc.vector.tensor_tensor(
+                    mid[c][:], far2[c][:].rearrange("p t n -> p (t n)"), high[c][:].rearrange("p t n -> p (t n)"), MAX
+                )
+                nc.scalar.copy(out=woven(z_bf[c][:]), in_=planar(mid[c][:].rearrange("p (t n) -> p t n", t=PACK)))
+        second_product(last)
+        planes(last - 1)
+        planes(last)
+        for quad in range(QUADS):
+            queue = nc.scalar if quad % 2 else nc.sync
+            queue.dma_start(
+                out=out_2[0, 4 * quad : 4 * quad + 4, :].bitcast(I32),
+                in_=o_sc[32 * quad : 32 * quad + 4, :].bitcast(I32),
+            )

@@ -34,8 +34,8 @@ def tile_picked_opening_relu_po_kernel(
         sb = ctx.enter_context(tc.tile_pool(name="sb", bufs=1))
         ps = ctx.enter_context(tc.psum_pool(name="ps", bufs=1))
 
-        def tile(shape, dtype, name):
-            return sb.tile(shape, dtype, name=name, align_bytes=64)
+        def tile(shape, dtype, name, tag=None):
+            return sb.tile(shape, dtype, name=name, tag=tag or name, align_bytes=64)
 
         w1_raw = [tile([P, PACK, H], F32, "w1_raw%d" % g) for g in range(PASSES)]
         x_tab = [tile([P, T], I32, "x_tab%d" % g) for g in range(PASSES)]
@@ -54,6 +54,7 @@ def tile_picked_opening_relu_po_kernel(
                 out=w1_raw[g][:], in_=w1[512 * g : 512 * (g + 1), :].rearrange("(p j) c -> p j c", j=PACK)
             )
 
+        nc.sync.dma_start(out=lists["offs"][:], in_=offs)
         load_w1(0)
         for quad in range(QUADS):
             nc.sync.dma_start(
@@ -61,7 +62,6 @@ def tile_picked_opening_relu_po_kernel(
                 in_=x_scales[:, 4 * quad : 4 * quad + 4, :].bitcast(I32),
             )
         load_w1(1)
-        nc.sync.dma_start(out=lists["offs"][:], in_=offs)
         for g in range(PASSES):
             nc.sync.dma_start(out=x_tab[g][:], in_=x_words[g].rearrange("p c r -> p (c r)").bitcast(I32))
         nc.sync.dma_start(out=lists["p1"][:], in_=p1)
@@ -79,10 +79,10 @@ def tile_picked_opening_relu_po_kernel(
         w1_codes = [tile([P, H], U32, "w1_codes%d" % g) for g in range(PASSES)]
         w1_sc = [tile([P, H], U8, "w1_sc%d" % g) for g in range(PASSES)]
 
-        def dealt(g):
+        def dealt(g, lo, hi):
             return dict(
-                out=w1_bf[g][:].rearrange("p (t m j) -> p m j t", t=PACK, j=PACK),
-                in_=w1_raw[g][:].rearrange("p j (m t) -> p m j t", t=PACK),
+                out=w1_bf[g][:].rearrange("p (t m j) -> p m j t", t=PACK, j=PACK)[:, lo:hi],
+                in_=w1_raw[g][:].rearrange("p j (m t) -> p m j t", t=PACK)[:, lo:hi],
             )
 
         def quantise_w1(g):
@@ -95,10 +95,11 @@ def tile_picked_opening_relu_po_kernel(
             picks = lists["offs"][:, first // STRIPE : (first + count) // STRIPE]
             nc.vector.tensor_copy(x_codes[g][:, first : first + count], x_tab[g][:].bitcast(U32).indirect(picks))
 
-        nc.scalar.copy(**dealt(0))
+        nc.vector.tensor_copy(**dealt(0, 0, P))
         nc.vector.tensor_copy(x_sc[:], xs_tab[:].indirect(lists["offs"][:]))
-        nc.vector.tensor_copy(**dealt(1))
         quantise_w1(0)
+        nc.scalar.copy(**dealt(1, 0, P // 2))
+        nc.vector.tensor_copy(**dealt(1, P // 2, P))
         quantise_w1(1)
         gather_words(0, 0, S)
         gather_words(1, 0, HALF)
@@ -130,12 +131,15 @@ def tile_picked_opening_relu_po_kernel(
             in_=w2s_raw[:].rearrange("p (m t) -> p m t", t=PACK),
         )
 
-        y = [tile([P, S], F32, "y%d" % t) for t in range(PACK)]
+        y_win = [tile([P, S if t == 0 else 2 * S], F32, "y%d" % t) for t in range(PACK)]
+        y = [y_win[t][:, 0:S] for t in range(PACK)]
+        near1 = [y_win[t + 1][:, S : 2 * S] for t in range(PACK - 1)] + [tile([P, S], F32, "near1_last")[:]]
         h = [tile([P, S], F32, "h%d" % t) for t in range(PACK)]
-        near1 = [tile([P, S], F32, "near1_%d" % t) for t in range(PACK)]
         near2 = [tile([P, S], F32, "near2_%d" % t) for t in range(PACK)]
         low = [tile([P, S], F32, "low%d" % t) for t in range(PACK)]
         h_bf = tile([P, PACK, S], BF16, "h_bf")
+        far1 = [tile([P, PACK, HALF], BF16, "far1_%d" % half, tag="far1") for half in range(2)]
+        high = [tile([P, PACK, HALF], BF16, "high%d" % half) for half in range(2)]
         for i, (t, first, count) in enumerate(pieces):
             nc.scalar.activation(y[t][:, first : first + count], y_ps[i][:], RELU)
 
@@ -145,30 +149,40 @@ def tile_picked_opening_relu_po_kernel(
             )
 
         def fetch_row(dst, window, name):
-            for first in range(0, S, HALF):
-                fetch(dst[:, first : first + HALF], window, name, first, HALF)
+            step = window.shape[1] // 2
+            for first in range(0, S, step):
+                fetch(dst[:, first : first + step], window, name, first, step)
 
         def finish_h(t):
             nc.vector.tensor_tensor(h[t][:], low[t][:], near2[t][:], MIN)
             nc.scalar.copy(out=h_bf[:, t, :], in_=h[t][:])
 
-        for t in range(PACK):
-            fetch_row(near1[t], y[t], "p1")
+        def fetch_far1(t, half):
+            fetch(far1[half][:, t, :], h[t], "q1", half * HALF, HALF)
+
+        def raise_h(half):
+            nc.vector.tensor_tensor(high[half][:], far1[half][:], h_bf[:, :, half * HALF : (half + 1) * HALF], MAX)
+
+        for t in range(PACK + 1):
+            if t < PACK:
+                fetch_row(near1[t], y_win[t], "p1")
             if t > 0:
                 finish_h(t - 1)
-            fetch_row(near2[t], y[t], "p2")
-            nc.vector.tensor_tensor(low[t][:], near1[t][:], y[t][:], MIN)
+            if t < PACK:
+                fetch_row(near2[t][:], y_win[t], "p2")
+                if t > 0:
+                    fetch_far1(t - 1, 0)
+                nc.vector.tensor_tensor(low[t][:], near1[t], y[t], MIN)
 
         spans = [(0, 2 * CHUNK), (2 * CHUNK, CHUNK), (3 * CHUNK, CHUNK)]
-        far1 = [tile([P, PACK, n], BF16, "far1_%d" % c) for c, n in spans]
-        far2 = [tile([P, PACK, n], BF16, "far2_%d" % c) for c, n in spans]
-        high = [tile([P, PACK, n], BF16, "high%d" % c) for c, n in spans]
-        mid = [tile([P, PACK * n], BF16, "mid%d" % c) for c, n in spans]
+        mid = [tile([P, PACK, n], BF16, "mid%d" % c, tag="held" if c == 0 else None) for c, n in spans]
+        far2_late = tile([P, 2, PACK, CHUNK], BF16, "far2_late", tag="held")
+        far2 = [tile([P, PACK, HALF], BF16, "far2_first"), far2_late[:, 0], far2_late[:, 1]]
         z_bf = [tile([P, PACK * n], BF16, "z_bf%d" % c) for c, n in spans]
+        o_bf = [tile([P, PACK * n], BF16, "o_bf%d" % c) for c, n in spans]
         z_codes = [tile([P, n], U32, "z_codes%d" % c) for c, n in spans]
         z_sc = [tile([P, n], U8, "z_sc%d" % c) for c, n in spans]
         o_f32 = [tile([P, PACK, CHUNK], F32, "o_f32_%d" % c) for c in range(CHUNKS)]
-        o_bf = [tile([P, PACK * n], BF16, "o_bf%d" % c) for c, n in spans]
         o_codes = [tile([P, n], U32, "o_codes%d" % c) for c, n in spans]
         o_sc = tile([P, S], U8, "o_sc")
         out_rows = out_0.rearrange("(p t) j -> p t j", t=PACK)
@@ -181,29 +195,36 @@ def tile_picked_opening_relu_po_kernel(
         def planar(ap):
             return ap.rearrange("p t (n i) -> p n t i", i=4)
 
+        def woven8(ap):
+            return ap.rearrange("p (n i t) -> p n t i", i=8, t=PACK)
+
+        def planar8(ap):
+            return ap.rearrange("p t (n i) -> p n t i", i=8)
+
+        def product(out, t, c, lo):
+            nc.tensor.matmul_mx(
+                out=out,
+                lhsT=w2_dealt[:, 2 * P * t : 2 * P * (t + 1)].bitcast(FP4X4),
+                lhsT_scale=w2s_dealt[:, P * t : P * (t + 1)],
+                rhs=z_codes[c][:, lo : lo + CHUNK].bitcast(FP8X4),
+                rhs_scale=z_sc[c][:, lo : lo + CHUNK],
+                start=True,
+                stop=True,
+            )
+
         def second_product(c):
             first, count = spans[c]
             nc.vector.quantize_mx(out=z_codes[c][:].bitcast(FP8X4), scales=z_sc[c][:], in_=z_bf[c][:])
             for lo in range(0, count, CHUNK):
                 unit = (first + lo) // CHUNK
-                o_ps = ps.tile([P, PACK, CHUNK], F32, name="o_ps%d" % unit, tag="bank%d" % (5 + unit % 3))
-                for t in range(PACK):
-                    nc.tensor.matmul_mx(
-                        out=o_ps[:, t, :],
-                        lhsT=w2_dealt[:, 2 * P * t : 2 * P * (t + 1)].bitcast(FP4X4),
-                        lhsT_scale=w2s_dealt[:, P * t : P * (t + 1)],
-                        rhs=z_codes[c][:, lo : lo + CHUNK].bitcast(FP8X4),
-                        rhs_scale=z_sc[c][:, lo : lo + CHUNK],
-                        start=True,
-                        stop=True,
-                    )
                 rounded = woven(o_bf[c][:, PACK * lo : PACK * (lo + CHUNK)])
-                if c == last:
-                    nc.vector.tensor_copy(out=rounded, in_=planar(o_ps[:]))
-                else:
-                    nc.scalar.copy(out=rounded, in_=planar(o_ps[:]))
+                cols = slice(first + lo, first + lo + CHUNK)
+                o_ps = ps.tile([P, PACK, CHUNK], F32, name="o_ps%d" % unit, tag="bank%d" % (4 + unit))
+                for t in range(PACK):
+                    product(o_ps[:, t, :], t, c, lo)
+                nc.scalar.copy(out=rounded, in_=planar(o_ps[:]))
                 nc.scalar.copy(out=o_f32[unit][:], in_=o_ps[:])
-                nc.sync.dma_start(out=out_rows[:, :, first + lo : first + lo + CHUNK], in_=o_f32[unit][:])
+                nc.sync.dma_start(out=out_rows[:, :, cols], in_=o_f32[unit][:])
 
         def planes(c):
             first, count = spans[c]
@@ -211,31 +232,44 @@ def tile_picked_opening_relu_po_kernel(
             nc.vector.quantize_mx(out=o_codes[c][:].bitcast(FP8X4), scales=o_sc[:, cols], in_=o_bf[c][:])
             nc.sync.dma_start(out=out_words[:, cols], in_=o_codes[c][:].bitcast(I32))
 
-        for c, (first, count) in enumerate(spans):
-            for t in range(PACK):
-                if c == 0 and t == 1:
-                    finish_h(PACK - 1)
-                fetch(far1[c][:, t, :], h[t], "q1", first, count)
-            fetch(far2[c][:, 0, :], h[0], "q2", first, count)
-            nc.vector.tensor_tensor(high[c][:], far1[c][:], h_bf[:, :, first : first + count], MAX)
-            if c == last:
-                nc.scalar.copy(out=woven(mid[c][:]), in_=planar(high[c][:]))
-            fetch(far2[c][:, 1, :], h[1], "q2", first, count)
-            if c > 0:
-                second_product(c - 1)
-            for t in range(2, PACK):
-                fetch(far2[c][:, t, :], h[t], "q2", first, count)
-            if c > 1:
-                planes(c - 2)
-            if c == last:
-                nc.vector.tensor_tensor(woven(z_bf[c][:]), planar(far2[c][:]), woven(mid[c][:]), MAX)
-            else:
-                nc.vector.tensor_tensor(
-                    mid[c][:], far2[c][:].rearrange("p t n -> p (t n)"), high[c][:].rearrange("p t n -> p (t n)"), MAX
-                )
-                nc.scalar.copy(out=woven(z_bf[c][:]), in_=planar(mid[c][:].rearrange("p (t n) -> p t n", t=PACK)))
+        def fetch_far2(c, t):
+            first, count = spans[c]
+            fetch(far2[c][:, t, :], h[t], "q2", first, count)
+
+        def largest(c):
+            first, count = spans[c]
+            lo = first % HALF
+            nc.vector.tensor_tensor(mid[c][:], far2[c][:], high[first // HALF][:, :, lo : lo + count], MAX)
+
+        def weave(c, copy):
+            copy(out=woven8(z_bf[c][:]), in_=planar8(mid[c][:]))
+
+        fetch_far2(0, 0)
+        fetch_far1(PACK - 1, 0)
+        fetch_far2(0, 1)
+        fetch_far2(0, 2)
+        raise_h(0)
+        fetch_far2(0, 3)
+        largest(0)
+        weave(0, nc.scalar.copy)
+        for t in range(PACK):
+            fetch_far1(t, 1)
+        second_product(0)
+        raise_h(1)
+        for t in range(PACK):
+            fetch_far2(1, t)
+        fetch_far2(2, 0)
+        largest(1)
+        fetch_far2(2, 1)
+        weave(1, nc.vector.tensor_copy)
+        fetch_far2(2, 2)
+        second_product(1)
+        fetch_far2(2, 3)
+        planes(0)
+        largest(2)
+        weave(2, nc.vector.tensor_copy)
+        planes(1)
         second_product(last)
-        planes(last - 1)
         planes(last)
         for quad in range(QUADS):
             queue = nc.scalar if quad % 2 else nc.sync

@@ -1,6 +1,7 @@
 from contextlib import ExitStack
 
 import concourse.mybir as mybir
+from concourse.masks import make_identity
 
 F32 = mybir.dt.float32
 BF16 = mybir.dt.bfloat16
@@ -10,9 +11,11 @@ U16 = mybir.dt.uint16
 U8 = mybir.dt.uint8
 FP8X4 = mybir.dt.float8_e4m3fn_x4
 FP4X4 = mybir.dt.float4_e2m1fn_x4
-MIN = mybir.AluOpType.min
 MAX = mybir.AluOpType.max
+MULT = mybir.AluOpType.mult
+ADD = mybir.AluOpType.add
 RELU = mybir.ActivationFunctionType.Relu
+COPY = mybir.ActivationFunctionType.Copy
 
 K, T, S, H, N = 1024, 2048, 512, 512, 512
 FLOPS = 2 * K * H * S + 2 * H * N * S
@@ -24,6 +27,8 @@ HALF = S // 2
 CHUNK = 128
 CHUNKS = S // CHUNK
 STRIPE = 16
+TURNED = 3
+MIN = mybir.AluOpType.min
 
 
 def tile_picked_opening_relu_po_kernel(
@@ -48,6 +53,8 @@ def tile_picked_opening_relu_po_kernel(
 
         nc.gpsimd.memset(xs_tab[:].bitcast(I32), 0)
         nc.vector.memset(w2s_raw[:].bitcast(I32), 0)
+        ident = tile([P, P], F32, "ident")
+        make_identity(nc, ident[:])
 
         def load_w1(g):
             nc.sync.dma_start(
@@ -153,9 +160,39 @@ def tile_picked_opening_relu_po_kernel(
             for first in range(0, S, step):
                 fetch(dst[:, first : first + step], window, name, first, step)
 
+        def fetch_row_negated(dst, window, name):
+            step = window.shape[1] // 2
+            for first in range(0, S, step):
+                picks = lists[name][:, first // STRIPE : (first + step) // STRIPE]
+                nc.vector.tensor_scalar(dst[:, first : first + step], window[:].indirect(picks), -1.0, 0.0, MULT, ADD)
+
+        def turned_sum(terms, name, bank):
+            acc = ps.tile([P, S], F32, name=name, tag=bank)
+            for i, term in enumerate(terms):
+                for lo in range(0, S, P):
+                    nc.tensor.matmul(
+                        out=acc[:, lo : lo + P],
+                        lhsT=term[:, lo : lo + P],
+                        rhs=ident[:],
+                        start=(i == 0 and lo == 0),
+                        stop=(i == len(terms) - 1 and lo == S - P),
+                        is_transpose=True,
+                    )
+            return acc
+
+        y_neg_turned = [tile([P, S], F32, "y_neg_turned%d" % t) for t in range(TURNED)]
+        excess = [tile([P, S], F32, "excess%d" % t) for t in range(TURNED)]
+        for t in range(TURNED):
+            acc = turned_sum([y[t]], "y_turned%d" % t, "bank%d" % (5 + t % 2))
+            nc.scalar.activation(y_neg_turned[t][:], acc[:], COPY, scale=-1.0)
+
         def finish_h(t):
-            nc.vector.tensor_tensor(h[t][:], low[t][:], near2[t][:], MIN)
-            nc.scalar.copy(out=h_bf[:, t, :], in_=h[t][:])
+            nc.vector.scalar_tensor_tensor(low[t][:], near1[t], -1.0, near2[t][:], MULT, MAX)
+            acc = turned_sum([y[t], low[t]], "gap%d" % t, "bank%d" % (t % 2))
+            nc.scalar.activation(excess[t][:], acc[:], RELU)
+            acc = turned_sum([y_neg_turned[t], excess[t]], "h_neg%d" % t, "bank%d" % (2 + t % 2))
+            nc.scalar.activation(h[t][:], acc[:], COPY, scale=-1.0)
+            nc.scalar.activation(h_bf[:, t, :], acc[:], COPY, scale=-1.0)
 
         def fetch_far1(t, half):
             fetch(far1[half][:, t, :], h[t], "q1", half * HALF, HALF)
@@ -163,16 +200,19 @@ def tile_picked_opening_relu_po_kernel(
         def raise_h(half):
             nc.vector.tensor_tensor(high[half][:], far1[half][:], h_bf[:, :, half * HALF : (half + 1) * HALF], MAX)
 
-        for t in range(PACK + 1):
-            if t < PACK:
-                fetch_row(near1[t], y_win[t], "p1")
+        for t in range(PACK):
+            fetch_row(near1[t], y_win[t], "p1")
             if t > 0:
                 finish_h(t - 1)
-            if t < PACK:
+            if t < TURNED:
+                fetch_row_negated(near2[t][:], y_win[t], "p2")
+            else:
                 fetch_row(near2[t][:], y_win[t], "p2")
-                if t > 0:
-                    fetch_far1(t - 1, 0)
-                nc.vector.tensor_tensor(low[t][:], near1[t], y[t], MIN)
+        t = PACK - 1
+        nc.vector.tensor_tensor(low[t][:], near1[t], y[t], MIN)
+        fetch_far1(0, 0)
+        nc.vector.tensor_tensor(h[t][:], low[t][:], near2[t][:], MIN)
+        nc.scalar.copy(out=h_bf[:, t, :], in_=h[t][:])
 
         spans = [(0, 2 * CHUNK), (2 * CHUNK, CHUNK), (3 * CHUNK, CHUNK)]
         mid = [tile([P, PACK, n], BF16, "mid%d" % c, tag="held" if c == 0 else None) for c, n in spans]
@@ -222,7 +262,10 @@ def tile_picked_opening_relu_po_kernel(
                 o_ps = ps.tile([P, PACK, CHUNK], F32, name="o_ps%d" % unit, tag="bank%d" % (4 + unit))
                 for t in range(PACK):
                     product(o_ps[:, t, :], t, c, lo)
-                nc.scalar.copy(out=rounded, in_=planar(o_ps[:]))
+                if c == last:
+                    nc.vector.tensor_copy(out=rounded, in_=planar(o_ps[:]))
+                else:
+                    nc.scalar.copy(out=rounded, in_=planar(o_ps[:]))
                 nc.scalar.copy(out=o_f32[unit][:], in_=o_ps[:])
                 nc.sync.dma_start(out=out_rows[:, :, cols], in_=o_f32[unit][:])
 
@@ -245,11 +288,10 @@ def tile_picked_opening_relu_po_kernel(
             copy(out=woven8(z_bf[c][:]), in_=planar8(mid[c][:]))
 
         fetch_far2(0, 0)
-        fetch_far1(PACK - 1, 0)
-        fetch_far2(0, 1)
-        fetch_far2(0, 2)
+        for t in (1, 3, 2):
+            fetch_far1(t, 0)
+            fetch_far2(0, t)
         raise_h(0)
-        fetch_far2(0, 3)
         largest(0)
         weave(0, nc.scalar.copy)
         for t in range(PACK):

@@ -12,8 +12,6 @@ U8 = mybir.dt.uint8
 FP8X4 = mybir.dt.float8_e4m3fn_x4
 FP4X4 = mybir.dt.float4_e2m1fn_x4
 MAX = mybir.AluOpType.max
-MULT = mybir.AluOpType.mult
-ADD = mybir.AluOpType.add
 RELU = mybir.ActivationFunctionType.Relu
 COPY = mybir.ActivationFunctionType.Copy
 
@@ -27,7 +25,7 @@ HALF = S // 2
 CHUNK = 128
 CHUNKS = S // CHUNK
 STRIPE = 16
-TURNED = 3
+TURNED = 2
 MIN = mybir.AluOpType.min
 
 
@@ -160,12 +158,6 @@ def tile_picked_opening_relu_po_kernel(
             for first in range(0, S, step):
                 fetch(dst[:, first : first + step], window, name, first, step)
 
-        def fetch_row_negated(dst, window, name):
-            step = window.shape[1] // 2
-            for first in range(0, S, step):
-                picks = lists[name][:, first // STRIPE : (first + step) // STRIPE]
-                nc.vector.tensor_scalar(dst[:, first : first + step], window[:].indirect(picks), -1.0, 0.0, MULT, ADD)
-
         def turned_sum(terms, name, bank):
             acc = ps.tile([P, S], F32, name=name, tag=bank)
             for i, term in enumerate(terms):
@@ -182,14 +174,16 @@ def tile_picked_opening_relu_po_kernel(
 
         y_neg_turned = [tile([P, S], F32, "y_neg_turned%d" % t) for t in range(TURNED)]
         excess = [tile([P, S], F32, "excess%d" % t) for t in range(TURNED)]
+        y_neg = [tile([P, S], F32, "y_neg%d" % t) for t in range(TURNED)]
         for t in range(TURNED):
+            nc.scalar.activation(y_neg[t][:], y[t], COPY, scale=-1.0)
             acc = turned_sum([y[t]], "y_turned%d" % t, "bank%d" % (5 + t % 2))
             nc.scalar.activation(y_neg_turned[t][:], acc[:], COPY, scale=-1.0)
 
         def finish_h(t):
-            nc.vector.scalar_tensor_tensor(low[t][:], near1[t], -1.0, near2[t][:], MULT, MAX)
-            acc = turned_sum([y[t], low[t]], "gap%d" % t, "bank%d" % (t % 2))
-            nc.scalar.activation(excess[t][:], acc[:], RELU)
+            nc.vector.tensor_tensor(low[t][:], near1[t], near2[t][:], MIN)
+            acc = turned_sum([y_neg[t], low[t]], "gap%d" % t, "bank%d" % (t % 2))
+            nc.scalar.activation(excess[t][:], acc[:], RELU, scale=-1.0)
             acc = turned_sum([y_neg_turned[t], excess[t]], "h_neg%d" % t, "bank%d" % (2 + t % 2))
             nc.scalar.activation(h[t][:], acc[:], COPY, scale=-1.0)
             nc.scalar.activation(h_bf[:, t, :], acc[:], COPY, scale=-1.0)
@@ -200,19 +194,21 @@ def tile_picked_opening_relu_po_kernel(
         def raise_h(half):
             nc.vector.tensor_tensor(high[half][:], far1[half][:], h_bf[:, :, half * HALF : (half + 1) * HALF], MAX)
 
+        def finish_h_here(t):
+            nc.vector.tensor_tensor(h[t][:], low[t][:], near2[t][:], MIN)
+            nc.scalar.copy(out=h_bf[:, t, :], in_=h[t][:])
+
         for t in range(PACK):
             fetch_row(near1[t], y_win[t], "p1")
-            if t > 0:
+            if 0 < t <= TURNED:
                 finish_h(t - 1)
-            if t < TURNED:
-                fetch_row_negated(near2[t][:], y_win[t], "p2")
-            else:
-                fetch_row(near2[t][:], y_win[t], "p2")
-        t = PACK - 1
-        nc.vector.tensor_tensor(low[t][:], near1[t], y[t], MIN)
+            elif t > 0:
+                finish_h_here(t - 1)
+            fetch_row(near2[t][:], y_win[t], "p2")
+            if t >= TURNED:
+                nc.vector.tensor_tensor(low[t][:], near1[t], y[t], MIN)
         fetch_far1(0, 0)
-        nc.vector.tensor_tensor(h[t][:], low[t][:], near2[t][:], MIN)
-        nc.scalar.copy(out=h_bf[:, t, :], in_=h[t][:])
+        finish_h_here(PACK - 1)
 
         spans = [(0, 2 * CHUNK), (2 * CHUNK, CHUNK), (3 * CHUNK, CHUNK)]
         mid = [tile([P, PACK, n], BF16, "mid%d" % c, tag="held" if c == 0 else None) for c, n in spans]
@@ -288,7 +284,7 @@ def tile_picked_opening_relu_po_kernel(
             copy(out=woven8(z_bf[c][:]), in_=planar8(mid[c][:]))
 
         fetch_far2(0, 0)
-        for t in (1, 3, 2):
+        for t in range(1, PACK):
             fetch_far1(t, 0)
             fetch_far2(0, t)
         raise_h(0)

@@ -13,7 +13,6 @@ FP8X4 = mybir.dt.float8_e4m3fn_x4
 FP4X4 = mybir.dt.float4_e2m1fn_x4
 MAX = mybir.AluOpType.max
 RELU = mybir.ActivationFunctionType.Relu
-COPY = mybir.ActivationFunctionType.Copy
 
 K, T, S, H, N = 1024, 2048, 512, 512, 512
 FLOPS = 2 * K * H * S + 2 * H * N * S
@@ -25,8 +24,8 @@ HALF = S // 2
 CHUNK = 128
 CHUNKS = S // CHUNK
 STRIPE = 16
-TURNED = 2
 MIN = mybir.AluOpType.min
+SUB = mybir.AluOpType.subtract
 
 
 def tile_picked_opening_relu_po_kernel(
@@ -67,11 +66,11 @@ def tile_picked_opening_relu_po_kernel(
                 in_=x_scales[:, 4 * quad : 4 * quad + 4, :].bitcast(I32),
             )
         load_w1(1)
+        nc.sync.dma_start(out=w2_raw[:].bitcast(I32), in_=w2_words[0].bitcast(I32))
         for g in range(PASSES):
             nc.sync.dma_start(out=x_tab[g][:], in_=x_words[g].rearrange("p c r -> p (c r)").bitcast(I32))
         nc.sync.dma_start(out=lists["p1"][:], in_=p1)
         nc.sync.dma_start(out=lists["p2"][:], in_=p2)
-        nc.sync.dma_start(out=w2_raw[:].bitcast(I32), in_=w2_words[0].bitcast(I32))
         for quad in range(QUADS):
             nc.sync.dma_start(
                 out=w2s_raw[32 * quad : 32 * quad + 4, :].bitcast(I32),
@@ -106,6 +105,12 @@ def tile_picked_opening_relu_po_kernel(
         nc.scalar.copy(**dealt(1, 0, P // 2))
         nc.vector.tensor_copy(**dealt(1, P // 2, P))
         quantise_w1(1)
+        w2_dealt = tile([P, 2 * N], U8, "w2_dealt")
+        w2s_dealt = tile([P, N], U8, "w2s_dealt")
+        nc.vector.tensor_copy(
+            out=w2_dealt[:].rearrange("p (t m b) -> p m t b", t=PACK, b=2),
+            in_=w2_raw[:].rearrange("p (m t b) -> p m t b", t=PACK, b=2),
+        )
         gather_words(0, 0, S)
         gather_words(1, 0, HALF)
         gather_words(1, HALF, HALF)
@@ -125,12 +130,6 @@ def tile_picked_opening_relu_po_kernel(
                     stop=(g == PASSES - 1),
                 )
 
-        w2_dealt = tile([P, 2 * N], U8, "w2_dealt")
-        w2s_dealt = tile([P, N], U8, "w2s_dealt")
-        nc.vector.tensor_copy(
-            out=w2_dealt[:].rearrange("p (t m b) -> p m t b", t=PACK, b=2),
-            in_=w2_raw[:].rearrange("p (m t b) -> p m t b", t=PACK, b=2),
-        )
         nc.vector.tensor_copy(
             out=w2s_dealt[:].rearrange("p (t m) -> p m t", t=PACK),
             in_=w2s_raw[:].rearrange("p (m t) -> p m t", t=PACK),
@@ -138,25 +137,34 @@ def tile_picked_opening_relu_po_kernel(
 
         y_win = [tile([P, S if t == 0 else 2 * S], F32, "y%d" % t) for t in range(PACK)]
         y = [y_win[t][:, 0:S] for t in range(PACK)]
-        near1 = [y_win[t + 1][:, S : 2 * S] for t in range(PACK - 1)] + [tile([P, S], F32, "near1_last")[:]]
+        y_again = [y_win[t + 1][:, S : 2 * S] for t in range(PACK - 1)] + [tile([P, S], F32, "y_again_last")[:]]
+        drop1 = [tile([P, S], F32, "drop1_%d" % t) for t in range(PACK)]
+        drop2 = [tile([P, S], F32, "drop2_%d" % t) for t in range(PACK)]
+        drop = [tile([P, S], F32, "drop%d" % t) for t in range(PACK)]
+        h_turned = [tile([P, S], F32, "h_turned%d" % t) for t in range(PACK)]
         h = [tile([P, S], F32, "h%d" % t) for t in range(PACK)]
-        near2 = [tile([P, S], F32, "near2_%d" % t) for t in range(PACK)]
-        low = [tile([P, S], F32, "low%d" % t) for t in range(PACK)]
         h_bf = tile([P, PACK, S], BF16, "h_bf")
         far1 = [tile([P, PACK, HALF], BF16, "far1_%d" % half, tag="far1") for half in range(2)]
         high = [tile([P, PACK, HALF], BF16, "high%d" % half) for half in range(2)]
-        for i, (t, first, count) in enumerate(pieces):
-            nc.scalar.activation(y[t][:, first : first + count], y_ps[i][:], RELU)
+        nc.scalar.activation(y[0][:, 0:HALF], y_ps[0][:], RELU)
+        nc.vector.tensor_scalar_max(y[0][:, HALF:S], y_ps[1][:], 0.0)
+        nc.scalar.activation(y_again[0][:, HALF:S], y_ps[1][:], RELU)
+        nc.vector.tensor_scalar_max(y_again[0][:, 0:HALF], y_ps[0][:], 0.0)
+        for t in range(1, PACK):
+            nc.scalar.activation(y[t], y_ps[t + 1][:], RELU)
+            nc.scalar.activation(y_again[t], y_ps[t + 1][:], RELU)
 
         def fetch(dst, window, name, first, count):
             nc.vector.tensor_copy(
                 dst, window[:].indirect(lists[name][:, first // STRIPE : (first + count) // STRIPE])
             )
 
-        def fetch_row(dst, window, name):
-            step = window.shape[1] // 2
+        def fetch_drop(dst, t, name):
+            step = y_win[t].shape[1] // 2
             for first in range(0, S, step):
-                fetch(dst[:, first : first + step], window, name, first, step)
+                picks = lists[name][:, first // STRIPE : (first + step) // STRIPE]
+                cols = slice(first, first + step)
+                nc.vector.tensor_tensor(dst[:, cols], y_win[t][:].indirect(picks), y_again[t][:, cols], SUB)
 
         def turned_sum(terms, name, bank):
             acc = ps.tile([P, S], F32, name=name, tag=bank)
@@ -172,21 +180,15 @@ def tile_picked_opening_relu_po_kernel(
                     )
             return acc
 
-        y_neg_turned = [tile([P, S], F32, "y_neg_turned%d" % t) for t in range(TURNED)]
-        excess = [tile([P, S], F32, "excess%d" % t) for t in range(TURNED)]
-        y_neg = [tile([P, S], F32, "y_neg%d" % t) for t in range(TURNED)]
-        for t in range(TURNED):
-            nc.scalar.activation(y_neg[t][:], y[t], COPY, scale=-1.0)
-            acc = turned_sum([y[t]], "y_turned%d" % t, "bank%d" % (5 + t % 2))
-            nc.scalar.activation(y_neg_turned[t][:], acc[:], COPY, scale=-1.0)
-
         def finish_h(t):
-            nc.vector.tensor_tensor(low[t][:], near1[t], near2[t][:], MIN)
-            acc = turned_sum([y_neg[t], low[t]], "gap%d" % t, "bank%d" % (t % 2))
-            nc.scalar.activation(excess[t][:], acc[:], RELU, scale=-1.0)
-            acc = turned_sum([y_neg_turned[t], excess[t]], "h_neg%d" % t, "bank%d" % (2 + t % 2))
-            nc.scalar.activation(h[t][:], acc[:], COPY, scale=-1.0)
-            nc.scalar.activation(h_bf[:, t, :], acc[:], COPY, scale=-1.0)
+            nc.vector.scalar_tensor_tensor(
+                out=drop[t][:], in0=drop1[t][:], scalar=0.0, in1=drop2[t][:], op0=MIN, op1=MIN
+            )
+            acc = turned_sum([y[t], drop[t]], "h_turned_ps%d" % t, "bank%d" % (4 - t % 2))
+            nc.scalar.copy(out=h_turned[t][:], in_=acc[:])
+            acc = turned_sum([h_turned[t]], "h_ps%d" % t, "bank%d" % (5 + t % 2))
+            nc.scalar.copy(out=h[t][:], in_=acc[:])
+            nc.scalar.copy(out=h_bf[:, t, :], in_=acc[:])
 
         def fetch_far1(t, half):
             fetch(far1[half][:, t, :], h[t], "q1", half * HALF, HALF)
@@ -194,21 +196,13 @@ def tile_picked_opening_relu_po_kernel(
         def raise_h(half):
             nc.vector.tensor_tensor(high[half][:], far1[half][:], h_bf[:, :, half * HALF : (half + 1) * HALF], MAX)
 
-        def finish_h_here(t):
-            nc.vector.tensor_tensor(h[t][:], low[t][:], near2[t][:], MIN)
-            nc.scalar.copy(out=h_bf[:, t, :], in_=h[t][:])
-
         for t in range(PACK):
-            fetch_row(near1[t], y_win[t], "p1")
-            if 0 < t <= TURNED:
+            fetch_drop(drop1[t], t, "p1")
+            if t > 0:
                 finish_h(t - 1)
-            elif t > 0:
-                finish_h_here(t - 1)
-            fetch_row(near2[t][:], y_win[t], "p2")
-            if t >= TURNED:
-                nc.vector.tensor_tensor(low[t][:], near1[t], y[t], MIN)
+            fetch_drop(drop2[t], t, "p2")
         fetch_far1(0, 0)
-        finish_h_here(PACK - 1)
+        finish_h(PACK - 1)
 
         spans = [(0, 2 * CHUNK), (2 * CHUNK, CHUNK), (3 * CHUNK, CHUNK)]
         mid = [tile([P, PACK, n], BF16, "mid%d" % c, tag="held" if c == 0 else None) for c, n in spans]
@@ -255,7 +249,7 @@ def tile_picked_opening_relu_po_kernel(
                 unit = (first + lo) // CHUNK
                 rounded = woven(o_bf[c][:, PACK * lo : PACK * (lo + CHUNK)])
                 cols = slice(first + lo, first + lo + CHUNK)
-                o_ps = ps.tile([P, PACK, CHUNK], F32, name="o_ps%d" % unit, tag="bank%d" % (4 + unit))
+                o_ps = ps.tile([P, PACK, CHUNK], F32, name="o_ps%d" % unit, tag="bank%d" % ((7 + unit) % 8))
                 for t in range(PACK):
                     product(o_ps[:, t, :], t, c, lo)
                 if c == last:

@@ -115,7 +115,7 @@ def tile_picked_opening_relu_po_kernel(
         gather_words(1, 0, HALF)
         gather_words(1, HALF, HALF)
 
-        pieces = [(0, 0, HALF), (0, HALF, HALF)] + [(t, 0, S) for t in range(1, PACK)]
+        pieces = [(0, 0, HALF), (0, HALF, CHUNK), (0, HALF + CHUNK, CHUNK)] + [(t, 0, S) for t in range(1, PACK)]
         y_ps = [ps.tile([P, count], F32, name="y_ps%d" % i, tag="bank%d" % i) for i, (t, first, count) in enumerate(pieces)]
         for g in range(PASSES):
             for i, (t, first, count) in enumerate(pieces):
@@ -146,13 +146,16 @@ def tile_picked_opening_relu_po_kernel(
         h_bf = tile([P, PACK, S], BF16, "h_bf")
         far1 = [tile([P, PACK, HALF], BF16, "far1_%d" % half, tag="far1") for half in range(2)]
         high = [tile([P, PACK, HALF], BF16, "high%d" % half) for half in range(2)]
+        third, fourth = slice(HALF, HALF + CHUNK), slice(HALF + CHUNK, S)
         nc.scalar.activation(y[0][:, 0:HALF], y_ps[0][:], RELU)
-        nc.vector.tensor_scalar_max(y[0][:, HALF:S], y_ps[1][:], 0.0)
-        nc.scalar.activation(y_again[0][:, HALF:S], y_ps[1][:], RELU)
-        nc.vector.tensor_scalar_max(y_again[0][:, 0:HALF], y_ps[0][:], 0.0)
+        nc.scalar.activation(y_again[0][:, 0:HALF], y_ps[0][:], RELU)
+        nc.scalar.activation(y[0][:, third], y_ps[1][:], RELU)
+        nc.vector.tensor_scalar_max(y[0][:, fourth], y_ps[2][:], 0.0)
+        nc.vector.tensor_scalar_max(y_again[0][:, third], y_ps[1][:], 0.0)
+        nc.scalar.activation(y_again[0][:, fourth], y_ps[2][:], RELU)
         for t in range(1, PACK):
-            nc.scalar.activation(y[t], y_ps[t + 1][:], RELU)
-            nc.scalar.activation(y_again[t], y_ps[t + 1][:], RELU)
+            nc.scalar.activation(y[t], y_ps[t + 2][:], RELU)
+            nc.scalar.activation(y_again[t], y_ps[t + 2][:], RELU)
 
         def fetch(dst, window, name, first, count):
             nc.vector.tensor_copy(
@@ -184,17 +187,18 @@ def tile_picked_opening_relu_po_kernel(
             nc.vector.scalar_tensor_tensor(
                 out=drop[t][:], in0=drop1[t][:], scalar=0.0, in1=drop2[t][:], op0=MIN, op1=MIN
             )
-            acc = turned_sum([y[t], drop[t]], "h_turned_ps%d" % t, "bank%d" % (4 - t % 2))
+            acc = turned_sum([y[t], drop[t]], "h_turned_ps%d" % t, "bank%d" % (5 - t % 2))
             nc.scalar.copy(out=h_turned[t][:], in_=acc[:])
-            acc = turned_sum([h_turned[t]], "h_ps%d" % t, "bank%d" % (5 + t % 2))
+            acc = turned_sum([h_turned[t]], "h_ps%d" % t, "bank%d" % (6 + t % 2))
             nc.scalar.copy(out=h[t][:], in_=acc[:])
             nc.scalar.copy(out=h_bf[:, t, :], in_=acc[:])
 
         def fetch_far1(t, half):
             fetch(far1[half][:, t, :], h[t], "q1", half * HALF, HALF)
 
-        def raise_h(half):
-            nc.vector.tensor_tensor(high[half][:], far1[half][:], h_bf[:, :, half * HALF : (half + 1) * HALF], MAX)
+        def raise_h(half, rows=slice(0, PACK)):
+            cols = slice(half * HALF, (half + 1) * HALF)
+            nc.vector.tensor_tensor(high[half][:, rows], far1[half][:, rows], h_bf[:, rows, cols], MAX)
 
         for t in range(PACK):
             fetch_drop(drop1[t], t, "p1")
@@ -213,7 +217,7 @@ def tile_picked_opening_relu_po_kernel(
         z_codes = [tile([P, n], U32, "z_codes%d" % c) for c, n in spans]
         z_sc = [tile([P, n], U8, "z_sc%d" % c) for c, n in spans]
         o_f32 = [tile([P, PACK, CHUNK], F32, "o_f32_%d" % c) for c in range(CHUNKS)]
-        o_codes = [tile([P, n], U32, "o_codes%d" % c) for c, n in spans]
+        o_codes = [tile([P, HALF], U32, "o_codes%d" % half) for half in range(2)]
         o_sc = tile([P, S], U8, "o_sc")
         out_rows = out_0.rearrange("(p t) j -> p t j", t=PACK)
         out_words = out_1[0].rearrange("p c r -> p (c r)").bitcast(I32)
@@ -249,40 +253,56 @@ def tile_picked_opening_relu_po_kernel(
                 unit = (first + lo) // CHUNK
                 rounded = woven(o_bf[c][:, PACK * lo : PACK * (lo + CHUNK)])
                 cols = slice(first + lo, first + lo + CHUNK)
-                o_ps = ps.tile([P, PACK, CHUNK], F32, name="o_ps%d" % unit, tag="bank%d" % ((7 + unit) % 8))
+                o_ps = ps.tile([P, PACK, CHUNK], F32, name="o_ps%d" % unit, tag="bank%d" % unit)
                 for t in range(PACK):
                     product(o_ps[:, t, :], t, c, lo)
                 if c == last:
                     nc.vector.tensor_copy(out=rounded, in_=planar(o_ps[:]))
+                    for pair in range(2):
+                        rows = slice(2 * pair, 2 * pair + 2)
+                        again = ps.tile([P, 2, CHUNK], F32, name="o_again%d" % pair, tag="bank%d" % (unit + 1 + pair))
+                        for t in range(2):
+                            product(again[:, t, :], 2 * pair + t, c, lo)
+                        nc.scalar.copy(out=o_f32[unit][:, rows], in_=again[:])
+                        nc.scalar.dma_start(out=out_rows[:, rows, cols], in_=o_f32[unit][:, rows])
                 else:
                     nc.scalar.copy(out=rounded, in_=planar(o_ps[:]))
-                nc.scalar.copy(out=o_f32[unit][:], in_=o_ps[:])
-                nc.sync.dma_start(out=out_rows[:, :, cols], in_=o_f32[unit][:])
+                    nc.scalar.copy(out=o_f32[unit][:], in_=o_ps[:])
+                    nc.sync.dma_start(out=out_rows[:, :, cols], in_=o_f32[unit][:])
 
         def planes(c):
             first, count = spans[c]
             cols = slice(first, first + count)
-            nc.vector.quantize_mx(out=o_codes[c][:].bitcast(FP8X4), scales=o_sc[:, cols], in_=o_bf[c][:])
-            nc.sync.dma_start(out=out_words[:, cols], in_=o_codes[c][:].bitcast(I32))
+            half, lo = divmod(first, HALF)
+            nc.vector.quantize_mx(
+                out=o_codes[half][:, lo : lo + count].bitcast(FP8X4), scales=o_sc[:, cols], in_=o_bf[c][:]
+            )
+            if lo + count == HALF:
+                nc.sync.dma_start(out=out_words[:, half * HALF : (half + 1) * HALF], in_=o_codes[half][:].bitcast(I32))
 
         def fetch_far2(c, t):
             first, count = spans[c]
             fetch(far2[c][:, t, :], h[t], "q2", first, count)
 
-        def largest(c):
+        def largest(c, rows=slice(0, PACK)):
             first, count = spans[c]
             lo = first % HALF
-            nc.vector.tensor_tensor(mid[c][:], far2[c][:], high[first // HALF][:, :, lo : lo + count], MAX)
+            nc.vector.tensor_tensor(mid[c][:, rows], far2[c][:, rows], high[first // HALF][:, rows, lo : lo + count], MAX)
 
         def weave(c, copy):
             copy(out=woven8(z_bf[c][:]), in_=planar8(mid[c][:]))
 
         fetch_far2(0, 0)
-        for t in range(1, PACK):
+        for t in range(1, PACK - 1):
             fetch_far1(t, 0)
             fetch_far2(0, t)
-        raise_h(0)
-        largest(0)
+        early, late = slice(0, PACK - 1), slice(PACK - 1, PACK)
+        raise_h(0, early)
+        largest(0, early)
+        fetch_far1(PACK - 1, 0)
+        fetch_far2(0, PACK - 1)
+        raise_h(0, late)
+        largest(0, late)
         weave(0, nc.scalar.copy)
         for t in range(PACK):
             fetch_far1(t, 1)

@@ -25,7 +25,10 @@ CHUNK = 128
 CHUNKS = S // CHUNK
 STRIPE = 16
 MIN = mybir.AluOpType.min
+ADD = mybir.AluOpType.add
 SUB = mybir.AluOpType.subtract
+COPY = mybir.ActivationFunctionType.Copy
+FREED = 2
 
 
 def tile_picked_opening_relu_po_kernel(
@@ -99,7 +102,8 @@ def tile_picked_opening_relu_po_kernel(
             picks = lists["offs"][:, first // STRIPE : (first + count) // STRIPE]
             nc.vector.tensor_copy(x_codes[g][:, first : first + count], x_tab[g][:].bitcast(U32).indirect(picks))
 
-        nc.vector.tensor_copy(**dealt(0, 0, P))
+        nc.scalar.copy(**dealt(0, 0, P // 2))
+        nc.vector.tensor_copy(**dealt(0, P // 2, P))
         nc.vector.tensor_copy(x_sc[:], xs_tab[:].indirect(lists["offs"][:]))
         quantise_w1(0)
         nc.scalar.copy(**dealt(1, 0, P // 2))
@@ -117,18 +121,26 @@ def tile_picked_opening_relu_po_kernel(
 
         pieces = [(0, 0, HALF), (0, HALF, CHUNK), (0, HALF + CHUNK, CHUNK)] + [(t, 0, S) for t in range(1, PACK)]
         y_ps = [ps.tile([P, count], F32, name="y_ps%d" % i, tag="bank%d" % i) for i, (t, first, count) in enumerate(pieces)]
+
+        def first_product(i, g, start):
+            t, first, count = pieces[i]
+            cols = slice(P * t, P * (t + 1))
+            nc.tensor.matmul_mx(
+                out=y_ps[i][:],
+                lhsT=w1_codes[g][:, cols].bitcast(FP8X4),
+                lhsT_scale=w1_sc[g][:, cols],
+                rhs=x_codes[g][:, first : first + count].bitcast(FP8X4),
+                rhs_scale=x_sc[4 * g : P, first : first + count],
+                start=start,
+                stop=not start,
+            )
+
         for g in range(PASSES):
-            for i, (t, first, count) in enumerate(pieces):
-                cols = slice(P * t, P * (t + 1))
-                nc.tensor.matmul_mx(
-                    out=y_ps[i][:],
-                    lhsT=w1_codes[g][:, cols].bitcast(FP8X4),
-                    lhsT_scale=w1_sc[g][:, cols],
-                    rhs=x_codes[g][:, first : first + count].bitcast(FP8X4),
-                    rhs_scale=x_sc[4 * g : P, first : first + count],
-                    start=(g == 0),
-                    stop=(g == PASSES - 1),
-                )
+            for i in range(len(pieces) - 2):
+                first_product(i, g, g == 0)
+        for i in range(len(pieces) - 2, len(pieces)):
+            first_product(i, 1, True)
+            first_product(i, 0, False)
 
         nc.vector.tensor_copy(
             out=w2s_dealt[:].rearrange("p (t m) -> p m t", t=PACK),
@@ -142,20 +154,25 @@ def tile_picked_opening_relu_po_kernel(
         drop2 = [tile([P, S], F32, "drop2_%d" % t) for t in range(PACK)]
         drop = [tile([P, S], F32, "drop%d" % t) for t in range(PACK)]
         h_turned = [tile([P, S], F32, "h_turned%d" % t) for t in range(PACK)]
+        excess = [tile([P, S], F32, "excess%d" % t) for t in range(FREED)]
         h = [tile([P, S], F32, "h%d" % t) for t in range(PACK)]
         h_bf = tile([P, PACK, S], BF16, "h_bf")
-        far1 = [tile([P, PACK, HALF], BF16, "far1_%d" % half, tag="far1") for half in range(2)]
+        far1_first = tile([P, PACK, HALF], BF16, "far1_first", tag="far1")
+        far1_second = [tile([P, 2, HALF], BF16, "far1_second%d" % pair, tag="far1" if pair else None) for pair in range(2)]
         high = [tile([P, PACK, HALF], BF16, "high%d" % half) for half in range(2)]
         third, fourth = slice(HALF, HALF + CHUNK), slice(HALF + CHUNK, S)
-        nc.scalar.activation(y[0][:, 0:HALF], y_ps[0][:], RELU)
-        nc.scalar.activation(y_again[0][:, 0:HALF], y_ps[0][:], RELU)
-        nc.scalar.activation(y[0][:, third], y_ps[1][:], RELU)
-        nc.vector.tensor_scalar_max(y[0][:, fourth], y_ps[2][:], 0.0)
-        nc.vector.tensor_scalar_max(y_again[0][:, third], y_ps[1][:], 0.0)
-        nc.scalar.activation(y_again[0][:, fourth], y_ps[2][:], RELU)
+        nc.scalar.copy(out=y[0][:, 0:HALF], in_=y_ps[0][:])
+        nc.scalar.activation(y_again[0][:, 0:HALF], y_ps[0][:], COPY, scale=-1.0)
+        nc.scalar.copy(out=y[0][:, third], in_=y_ps[1][:])
+        nc.vector.tensor_copy(y[0][:, fourth], y_ps[2][:])
+        nc.scalar.activation(y_again[0][:, third], y_ps[1][:], COPY, scale=-1.0)
+        nc.scalar.activation(y_again[0][:, fourth], y_ps[2][:], COPY, scale=-1.0)
         for t in range(1, PACK):
-            nc.scalar.activation(y[t], y_ps[t + 2][:], RELU)
-            nc.scalar.activation(y_again[t], y_ps[t + 2][:], RELU)
+            nc.scalar.copy(out=y[t], in_=y_ps[t + 2][:])
+            if t < FREED:
+                nc.scalar.activation(y_again[t], y_ps[t + 2][:], COPY, scale=-1.0)
+            else:
+                nc.sync.dma_start(out=y_again[t], in_=y[t])
 
         def fetch(dst, window, name, first, count):
             nc.vector.tensor_copy(
@@ -167,7 +184,7 @@ def tile_picked_opening_relu_po_kernel(
             for first in range(0, S, step):
                 picks = lists[name][:, first // STRIPE : (first + step) // STRIPE]
                 cols = slice(first, first + step)
-                nc.vector.tensor_tensor(dst[:, cols], y_win[t][:].indirect(picks), y_again[t][:, cols], SUB)
+                nc.vector.tensor_tensor(dst[:, cols], y_win[t][:].indirect(picks), y_again[t][:, cols], ADD if t < FREED else SUB)
 
         def turned_sum(terms, name, bank):
             acc = ps.tile([P, S], F32, name=name, tag=bank)
@@ -184,21 +201,33 @@ def tile_picked_opening_relu_po_kernel(
             return acc
 
         def finish_h(t):
-            nc.vector.scalar_tensor_tensor(
-                out=drop[t][:], in0=drop1[t][:], scalar=0.0, in1=drop2[t][:], op0=MIN, op1=MIN
-            )
-            acc = turned_sum([y[t], drop[t]], "h_turned_ps%d" % t, "bank%d" % (5 - t % 2))
-            nc.scalar.copy(out=h_turned[t][:], in_=acc[:])
-            acc = turned_sum([h_turned[t]], "h_ps%d" % t, "bank%d" % (6 + t % 2))
-            nc.scalar.copy(out=h[t][:], in_=acc[:])
-            nc.scalar.copy(out=h_bf[:, t, :], in_=acc[:])
+            if t < FREED:
+                nc.scalar.activation(drop[t][:], drop1[t][:], RELU, scale=-1.0)
+                acc = turned_sum([y_again[t], drop[t]], "low_turned_ps%d" % t, "bank%d" % (5 - t % 2))
+                nc.scalar.copy(out=h_turned[t][:], in_=acc[:])
+                acc = turned_sum([drop[t], drop2[t]], "gap_turned_ps%d" % t, "bank%d" % (3 - t % 2))
+                nc.scalar.activation(excess[t][:], acc[:], RELU, scale=-1.0)
+                acc = turned_sum([h_turned[t], excess[t]], "h_ps%d" % t, "bank%d" % (6 + t % 2))
+                sign = -1.0
+            else:
+                nc.vector.scalar_tensor_tensor(
+                    out=drop[t][:], in0=drop1[t][:], scalar=0.0, in1=drop2[t][:], op0=MIN, op1=MIN
+                )
+                acc = turned_sum([y[t], drop[t]], "h_turned_ps%d" % t, "bank%d" % (5 - t % 2))
+                nc.scalar.copy(out=h_turned[t][:], in_=acc[:])
+                acc = turned_sum([h_turned[t]], "h_ps%d" % t, "bank%d" % (6 + t % 2))
+                sign = 1.0
+            nc.scalar.activation(h[t][:], acc[:], RELU, scale=sign)
+            nc.scalar.activation(h_bf[:, t, :], acc[:], RELU, scale=sign)
 
         def fetch_far1(t, half):
-            fetch(far1[half][:, t, :], h[t], "q1", half * HALF, HALF)
+            dst = far1_second[t // 2][:, t % 2, :] if half else far1_first[:, t, :]
+            fetch(dst, h[t], "q1", half * HALF, HALF)
 
-        def raise_h(half, rows=slice(0, PACK)):
+        def raise_h(half, rows):
             cols = slice(half * HALF, (half + 1) * HALF)
-            nc.vector.tensor_tensor(high[half][:, rows], far1[half][:, rows], h_bf[:, rows, cols], MAX)
+            far = far1_second[rows.start // 2][:] if half else far1_first[:, rows]
+            nc.vector.tensor_tensor(high[half][:, rows], far, h_bf[:, rows, cols], MAX)
 
         for t in range(PACK):
             fetch_drop(drop1[t], t, "p1")
@@ -293,21 +322,25 @@ def tile_picked_opening_relu_po_kernel(
             copy(out=woven8(z_bf[c][:]), in_=planar8(mid[c][:]))
 
         fetch_far2(0, 0)
-        for t in range(1, PACK - 1):
-            fetch_far1(t, 0)
-            fetch_far2(0, t)
+        fetch_far1(0, 1)
+        fetch_far1(1, 0)
+        fetch_far2(0, 1)
+        fetch_far1(1, 1)
+        fetch_far1(2, 0)
+        fetch_far2(0, 2)
         early, late = slice(0, PACK - 1), slice(PACK - 1, PACK)
         raise_h(0, early)
+        raise_h(1, slice(0, 2))
         largest(0, early)
         fetch_far1(PACK - 1, 0)
         fetch_far2(0, PACK - 1)
         raise_h(0, late)
         largest(0, late)
         weave(0, nc.scalar.copy)
-        for t in range(PACK):
-            fetch_far1(t, 1)
+        fetch_far1(2, 1)
+        fetch_far1(3, 1)
         second_product(0)
-        raise_h(1)
+        raise_h(1, slice(2, PACK))
         for t in range(PACK):
             fetch_far2(1, t)
         fetch_far2(2, 0)

@@ -294,6 +294,10 @@ def tile_picked_opening_relu_po_kernel(
                             product(again[:, t, :], 2 * pair + t, c, lo)
                         nc.scalar.copy(out=o_f32[unit][:, rows], in_=again[:])
                         nc.scalar.dma_start(out=out_rows[:, rows, cols], in_=o_f32[unit][:, rows])
+                elif c == 1:
+                    nc.scalar.copy(out=o_f32[unit][:], in_=o_ps[:])
+                    nc.sync.dma_start(out=out_rows[:, :, cols], in_=o_f32[unit][:])
+                    nc.scalar.copy(out=rounded, in_=planar(o_ps[:]))
                 else:
                     nc.scalar.copy(out=rounded, in_=planar(o_ps[:]))
                     nc.scalar.copy(out=o_f32[unit][:], in_=o_ps[:])

@@ -12,7 +12,11 @@ U8 = mybir.dt.uint8
 FP8X4 = mybir.dt.float8_e4m3fn_x4
 FP4X4 = mybir.dt.float4_e2m1fn_x4
 MAX = mybir.AluOpType.max
+MIN = mybir.AluOpType.min
+ADD = mybir.AluOpType.add
+SUB = mybir.AluOpType.subtract
 RELU = mybir.ActivationFunctionType.Relu
+COPY = mybir.ActivationFunctionType.Copy
 
 K, T, S, H, N = 1024, 2048, 512, 512, 512
 FLOPS = 2 * K * H * S + 2 * H * N * S
@@ -22,13 +26,8 @@ PASSES = K // (P * PACK)
 QUADS = 4
 HALF = S // 2
 CHUNK = 128
-CHUNKS = S // CHUNK
 STRIPE = 16
-MIN = mybir.AluOpType.min
-ADD = mybir.AluOpType.add
-SUB = mybir.AluOpType.subtract
-COPY = mybir.ActivationFunctionType.Copy
-FREED = 2
+OFF_VECTOR = 2
 
 
 def tile_picked_opening_relu_po_kernel(
@@ -42,41 +41,43 @@ def tile_picked_opening_relu_po_kernel(
         def tile(shape, dtype, name, tag=None):
             return sb.tile(shape, dtype, name=name, tag=tag or name, align_bytes=64)
 
+        def bank_tile(shape, name, bank):
+            return ps.tile(shape, F32, name=name, tag="bank%d" % bank)
+
         w1_raw = [tile([P, PACK, H], F32, "w1_raw%d" % g) for g in range(PASSES)]
-        x_tab = [tile([P, T], I32, "x_tab%d" % g) for g in range(PASSES)]
-        xs_tab = tile([P, T], U8, "xs_tab")
+        x_table = [tile([P, T], I32, "x_table%d" % g) for g in range(PASSES)]
+        x_scale_table = tile([P, T], U8, "x_scale_table")
         w2_raw = tile([P, 2 * N], U8, "w2_raw")
-        w2s_raw = tile([P, N], U8, "w2s_raw")
+        w2_scale_raw = tile([P, N], U8, "w2_scale_raw")
         lists = {}
         for name in ("offs", "p1", "p2", "q1", "q2"):
             lists[name] = tile([P, S // STRIPE], U16, "list_" + name)
 
-        nc.gpsimd.memset(xs_tab[:].bitcast(I32), 0)
-        nc.vector.memset(w2s_raw[:].bitcast(I32), 0)
+        nc.gpsimd.memset(x_scale_table[:].bitcast(I32), 0)
+        nc.vector.memset(w2_scale_raw[:].bitcast(I32), 0)
         ident = tile([P, P], F32, "ident")
         make_identity(nc, ident[:])
 
         def load_w1(g):
-            nc.sync.dma_start(
-                out=w1_raw[g][:], in_=w1[512 * g : 512 * (g + 1), :].rearrange("(p j) c -> p j c", j=PACK)
-            )
+            rows = w1[P * PACK * g : P * PACK * (g + 1), :]
+            nc.sync.dma_start(out=w1_raw[g][:], in_=rows.rearrange("(p j) c -> p j c", j=PACK))
 
         nc.sync.dma_start(out=lists["offs"][:], in_=offs)
         load_w1(0)
         for quad in range(QUADS):
             nc.sync.dma_start(
-                out=xs_tab[32 * quad : 32 * quad + 4 * PASSES, :].bitcast(I32),
+                out=x_scale_table[32 * quad : 32 * quad + 4 * PASSES, :].bitcast(I32),
                 in_=x_scales[:, 4 * quad : 4 * quad + 4, :].bitcast(I32),
             )
         load_w1(1)
         nc.sync.dma_start(out=w2_raw[:].bitcast(I32), in_=w2_words[0].bitcast(I32))
         for g in range(PASSES):
-            nc.sync.dma_start(out=x_tab[g][:], in_=x_words[g].rearrange("p c r -> p (c r)").bitcast(I32))
+            nc.sync.dma_start(out=x_table[g][:], in_=x_words[g].rearrange("p c r -> p (c r)").bitcast(I32))
         nc.sync.dma_start(out=lists["p1"][:], in_=p1)
         nc.sync.dma_start(out=lists["p2"][:], in_=p2)
         for quad in range(QUADS):
             nc.sync.dma_start(
-                out=w2s_raw[32 * quad : 32 * quad + 4, :].bitcast(I32),
+                out=w2_scale_raw[32 * quad : 32 * quad + 4, :].bitcast(I32),
                 in_=w2_scales[0, 4 * quad : 4 * quad + 4, :].bitcast(I32),
             )
         nc.sync.dma_start(out=lists["q1"][:], in_=q1)
@@ -84,33 +85,35 @@ def tile_picked_opening_relu_po_kernel(
 
         w1_bf = [tile([P, PACK * H], BF16, "w1_bf%d" % g) for g in range(PASSES)]
         w1_codes = [tile([P, H], U32, "w1_codes%d" % g) for g in range(PASSES)]
-        w1_sc = [tile([P, H], U8, "w1_sc%d" % g) for g in range(PASSES)]
+        w1_scales = [tile([P, H], U8, "w1_scales%d" % g) for g in range(PASSES)]
 
-        def dealt(g, lo, hi):
-            return dict(
-                out=w1_bf[g][:].rearrange("p (t m j) -> p m j t", t=PACK, j=PACK)[:, lo:hi],
-                in_=w1_raw[g][:].rearrange("p j (m t) -> p m j t", t=PACK)[:, lo:hi],
-            )
+        def round_w1(g):
+            dst = w1_bf[g][:].rearrange("p (t m j) -> p m j t", t=PACK, j=PACK)
+            src = w1_raw[g][:].rearrange("p j (m t) -> p m j t", t=PACK)
+            nc.scalar.copy(out=dst[:, 0 : P // 2], in_=src[:, 0 : P // 2])
+            nc.vector.tensor_copy(out=dst[:, P // 2 : P], in_=src[:, P // 2 : P])
 
         def quantise_w1(g):
-            nc.vector.quantize_mx(out=w1_codes[g][:].bitcast(FP8X4), scales=w1_sc[g][:], in_=w1_bf[g][:])
+            nc.vector.quantize_mx(out=w1_codes[g][:].bitcast(FP8X4), scales=w1_scales[g][:], in_=w1_bf[g][:])
 
         x_codes = [tile([P, S], U32, "x_codes%d" % g) for g in range(PASSES)]
-        x_sc = tile([P, S], U8, "x_sc")
+        x_picked_scales = tile([P, S], U8, "x_picked_scales")
+
+        def entries(name, first, count):
+            return lists[name][:, first // STRIPE : (first + count) // STRIPE]
 
         def gather_words(g, first, count):
-            picks = lists["offs"][:, first // STRIPE : (first + count) // STRIPE]
-            nc.vector.tensor_copy(x_codes[g][:, first : first + count], x_tab[g][:].bitcast(U32).indirect(picks))
+            nc.vector.tensor_copy(
+                x_codes[g][:, first : first + count], x_table[g][:].bitcast(U32).indirect(entries("offs", first, count))
+            )
 
-        nc.scalar.copy(**dealt(0, 0, P // 2))
-        nc.vector.tensor_copy(**dealt(0, P // 2, P))
-        nc.vector.tensor_copy(x_sc[:], xs_tab[:].indirect(lists["offs"][:]))
+        round_w1(0)
+        nc.vector.tensor_copy(x_picked_scales[:], x_scale_table[:].indirect(lists["offs"][:]))
         quantise_w1(0)
-        nc.scalar.copy(**dealt(1, 0, P // 2))
-        nc.vector.tensor_copy(**dealt(1, P // 2, P))
+        round_w1(1)
         quantise_w1(1)
         w2_dealt = tile([P, 2 * N], U8, "w2_dealt")
-        w2s_dealt = tile([P, N], U8, "w2s_dealt")
+        w2_scale_dealt = tile([P, N], U8, "w2_scale_dealt")
         nc.vector.tensor_copy(
             out=w2_dealt[:].rearrange("p (t m b) -> p m t b", t=PACK, b=2),
             in_=w2_raw[:].rearrange("p (m t b) -> p m t b", t=PACK, b=2),
@@ -120,7 +123,8 @@ def tile_picked_opening_relu_po_kernel(
         gather_words(1, HALF, HALF)
 
         pieces = [(0, 0, HALF), (0, HALF, CHUNK), (0, HALF + CHUNK, CHUNK)] + [(t, 0, S) for t in range(1, PACK)]
-        y_ps = [ps.tile([P, count], F32, name="y_ps%d" % i, tag="bank%d" % i) for i, (t, first, count) in enumerate(pieces)]
+        y_ps = [bank_tile([P, count], "y_ps%d" % i, i) for i, (t, first, count) in enumerate(pieces)]
+        y_bank = {t: i for i, (t, first, count) in enumerate(pieces)}
 
         def first_product(i, g, start):
             t, first, count = pieces[i]
@@ -128,66 +132,69 @@ def tile_picked_opening_relu_po_kernel(
             nc.tensor.matmul_mx(
                 out=y_ps[i][:],
                 lhsT=w1_codes[g][:, cols].bitcast(FP8X4),
-                lhsT_scale=w1_sc[g][:, cols],
+                lhsT_scale=w1_scales[g][:, cols],
                 rhs=x_codes[g][:, first : first + count].bitcast(FP8X4),
-                rhs_scale=x_sc[4 * g : P, first : first + count],
+                rhs_scale=x_picked_scales[4 * g : P, first : first + count],
                 start=start,
                 stop=not start,
             )
 
         for g in range(PASSES):
-            for i in range(len(pieces) - 2):
+            for i in range(y_bank[2]):
                 first_product(i, g, g == 0)
-        for i in range(len(pieces) - 2, len(pieces)):
+        for i in range(y_bank[2], len(pieces)):
             first_product(i, 1, True)
             first_product(i, 0, False)
 
         nc.vector.tensor_copy(
-            out=w2s_dealt[:].rearrange("p (t m) -> p m t", t=PACK),
-            in_=w2s_raw[:].rearrange("p (m t) -> p m t", t=PACK),
+            out=w2_scale_dealt[:].rearrange("p (t m) -> p m t", t=PACK),
+            in_=w2_scale_raw[:].rearrange("p (m t) -> p m t", t=PACK),
         )
 
-        y_win = [tile([P, S if t == 0 else 2 * S], F32, "y%d" % t) for t in range(PACK)]
-        y = [y_win[t][:, 0:S] for t in range(PACK)]
-        y_again = [y_win[t + 1][:, S : 2 * S] for t in range(PACK - 1)] + [tile([P, S], F32, "y_again_last")[:]]
-        drop1 = [tile([P, S], F32, "drop1_%d" % t) for t in range(PACK)]
-        drop2 = [tile([P, S], F32, "drop2_%d" % t) for t in range(PACK)]
-        drop = [tile([P, S], F32, "drop%d" % t) for t in range(PACK)]
-        h_turned = [tile([P, S], F32, "h_turned%d" % t) for t in range(PACK)]
-        excess = [tile([P, S], F32, "excess%d" % t) for t in range(FREED)]
+        y_window = [tile([P, S if t == 0 else 2 * S], F32, "y_window%d" % t) for t in range(PACK)]
+        y = [y_window[t][:, 0:S] for t in range(PACK)]
+        own = [y_window[t + 1][:, S : 2 * S] for t in range(PACK - 1)] + [tile([P, S], F32, "own_last")[:]]
+        diff1 = [tile([P, S], F32, "diff1_%d" % t) for t in range(PACK)]
+        diff2 = [tile([P, S], F32, "diff2_%d" % t) for t in range(PACK)]
+        stage = [tile([P, S], F32, "stage%d" % t) for t in range(PACK)]
+        turned = [tile([P, S], F32, "turned%d" % t) for t in range(PACK)]
+        over2_turned = [tile([P, S], F32, "over2_turned%d" % t) for t in range(OFF_VECTOR)]
         h = [tile([P, S], F32, "h%d" % t) for t in range(PACK)]
         h_bf = tile([P, PACK, S], BF16, "h_bf")
         far1_first = tile([P, PACK, HALF], BF16, "far1_first", tag="far1")
-        far1_second = [tile([P, 2, HALF], BF16, "far1_second%d" % pair, tag="far1" if pair else None) for pair in range(2)]
+        far1_second = [
+            tile([P, 2, HALF], BF16, "far1_second0"),
+            tile([P, 2, HALF], BF16, "far1_second1", tag="far1"),
+        ]
         high = [tile([P, PACK, HALF], BF16, "high%d" % half) for half in range(2)]
+
         third, fourth = slice(HALF, HALF + CHUNK), slice(HALF + CHUNK, S)
         nc.scalar.copy(out=y[0][:, 0:HALF], in_=y_ps[0][:])
-        nc.scalar.activation(y_again[0][:, 0:HALF], y_ps[0][:], COPY, scale=-1.0)
+        nc.scalar.activation(own[0][:, 0:HALF], y_ps[0][:], COPY, scale=-1.0)
         nc.scalar.copy(out=y[0][:, third], in_=y_ps[1][:])
         nc.vector.tensor_copy(y[0][:, fourth], y_ps[2][:])
-        nc.scalar.activation(y_again[0][:, third], y_ps[1][:], COPY, scale=-1.0)
-        nc.scalar.activation(y_again[0][:, fourth], y_ps[2][:], COPY, scale=-1.0)
+        nc.scalar.activation(own[0][:, third], y_ps[1][:], COPY, scale=-1.0)
+        nc.scalar.activation(own[0][:, fourth], y_ps[2][:], COPY, scale=-1.0)
         for t in range(1, PACK):
-            nc.scalar.copy(out=y[t], in_=y_ps[t + 2][:])
-            if t < FREED:
-                nc.scalar.activation(y_again[t], y_ps[t + 2][:], COPY, scale=-1.0)
+            nc.scalar.copy(out=y[t], in_=y_ps[y_bank[t]][:])
+            if t < OFF_VECTOR:
+                nc.scalar.activation(own[t], y_ps[y_bank[t]][:], COPY, scale=-1.0)
             else:
-                nc.sync.dma_start(out=y_again[t], in_=y[t])
+                nc.sync.dma_start(out=own[t], in_=y[t])
 
-        def fetch(dst, window, name, first, count):
-            nc.vector.tensor_copy(
-                dst, window[:].indirect(lists[name][:, first // STRIPE : (first + count) // STRIPE])
-            )
-
-        def fetch_drop(dst, t, name):
-            step = y_win[t].shape[1] // 2
+        def fetch_diff(dst, t, name):
+            step = y_window[t].shape[1] // 2
             for first in range(0, S, step):
-                picks = lists[name][:, first // STRIPE : (first + step) // STRIPE]
                 cols = slice(first, first + step)
-                nc.vector.tensor_tensor(dst[:, cols], y_win[t][:].indirect(picks), y_again[t][:, cols], ADD if t < FREED else SUB)
+                nc.vector.tensor_tensor(
+                    dst[:, cols],
+                    y_window[t][:].indirect(entries(name, first, step)),
+                    own[t][:, cols],
+                    ADD if t < OFF_VECTOR else SUB,
+                )
 
         def turned_sum(terms, name, bank):
-            acc = ps.tile([P, S], F32, name=name, tag=bank)
+            acc = bank_tile([P, S], name, bank)
             for i, term in enumerate(terms):
                 for lo in range(0, S, P):
                     nc.tensor.matmul(
@@ -200,169 +207,194 @@ def tile_picked_opening_relu_po_kernel(
                     )
             return acc
 
+        def first_sum_bank(t):
+            return y_bank[3] - t % 2
+
+        def second_sum_bank(t):
+            return y_bank[1] - t % 2
+
+        def h_bank(t):
+            return len(pieces) + t % 2
+
+        def minus_h_off_vector(t):
+            over1, minus_low_turned = stage[t], turned[t]
+            nc.scalar.activation(over1[:], diff1[t][:], RELU, scale=-1.0)
+            acc = turned_sum([own[t], over1], "minus_low_ps%d" % t, first_sum_bank(t))
+            nc.scalar.copy(out=minus_low_turned[:], in_=acc[:])
+            acc = turned_sum([over1, diff2[t]], "near2_less_low_ps%d" % t, second_sum_bank(t))
+            nc.scalar.activation(over2_turned[t][:], acc[:], RELU, scale=-1.0)
+            return turned_sum([minus_low_turned, over2_turned[t]], "minus_h_ps%d" % t, h_bank(t))
+
+        def h_with_vector(t):
+            drop, h_turned = stage[t], turned[t]
+            nc.vector.scalar_tensor_tensor(out=drop[:], in0=diff1[t][:], scalar=0.0, in1=diff2[t][:], op0=MIN, op1=MIN)
+            acc = turned_sum([y[t], drop], "h_turned_ps%d" % t, first_sum_bank(t))
+            nc.scalar.copy(out=h_turned[:], in_=acc[:])
+            return turned_sum([h_turned], "h_ps%d" % t, h_bank(t))
+
         def finish_h(t):
-            if t < FREED:
-                nc.scalar.activation(drop[t][:], drop1[t][:], RELU, scale=-1.0)
-                acc = turned_sum([y_again[t], drop[t]], "low_turned_ps%d" % t, "bank%d" % (5 - t % 2))
-                nc.scalar.copy(out=h_turned[t][:], in_=acc[:])
-                acc = turned_sum([drop[t], drop2[t]], "gap_turned_ps%d" % t, "bank%d" % (3 - t % 2))
-                nc.scalar.activation(excess[t][:], acc[:], RELU, scale=-1.0)
-                acc = turned_sum([h_turned[t], excess[t]], "h_ps%d" % t, "bank%d" % (6 + t % 2))
-                sign = -1.0
-            else:
-                nc.vector.scalar_tensor_tensor(
-                    out=drop[t][:], in0=drop1[t][:], scalar=0.0, in1=drop2[t][:], op0=MIN, op1=MIN
-                )
-                acc = turned_sum([y[t], drop[t]], "h_turned_ps%d" % t, "bank%d" % (5 - t % 2))
-                nc.scalar.copy(out=h_turned[t][:], in_=acc[:])
-                acc = turned_sum([h_turned[t]], "h_ps%d" % t, "bank%d" % (6 + t % 2))
-                sign = 1.0
+            acc, sign = (minus_h_off_vector(t), -1.0) if t < OFF_VECTOR else (h_with_vector(t), 1.0)
             nc.scalar.activation(h[t][:], acc[:], RELU, scale=sign)
             nc.scalar.activation(h_bf[:, t, :], acc[:], RELU, scale=sign)
 
+        def fetch_h(dst, t, name, first, count):
+            nc.vector.tensor_copy(dst, h[t][:].indirect(entries(name, first, count)))
+
         def fetch_far1(t, half):
             dst = far1_second[t // 2][:, t % 2, :] if half else far1_first[:, t, :]
-            fetch(dst, h[t], "q1", half * HALF, HALF)
+            fetch_h(dst, t, "q1", half * HALF, HALF)
 
-        def raise_h(half, rows):
+        def make_high(half, quarters):
             cols = slice(half * HALF, (half + 1) * HALF)
-            far = far1_second[rows.start // 2][:] if half else far1_first[:, rows]
-            nc.vector.tensor_tensor(high[half][:, rows], far, h_bf[:, rows, cols], MAX)
+            far = far1_second[quarters.start // 2][:] if half else far1_first[:, quarters]
+            nc.vector.tensor_tensor(high[half][:, quarters], far, h_bf[:, quarters, cols], MAX)
 
         for t in range(PACK):
-            fetch_drop(drop1[t], t, "p1")
+            fetch_diff(diff1[t], t, "p1")
             if t > 0:
                 finish_h(t - 1)
-            fetch_drop(drop2[t], t, "p2")
+            fetch_diff(diff2[t], t, "p2")
         fetch_far1(0, 0)
         finish_h(PACK - 1)
 
-        spans = [(0, 2 * CHUNK), (2 * CHUNK, CHUNK), (3 * CHUNK, CHUNK)]
-        mid = [tile([P, PACK, n], BF16, "mid%d" % c, tag="held" if c == 0 else None) for c, n in spans]
+        spans = [(0, HALF), (HALF, CHUNK), (HALF + CHUNK, CHUNK)]
+        FIRST, MIDDLE, LAST = range(len(spans))
+        z_planar = [
+            tile([P, PACK, count], BF16, "z_planar%d" % first, tag="held" if first == 0 else None) for first, count in spans
+        ]
         far2_late = tile([P, 2, PACK, CHUNK], BF16, "far2_late", tag="held")
         far2 = [tile([P, PACK, HALF], BF16, "far2_first"), far2_late[:, 0], far2_late[:, 1]]
-        z_bf = [tile([P, PACK * n], BF16, "z_bf%d" % c) for c, n in spans]
-        o_bf = [tile([P, PACK * n], BF16, "o_bf%d" % c) for c, n in spans]
-        z_codes = [tile([P, n], U32, "z_codes%d" % c) for c, n in spans]
-        z_sc = [tile([P, n], U8, "z_sc%d" % c) for c, n in spans]
-        o_f32 = [tile([P, PACK, CHUNK], F32, "o_f32_%d" % c) for c in range(CHUNKS)]
-        o_codes = [tile([P, HALF], U32, "o_codes%d" % half) for half in range(2)]
-        o_sc = tile([P, S], U8, "o_sc")
+        z_woven = [tile([P, PACK * count], BF16, "z_woven%d" % first) for first, count in spans]
+        out_woven = [tile([P, PACK * count], BF16, "out_woven%d" % first) for first, count in spans]
+        z_codes = [tile([P, count], U32, "z_codes%d" % first) for first, count in spans]
+        z_scales = [tile([P, count], U8, "z_scales%d" % first) for first, count in spans]
+        out_f32 = [tile([P, PACK, count], F32, "out_f32_%d" % first) for first, count in spans]
+        out_codes = [tile([P, HALF], U32, "out_codes%d" % half) for half in range(2)]
+        out_scales = tile([P, S], U8, "out_scales")
         out_rows = out_0.rearrange("(p t) j -> p t j", t=PACK)
         out_words = out_1[0].rearrange("p c r -> p (c r)").bitcast(I32)
-        last = len(spans) - 1
 
-        def woven(ap):
-            return ap.rearrange("p (n i t) -> p n t i", i=4, t=PACK)
+        def weave(copy, dst, src, run):
+            copy(
+                out=dst.rearrange("p (n i t) -> p n t i", i=run, t=PACK),
+                in_=src.rearrange("p t (n i) -> p n t i", i=run),
+            )
 
-        def planar(ap):
-            return ap.rearrange("p t (n i) -> p n t i", i=4)
+        def fetch_far2(span, t):
+            first, count = spans[span]
+            fetch_h(far2[span][:, t, :], t, "q2", first, count)
 
-        def woven8(ap):
-            return ap.rearrange("p (n i t) -> p n t i", i=8, t=PACK)
+        def make_z(span, quarters=slice(0, PACK)):
+            first, count = spans[span]
+            half, lo = divmod(first, HALF)
+            nc.vector.tensor_tensor(
+                z_planar[span][:, quarters], far2[span][:, quarters], high[half][:, quarters, lo : lo + count], MAX
+            )
 
-        def planar8(ap):
-            return ap.rearrange("p t (n i) -> p n t i", i=8)
+        def weave_z(span, copy):
+            weave(copy, z_woven[span][:], z_planar[span][:], 8)
 
-        def product(out, t, c, lo):
+        def quantise_z(span):
+            nc.vector.quantize_mx(out=z_codes[span][:].bitcast(FP8X4), scales=z_scales[span][:], in_=z_woven[span][:])
+
+        def product(out, t, span, lo, count):
             nc.tensor.matmul_mx(
                 out=out,
                 lhsT=w2_dealt[:, 2 * P * t : 2 * P * (t + 1)].bitcast(FP4X4),
-                lhsT_scale=w2s_dealt[:, P * t : P * (t + 1)],
-                rhs=z_codes[c][:, lo : lo + CHUNK].bitcast(FP8X4),
-                rhs_scale=z_sc[c][:, lo : lo + CHUNK],
+                lhsT_scale=w2_scale_dealt[:, P * t : P * (t + 1)],
+                rhs=z_codes[span][:, lo : lo + count].bitcast(FP8X4),
+                rhs_scale=z_scales[span][:, lo : lo + count],
                 start=True,
                 stop=True,
             )
 
-        def second_product(c):
-            first, count = spans[c]
-            nc.vector.quantize_mx(out=z_codes[c][:].bitcast(FP8X4), scales=z_sc[c][:], in_=z_bf[c][:])
-            for lo in range(0, count, CHUNK):
-                unit = (first + lo) // CHUNK
-                rounded = woven(o_bf[c][:, PACK * lo : PACK * (lo + CHUNK)])
-                cols = slice(first + lo, first + lo + CHUNK)
-                o_ps = ps.tile([P, PACK, CHUNK], F32, name="o_ps%d" % unit, tag="bank%d" % unit)
-                for t in range(PACK):
-                    product(o_ps[:, t, :], t, c, lo)
-                if c == last:
-                    nc.vector.tensor_copy(out=rounded, in_=planar(o_ps[:]))
-                    for pair in range(2):
-                        rows = slice(2 * pair, 2 * pair + 2)
-                        again = ps.tile([P, 2, CHUNK], F32, name="o_again%d" % pair, tag="bank%d" % (unit + 1 + pair))
-                        for t in range(2):
-                            product(again[:, t, :], 2 * pair + t, c, lo)
-                        nc.scalar.copy(out=o_f32[unit][:, rows], in_=again[:])
-                        nc.scalar.dma_start(out=out_rows[:, rows, cols], in_=o_f32[unit][:, rows])
-                elif c == 1:
-                    nc.scalar.copy(out=o_f32[unit][:], in_=o_ps[:])
-                    nc.sync.dma_start(out=out_rows[:, :, cols], in_=o_f32[unit][:])
-                    nc.scalar.copy(out=rounded, in_=planar(o_ps[:]))
-                else:
-                    nc.scalar.copy(out=rounded, in_=planar(o_ps[:]))
-                    nc.scalar.copy(out=o_f32[unit][:], in_=o_ps[:])
-                    nc.sync.dma_start(out=out_rows[:, :, cols], in_=o_f32[unit][:])
+        def chunk_product(span, lo):
+            n = (spans[span][0] + lo) // CHUNK
+            acc = bank_tile([P, PACK, CHUNK], "out_chunk_ps%d" % n, n)
+            for t in range(PACK):
+                product(acc[:, t, :], t, span, lo, CHUNK)
+            return acc
 
-        def planes(c):
-            first, count = spans[c]
-            cols = slice(first, first + count)
+        def round_chunk(copy, span, lo, acc):
+            weave(copy, out_woven[span][:, PACK * lo : PACK * (lo + CHUNK)], acc[:], 4)
+
+        def store_pair(span, pair, bank, queue):
+            first, count = spans[span]
+            quarters = slice(2 * pair, 2 * pair + 2)
+            acc = bank_tile([P, 2, count], "out_pair_ps%d_%d" % (span, pair), bank)
+            for t in range(2):
+                product(acc[:, t, :], 2 * pair + t, span, 0, count)
+            nc.scalar.copy(out=out_f32[span][:, quarters], in_=acc[:])
+            queue.dma_start(out=out_rows[:, quarters, first : first + count], in_=out_f32[span][:, quarters])
+
+        def first_span_out():
+            quantise_z(FIRST)
+            for pair in range(2):
+                round_chunk(nc.scalar.copy, FIRST, pair * CHUNK, chunk_product(FIRST, pair * CHUNK))
+                store_pair(FIRST, pair, h_bank(pair), nc.sync)
+
+        def middle_span_out():
+            first, count = spans[MIDDLE]
+            quantise_z(MIDDLE)
+            acc = chunk_product(MIDDLE, 0)
+            nc.scalar.copy(out=out_f32[MIDDLE][:], in_=acc[:])
+            nc.sync.dma_start(out=out_rows[:, :, first : first + count], in_=out_f32[MIDDLE][:])
+            round_chunk(nc.scalar.copy, MIDDLE, 0, acc)
+
+        def last_span_out():
+            quantise_z(LAST)
+            round_chunk(nc.vector.tensor_copy, LAST, 0, chunk_product(LAST, 0))
+            for pair in range(2):
+                store_pair(LAST, pair, S // CHUNK + pair, nc.scalar)
+
+        def planes(span):
+            first, count = spans[span]
             half, lo = divmod(first, HALF)
             nc.vector.quantize_mx(
-                out=o_codes[half][:, lo : lo + count].bitcast(FP8X4), scales=o_sc[:, cols], in_=o_bf[c][:]
+                out=out_codes[half][:, lo : lo + count].bitcast(FP8X4),
+                scales=out_scales[:, first : first + count],
+                in_=out_woven[span][:],
             )
             if lo + count == HALF:
-                nc.sync.dma_start(out=out_words[:, half * HALF : (half + 1) * HALF], in_=o_codes[half][:].bitcast(I32))
+                nc.sync.dma_start(out=out_words[:, half * HALF : (half + 1) * HALF], in_=out_codes[half][:].bitcast(I32))
 
-        def fetch_far2(c, t):
-            first, count = spans[c]
-            fetch(far2[c][:, t, :], h[t], "q2", first, count)
-
-        def largest(c, rows=slice(0, PACK)):
-            first, count = spans[c]
-            lo = first % HALF
-            nc.vector.tensor_tensor(mid[c][:, rows], far2[c][:, rows], high[first // HALF][:, rows, lo : lo + count], MAX)
-
-        def weave(c, copy):
-            copy(out=woven8(z_bf[c][:]), in_=planar8(mid[c][:]))
-
-        fetch_far2(0, 0)
+        fetch_far2(FIRST, 0)
         fetch_far1(0, 1)
         fetch_far1(1, 0)
-        fetch_far2(0, 1)
+        fetch_far2(FIRST, 1)
         fetch_far1(1, 1)
         fetch_far1(2, 0)
-        fetch_far2(0, 2)
-        early, late = slice(0, PACK - 1), slice(PACK - 1, PACK)
-        raise_h(0, early)
-        raise_h(1, slice(0, 2))
-        largest(0, early)
-        fetch_far1(PACK - 1, 0)
-        fetch_far2(0, PACK - 1)
-        raise_h(0, late)
-        largest(0, late)
-        weave(0, nc.scalar.copy)
+        fetch_far2(FIRST, 2)
+        make_high(0, slice(0, 3))
+        make_high(1, slice(0, 2))
+        make_z(FIRST, slice(0, 3))
+        fetch_far1(3, 0)
+        fetch_far2(FIRST, 3)
+        make_high(0, slice(3, 4))
+        make_z(FIRST, slice(3, 4))
+        weave_z(FIRST, nc.scalar.copy)
         fetch_far1(2, 1)
         fetch_far1(3, 1)
-        second_product(0)
-        raise_h(1, slice(2, PACK))
+        first_span_out()
+        make_high(1, slice(2, 4))
         for t in range(PACK):
-            fetch_far2(1, t)
-        fetch_far2(2, 0)
-        largest(1)
-        fetch_far2(2, 1)
-        weave(1, nc.vector.tensor_copy)
-        fetch_far2(2, 2)
-        second_product(1)
-        fetch_far2(2, 3)
-        planes(0)
-        largest(2)
-        weave(2, nc.vector.tensor_copy)
-        planes(1)
-        second_product(last)
-        planes(last)
+            fetch_far2(MIDDLE, t)
+        fetch_far2(LAST, 0)
+        make_z(MIDDLE)
+        fetch_far2(LAST, 1)
+        weave_z(MIDDLE, nc.vector.tensor_copy)
+        fetch_far2(LAST, 2)
+        middle_span_out()
+        fetch_far2(LAST, 3)
+        planes(FIRST)
+        make_z(LAST)
+        weave_z(LAST, nc.vector.tensor_copy)
+        planes(MIDDLE)
+        last_span_out()
+        planes(LAST)
         for quad in range(QUADS):
             queue = nc.scalar if quad % 2 else nc.sync
             queue.dma_start(
                 out=out_2[0, 4 * quad : 4 * quad + 4, :].bitcast(I32),
-                in_=o_sc[32 * quad : 32 * quad + 4, :].bitcast(I32),
+                in_=out_scales[32 * quad : 32 * quad + 4, :].bitcast(I32),
             )

@@ -44,7 +44,8 @@ def tile_picked_opening_relu_po_kernel(
         def bank_tile(shape, name, bank):
             return ps.tile(shape, F32, name=name, tag="bank%d" % bank)
 
-        w1_raw = [tile([P, PACK, H], F32, "w1_raw%d" % g) for g in range(PASSES)]
+        w1_early = tile([P, PACK, H], F32, "w1_early")
+        w1_late = [tile([P, 2, H], F32, "w1_late%d" % pair) for pair in range(2)]
         x_table = [tile([P, T], I32, "x_table%d" % g) for g in range(PASSES)]
         x_scale_table = tile([P, T], U8, "x_scale_table")
         w2_raw = tile([P, 2 * N], U8, "w2_raw")
@@ -58,28 +59,31 @@ def tile_picked_opening_relu_po_kernel(
         ident = tile([P, P], F32, "ident")
         make_identity(nc, ident[:])
 
-        def load_w1(g):
-            rows = w1[P * PACK * g : P * PACK * (g + 1), :]
-            nc.sync.dma_start(out=w1_raw[g][:], in_=rows.rearrange("(p j) c -> p j c", j=PACK))
+        def w1_rows(g):
+            return w1[P * PACK * g : P * PACK * (g + 1), :].rearrange("(p j) c -> p j c", j=PACK)
+
+        def load_x(g):
+            nc.sync.dma_start(out=x_table[g][:], in_=x_words[g].rearrange("p c r -> p (c r)").bitcast(I32))
 
         nc.sync.dma_start(out=lists["offs"][:], in_=offs)
-        load_w1(0)
+        nc.sync.dma_start(out=w1_early[:], in_=w1_rows(0))
         for quad in range(QUADS):
             nc.sync.dma_start(
                 out=x_scale_table[32 * quad : 32 * quad + 4 * PASSES, :].bitcast(I32),
                 in_=x_scales[:, 4 * quad : 4 * quad + 4, :].bitcast(I32),
             )
-        load_w1(1)
+        load_x(1)
         nc.sync.dma_start(out=w2_raw[:].bitcast(I32), in_=w2_words[0].bitcast(I32))
-        for g in range(PASSES):
-            nc.sync.dma_start(out=x_table[g][:], in_=x_words[g].rearrange("p c r -> p (c r)").bitcast(I32))
-        nc.sync.dma_start(out=lists["p1"][:], in_=p1)
-        nc.sync.dma_start(out=lists["p2"][:], in_=p2)
         for quad in range(QUADS):
             nc.sync.dma_start(
                 out=w2_scale_raw[32 * quad : 32 * quad + 4, :].bitcast(I32),
                 in_=w2_scales[0, 4 * quad : 4 * quad + 4, :].bitcast(I32),
             )
+        load_x(0)
+        for pair in range(2):
+            nc.sync.dma_start(out=w1_late[pair][:], in_=w1_rows(1)[:, 2 * pair : 2 * pair + 2, :])
+        nc.sync.dma_start(out=lists["p1"][:], in_=p1)
+        nc.sync.dma_start(out=lists["p2"][:], in_=p2)
         nc.sync.dma_start(out=lists["q1"][:], in_=q1)
         nc.sync.dma_start(out=lists["q2"][:], in_=q2)
 
@@ -87,14 +91,24 @@ def tile_picked_opening_relu_po_kernel(
         w1_codes = [tile([P, H], U32, "w1_codes%d" % g) for g in range(PASSES)]
         w1_scales = [tile([P, H], U8, "w1_scales%d" % g) for g in range(PASSES)]
 
-        def round_w1(g):
-            dst = w1_bf[g][:].rearrange("p (t m j) -> p m j t", t=PACK, j=PACK)
-            src = w1_raw[g][:].rearrange("p j (m t) -> p m j t", t=PACK)
+        def round_early():
+            dst = w1_bf[0][:].rearrange("p (t m j) -> p m j t", t=PACK, j=PACK)
+            src = w1_early[:].rearrange("p j (m t) -> p m j t", t=PACK)
             nc.scalar.copy(out=dst[:, 0 : P // 2], in_=src[:, 0 : P // 2])
             nc.vector.tensor_copy(out=dst[:, P // 2 : P], in_=src[:, P // 2 : P])
 
-        def quantise_w1(g):
-            nc.vector.quantize_mx(out=w1_codes[g][:].bitcast(FP8X4), scales=w1_scales[g][:], in_=w1_bf[g][:])
+        def round_late(copy, pair, first, count):
+            dst = w1_bf[1][:].rearrange("p (t m j) -> p m t j", t=PACK, j=PACK)
+            src = w1_late[pair][:].rearrange("p j (m t) -> p m t j", t=PACK)
+            copy(out=dst[:, :, first : first + count, 2 * pair : 2 * pair + 2], in_=src[:, :, first : first + count, :])
+
+        def quantise_w1(g, first, count):
+            cols = slice(P * first, P * (first + count))
+            nc.vector.quantize_mx(
+                out=w1_codes[g][:, cols].bitcast(FP8X4),
+                scales=w1_scales[g][:, cols],
+                in_=w1_bf[g][:, PACK * P * first : PACK * P * (first + count)],
+            )
 
         x_codes = [tile([P, S], U32, "x_codes%d" % g) for g in range(PASSES)]
         x_picked_scales = tile([P, S], U8, "x_picked_scales")
@@ -107,24 +121,34 @@ def tile_picked_opening_relu_po_kernel(
                 x_codes[g][:, first : first + count], x_table[g][:].bitcast(U32).indirect(entries("offs", first, count))
             )
 
-        round_w1(0)
+        round_early()
         nc.vector.tensor_copy(x_picked_scales[:], x_scale_table[:].indirect(lists["offs"][:]))
-        quantise_w1(0)
-        round_w1(1)
-        quantise_w1(1)
+        quantise_w1(0, 0, PACK)
+        gather_words(1, 0, S)
         w2_dealt = tile([P, 2 * N], U8, "w2_dealt")
         w2_scale_dealt = tile([P, N], U8, "w2_scale_dealt")
         nc.vector.tensor_copy(
             out=w2_dealt[:].rearrange("p (t m b) -> p m t b", t=PACK, b=2),
             in_=w2_raw[:].rearrange("p (m t b) -> p m t b", t=PACK, b=2),
         )
+        nc.vector.tensor_copy(
+            out=w2_scale_dealt[:].rearrange("p (t m) -> p m t", t=PACK),
+            in_=w2_scale_raw[:].rearrange("p (m t) -> p m t", t=PACK),
+        )
         gather_words(0, 0, S)
-        gather_words(1, 0, HALF)
-        gather_words(1, HALF, HALF)
+        round_late(nc.scalar.copy, 0, 2, 2)
+        round_late(nc.vector.tensor_copy, 0, 0, 2)
+        round_late(nc.scalar.copy, 1, 2, 2)
+        round_late(nc.vector.tensor_copy, 1, 0, 1)
+        round_late(nc.vector.tensor_copy, 1, 1, 1)
+        quantise_w1(1, 0, 1)
+        quantise_w1(1, 1, 1)
+        quantise_w1(1, 2, 2)
 
-        pieces = [(0, 0, HALF), (0, HALF, CHUNK), (0, HALF + CHUNK, CHUNK)] + [(t, 0, S) for t in range(1, PACK)]
-        y_ps = [bank_tile([P, count], "y_ps%d" % i, i) for i, (t, first, count) in enumerate(pieces)]
-        y_bank = {t: i for i, (t, first, count) in enumerate(pieces)}
+        pieces = [(0, 0, HALF), (0, HALF, HALF)] + [(t, 0, S) for t in range(1, PACK)]
+        y_ps = [bank_tile([P, count], "y_ps%d" % i, i + 1) for i, (t, first, count) in enumerate(pieces)]
+        y_piece = {t: i for i, (t, first, count) in enumerate(pieces)}
+        y_bank = {t: y_piece[t] + 1 for t in range(PACK)}
 
         def first_product(i, g, start):
             t, first, count = pieces[i]
@@ -140,16 +164,11 @@ def tile_picked_opening_relu_po_kernel(
             )
 
         for g in range(PASSES):
-            for i in range(y_bank[2]):
+            for i in range(y_piece[2]):
                 first_product(i, g, g == 0)
-        for i in range(y_bank[2], len(pieces)):
+        for i in range(y_piece[2], len(pieces)):
             first_product(i, 1, True)
             first_product(i, 0, False)
-
-        nc.vector.tensor_copy(
-            out=w2_scale_dealt[:].rearrange("p (t m) -> p m t", t=PACK),
-            in_=w2_scale_raw[:].rearrange("p (m t) -> p m t", t=PACK),
-        )
 
         y_window = [tile([P, S if t == 0 else 2 * S], F32, "y_window%d" % t) for t in range(PACK)]
         y = [y_window[t][:, 0:S] for t in range(PACK)]
@@ -168,17 +187,15 @@ def tile_picked_opening_relu_po_kernel(
         ]
         high = [tile([P, PACK, HALF], BF16, "high%d" % half) for half in range(2)]
 
-        third, fourth = slice(HALF, HALF + CHUNK), slice(HALF + CHUNK, S)
         nc.scalar.copy(out=y[0][:, 0:HALF], in_=y_ps[0][:])
         nc.scalar.activation(own[0][:, 0:HALF], y_ps[0][:], COPY, scale=-1.0)
-        nc.scalar.copy(out=y[0][:, third], in_=y_ps[1][:])
-        nc.vector.tensor_copy(y[0][:, fourth], y_ps[2][:])
-        nc.scalar.activation(own[0][:, third], y_ps[1][:], COPY, scale=-1.0)
-        nc.scalar.activation(own[0][:, fourth], y_ps[2][:], COPY, scale=-1.0)
-        for t in range(1, PACK):
-            nc.scalar.copy(out=y[t], in_=y_ps[y_bank[t]][:])
+        nc.vector.tensor_copy(y[0][:, HALF:S], y_ps[1][:])
+        nc.scalar.activation(own[0][:, HALF:S], y_ps[1][:], COPY, scale=-1.0)
+
+        def empty_y(t):
+            nc.scalar.copy(out=y[t], in_=y_ps[y_piece[t]][:])
             if t < OFF_VECTOR:
-                nc.scalar.activation(own[t], y_ps[y_bank[t]][:], COPY, scale=-1.0)
+                nc.scalar.activation(own[t], y_ps[y_piece[t]][:], COPY, scale=-1.0)
             else:
                 nc.sync.dma_start(out=own[t], in_=y[t])
 
@@ -207,35 +224,40 @@ def tile_picked_opening_relu_po_kernel(
                     )
             return acc
 
-        def first_sum_bank(t):
-            return y_bank[3] - t % 2
-
-        def second_sum_bank(t):
-            return y_bank[1] - t % 2
-
         def h_bank(t):
-            return len(pieces) + t % 2
+            return len(pieces) + 1 + t % 2
 
-        def minus_h_off_vector(t):
-            over1, minus_low_turned = stage[t], turned[t]
-            nc.scalar.activation(over1[:], diff1[t][:], RELU, scale=-1.0)
-            acc = turned_sum([own[t], over1], "minus_low_ps%d" % t, first_sum_bank(t))
-            nc.scalar.copy(out=minus_low_turned[:], in_=acc[:])
-            acc = turned_sum([over1, diff2[t]], "near2_less_low_ps%d" % t, second_sum_bank(t))
-            nc.scalar.activation(over2_turned[t][:], acc[:], RELU, scale=-1.0)
-            return turned_sum([minus_low_turned, over2_turned[t]], "minus_h_ps%d" % t, h_bank(t))
+        sums = {}
+
+        def make_over1(t):
+            nc.scalar.activation(stage[t][:], diff1[t][:], RELU, scale=-1.0)
+
+        def sum_minus_low(t):
+            sums["low", t] = turned_sum([own[t], stage[t]], "minus_low_ps%d" % t, y_bank[t] - 1 + t)
+
+        def sum_near2_less_low(t):
+            sums["near2", t] = turned_sum([stage[t], diff2[t]], "near2_less_low_ps%d" % t, y_bank[2 * t])
+
+        def empty_low(t):
+            nc.scalar.copy(out=turned[t][:], in_=sums["low", t][:])
+
+        def make_over2(t):
+            nc.scalar.activation(over2_turned[t][:], sums["near2", t][:], RELU, scale=-1.0)
+
+        def sum_minus_h(t):
+            sums["h", t] = turned_sum([turned[t], over2_turned[t]], "minus_h_ps%d" % t, h_bank(t))
+
+        def empty_h(t):
+            sign = -1.0 if t < OFF_VECTOR else 1.0
+            nc.scalar.activation(h[t][:], sums["h", t][:], RELU, scale=sign)
+            nc.scalar.activation(h_bf[:, t, :], sums["h", t][:], RELU, scale=sign)
 
         def h_with_vector(t):
-            drop, h_turned = stage[t], turned[t]
-            nc.vector.scalar_tensor_tensor(out=drop[:], in0=diff1[t][:], scalar=0.0, in1=diff2[t][:], op0=MIN, op1=MIN)
-            acc = turned_sum([y[t], drop], "h_turned_ps%d" % t, first_sum_bank(t))
-            nc.scalar.copy(out=h_turned[:], in_=acc[:])
-            return turned_sum([h_turned], "h_ps%d" % t, h_bank(t))
-
-        def finish_h(t):
-            acc, sign = (minus_h_off_vector(t), -1.0) if t < OFF_VECTOR else (h_with_vector(t), 1.0)
-            nc.scalar.activation(h[t][:], acc[:], RELU, scale=sign)
-            nc.scalar.activation(h_bf[:, t, :], acc[:], RELU, scale=sign)
+            nc.vector.scalar_tensor_tensor(out=stage[t][:], in0=diff1[t][:], scalar=0.0, in1=diff2[t][:], op0=MIN, op1=MIN)
+            sums["low", t] = turned_sum([y[t], stage[t]], "h_turned_ps%d" % t, y_bank[2])
+            empty_low(t)
+            sums["h", t] = turned_sum([turned[t]], "h_ps%d" % t, h_bank(t))
+            empty_h(t)
 
         def fetch_h(dst, t, name, first, count):
             nc.vector.tensor_copy(dst, h[t][:].indirect(entries(name, first, count)))
@@ -249,13 +271,34 @@ def tile_picked_opening_relu_po_kernel(
             far = far1_second[quarters.start // 2][:] if half else far1_first[:, quarters]
             nc.vector.tensor_tensor(high[half][:, quarters], far, h_bf[:, quarters, cols], MAX)
 
-        for t in range(PACK):
-            fetch_diff(diff1[t], t, "p1")
-            if t > 0:
-                finish_h(t - 1)
-            fetch_diff(diff2[t], t, "p2")
+        empty_y(1)
+        fetch_diff(diff1[0], 0, "p1")
+        make_over1(0)
+        empty_y(2)
+        empty_y(3)
+        sum_minus_low(0)
+        empty_low(0)
+        fetch_diff(diff2[0], 0, "p2")
+        sum_near2_less_low(0)
+        fetch_diff(diff1[1], 1, "p1")
+        make_over1(1)
+        make_over2(0)
+        sum_minus_low(1)
+        sum_minus_h(0)
+        empty_low(1)
+        fetch_diff(diff2[1], 1, "p2")
+        sum_near2_less_low(1)
+        empty_h(0)
+        make_over2(1)
+        sum_minus_h(1)
+        empty_h(1)
+        fetch_diff(diff1[2], 2, "p1")
+        fetch_diff(diff2[2], 2, "p2")
+        fetch_diff(diff1[3], 3, "p1")
+        h_with_vector(2)
+        fetch_diff(diff2[3], 3, "p2")
         fetch_far1(0, 0)
-        finish_h(PACK - 1)
+        h_with_vector(3)
 
         spans = [(0, HALF), (HALF, CHUNK), (HALF + CHUNK, CHUNK)]
         FIRST, MIDDLE, LAST = range(len(spans))

@@ -176,7 +176,7 @@ def tile_picked_opening_relu_po_kernel(
         diff1 = [tile([P, S], F32, "diff1_%d" % t) for t in range(PACK)]
         diff2 = [tile([P, S], F32, "diff2_%d" % t) for t in range(PACK)]
         stage = [tile([P, S], F32, "stage%d" % t) for t in range(PACK)]
-        turned = [tile([P, S], F32, "turned%d" % t) for t in range(PACK)]
+        turned = [tile([P, S], F32, "turned%d" % t) for t in range(OFF_VECTOR)]
         over2_turned = [tile([P, S], F32, "over2_turned%d" % t) for t in range(OFF_VECTOR)]
         h = [tile([P, S], F32, "h%d" % t) for t in range(PACK)]
         h_bf = tile([P, PACK, S], BF16, "h_bf")
@@ -193,10 +193,11 @@ def tile_picked_opening_relu_po_kernel(
         nc.scalar.activation(own[0][:, HALF:S], y_ps[1][:], COPY, scale=-1.0)
 
         def empty_y(t):
-            nc.scalar.copy(out=y[t], in_=y_ps[y_piece[t]][:])
             if t < OFF_VECTOR:
+                nc.scalar.copy(out=y[t], in_=y_ps[y_piece[t]][:])
                 nc.scalar.activation(own[t], y_ps[y_piece[t]][:], COPY, scale=-1.0)
             else:
+                nc.scalar.activation(y[t], y_ps[y_piece[t]][:], RELU)
                 nc.sync.dma_start(out=own[t], in_=y[t])
 
         def fetch_diff(dst, t, name):
@@ -248,16 +249,14 @@ def tile_picked_opening_relu_po_kernel(
             sums["h", t] = turned_sum([turned[t], over2_turned[t]], "minus_h_ps%d" % t, h_bank(t))
 
         def empty_h(t):
-            sign = -1.0 if t < OFF_VECTOR else 1.0
+            sign = -1.0
             nc.scalar.activation(h[t][:], sums["h", t][:], RELU, scale=sign)
             nc.scalar.activation(h_bf[:, t, :], sums["h", t][:], RELU, scale=sign)
 
         def h_with_vector(t):
             nc.vector.scalar_tensor_tensor(out=stage[t][:], in0=diff1[t][:], scalar=0.0, in1=diff2[t][:], op0=MIN, op1=MIN)
-            sums["low", t] = turned_sum([y[t], stage[t]], "h_turned_ps%d" % t, y_bank[2])
-            empty_low(t)
-            sums["h", t] = turned_sum([turned[t]], "h_ps%d" % t, h_bank(t))
-            empty_h(t)
+            nc.gpsimd.tensor_tensor(h[t][:], y[t], stage[t][:], ADD)
+            nc.scalar.copy(out=h_bf[:, t, :], in_=h[t][:])
 
         def fetch_h(dst, t, name, first, count):
             nc.vector.tensor_copy(dst, h[t][:].indirect(entries(name, first, count)))
@@ -295,10 +294,10 @@ def tile_picked_opening_relu_po_kernel(
         fetch_diff(diff1[2], 2, "p1")
         fetch_diff(diff2[2], 2, "p2")
         fetch_diff(diff1[3], 3, "p1")
-        h_with_vector(2)
         fetch_diff(diff2[3], 3, "p2")
-        fetch_far1(0, 0)
+        h_with_vector(2)
         h_with_vector(3)
+        fetch_far1(0, 0)
 
         spans = [(0, HALF), (HALF, CHUNK), (HALF + CHUNK, CHUNK)]
         FIRST, MIDDLE, LAST = range(len(spans))

@@ -14,6 +14,7 @@ FP4X4 = mybir.dt.float4_e2m1fn_x4
 MAX = mybir.AluOpType.max
 MIN = mybir.AluOpType.min
 ADD = mybir.AluOpType.add
+MULT = mybir.AluOpType.mult
 SUB = mybir.AluOpType.subtract
 RELU = mybir.ActivationFunctionType.Relu
 COPY = mybir.ActivationFunctionType.Copy
@@ -27,7 +28,8 @@ QUADS = 4
 HALF = S // 2
 CHUNK = 128
 STRIPE = 16
-OFF_VECTOR = 2
+ORDER = (0, 1, 3, 2)
+ON_VECTOR = 2
 
 
 def tile_picked_opening_relu_po_kernel(
@@ -166,26 +168,28 @@ def tile_picked_opening_relu_po_kernel(
         for g in range(PASSES):
             for i in range(y_piece[2]):
                 first_product(i, g, g == 0)
-        for i in range(y_piece[2], len(pieces)):
-            first_product(i, 1, True)
-            first_product(i, 0, False)
+        for t in ORDER[2:]:
+            first_product(y_piece[t], 1, True)
+            first_product(y_piece[t], 0, False)
 
         y_window = [tile([P, S if t == 0 else 2 * S], F32, "y_window%d" % t) for t in range(PACK)]
         y = [y_window[t][:, 0:S] for t in range(PACK)]
-        own = [y_window[t + 1][:, S : 2 * S] for t in range(PACK - 1)] + [tile([P, S], F32, "own_last")[:]]
+        own = {ORDER[i]: y_window[ORDER[i + 1]][:, S : 2 * S] for i in range(PACK - 1)}
+        own[ORDER[-1]] = tile([P, S], F32, "own_last")[:]
         diff1 = [tile([P, S], F32, "diff1_%d" % t) for t in range(PACK)]
         diff2 = [tile([P, S], F32, "diff2_%d" % t) for t in range(PACK)]
-        stage = [tile([P, S], F32, "stage%d" % t) for t in range(PACK)]
-        turned = [tile([P, S], F32, "turned%d" % t) for t in range(OFF_VECTOR)]
-        over2_turned = [tile([P, S], F32, "over2_turned%d" % t) for t in range(OFF_VECTOR)]
-        h = [tile([P, S], F32, "h%d" % t) for t in range(PACK)]
+        stage = [tile([P, S], F32, "stage%d" % t) for t in range(PACK - 1)]
+        turned = {t: tile([P, S], F32, "turned%d" % t) for t in ORDER[:-1]}
+        over2_turned = {t: tile([P, S], F32, "over2_turned%d" % t) for t in ORDER[:-1]}
+        stage.append(tile([P, S], F32, "stage3", tag="over2_turned0"))
+        h = [tile([P, S], F32, "h%d" % t, tag="over2_turned0" if t == ON_VECTOR else None) for t in range(PACK)]
         h_bf = tile([P, PACK, S], BF16, "h_bf")
         far1_first = tile([P, PACK, HALF], BF16, "far1_first", tag="far1")
         far1_second = [
             tile([P, 2, HALF], BF16, "far1_second0"),
-            tile([P, 2, HALF], BF16, "far1_second1", tag="far1"),
         ]
         high = [tile([P, PACK, HALF], BF16, "high%d" % half) for half in range(2)]
+        far1_second.append(tile([P, 2, HALF], BF16, "far1_second1", tag="high0"))
 
         nc.scalar.copy(out=y[0][:, 0:HALF], in_=y_ps[0][:])
         nc.scalar.activation(own[0][:, 0:HALF], y_ps[0][:], COPY, scale=-1.0)
@@ -193,7 +197,7 @@ def tile_picked_opening_relu_po_kernel(
         nc.scalar.activation(own[0][:, HALF:S], y_ps[1][:], COPY, scale=-1.0)
 
         def empty_y(t):
-            if t < OFF_VECTOR:
+            if t != ON_VECTOR:
                 nc.scalar.copy(out=y[t], in_=y_ps[y_piece[t]][:])
                 nc.scalar.activation(own[t], y_ps[y_piece[t]][:], COPY, scale=-1.0)
             else:
@@ -208,7 +212,7 @@ def tile_picked_opening_relu_po_kernel(
                     dst[:, cols],
                     y_window[t][:].indirect(entries(name, first, step)),
                     own[t][:, cols],
-                    ADD if t < OFF_VECTOR else SUB,
+                    SUB if t == ON_VECTOR else ADD,
                 )
 
         def turned_sum(terms, name, bank):
@@ -234,10 +238,10 @@ def tile_picked_opening_relu_po_kernel(
             nc.scalar.activation(stage[t][:], diff1[t][:], RELU, scale=-1.0)
 
         def sum_minus_low(t):
-            sums["low", t] = turned_sum([own[t], stage[t]], "minus_low_ps%d" % t, y_bank[t] - 1 + t)
+            sums["low", t] = turned_sum([own[t], stage[t]], "minus_low_ps%d" % t, {0: 1, 1: 3, 3: 3}[t])
 
         def sum_near2_less_low(t):
-            sums["near2", t] = turned_sum([stage[t], diff2[t]], "near2_less_low_ps%d" % t, y_bank[2 * t])
+            sums["near2", t] = turned_sum([stage[t], diff2[t]], "near2_less_low_ps%d" % t, 2)
 
         def empty_low(t):
             nc.scalar.copy(out=turned[t][:], in_=sums["low", t][:])
@@ -246,17 +250,18 @@ def tile_picked_opening_relu_po_kernel(
             nc.scalar.activation(over2_turned[t][:], sums["near2", t][:], RELU, scale=-1.0)
 
         def sum_minus_h(t):
-            sums["h", t] = turned_sum([turned[t], over2_turned[t]], "minus_h_ps%d" % t, h_bank(t))
+            sums["h", t] = turned_sum([turned[t], over2_turned[t]], "minus_h_ps%d" % t, h_bank(ORDER.index(t)))
 
         def empty_h(t):
-            sign = -1.0
-            nc.scalar.activation(h[t][:], sums["h", t][:], RELU, scale=sign)
-            nc.scalar.activation(h_bf[:, t, :], sums["h", t][:], RELU, scale=sign)
+            nc.scalar.activation(h[t][:], sums["h", t][:], RELU, scale=-1.0)
+
+        def round_h(t):
+            nc.scalar.activation(h_bf[:, t, :], sums["h", t][:], RELU, scale=-1.0)
 
         def h_with_vector(t):
             nc.vector.scalar_tensor_tensor(out=stage[t][:], in0=diff1[t][:], scalar=0.0, in1=diff2[t][:], op0=MIN, op1=MIN)
             nc.gpsimd.tensor_tensor(h[t][:], y[t], stage[t][:], ADD)
-            nc.scalar.copy(out=h_bf[:, t, :], in_=h[t][:])
+            nc.gpsimd.tensor_scalar(h_bf[:, t, :], h[t][:], 1.0, 0.0, MULT, ADD)
 
         def fetch_h(dst, t, name, first, count):
             nc.vector.tensor_copy(dst, h[t][:].indirect(entries(name, first, count)))
@@ -273,10 +278,10 @@ def tile_picked_opening_relu_po_kernel(
         empty_y(1)
         fetch_diff(diff1[0], 0, "p1")
         make_over1(0)
-        empty_y(2)
         empty_y(3)
         sum_minus_low(0)
         empty_low(0)
+        empty_y(2)
         fetch_diff(diff2[0], 0, "p2")
         sum_near2_less_low(0)
         fetch_diff(diff1[1], 1, "p1")
@@ -287,17 +292,26 @@ def tile_picked_opening_relu_po_kernel(
         empty_low(1)
         fetch_diff(diff2[1], 1, "p2")
         sum_near2_less_low(1)
+        fetch_diff(diff1[3], 3, "p1")
         empty_h(0)
+        make_over1(3)
+        round_h(0)
         make_over2(1)
+        sum_minus_low(3)
         sum_minus_h(1)
         empty_h(1)
+        empty_low(3)
+        round_h(1)
+        fetch_diff(diff2[3], 3, "p2")
+        sum_near2_less_low(3)
+        make_over2(3)
+        sum_minus_h(3)
         fetch_diff(diff1[2], 2, "p1")
         fetch_diff(diff2[2], 2, "p2")
-        fetch_diff(diff1[3], 3, "p1")
-        fetch_diff(diff2[3], 3, "p2")
-        h_with_vector(2)
-        h_with_vector(3)
         fetch_far1(0, 0)
+        h_with_vector(2)
+        empty_h(3)
+        round_h(3)
 
         spans = [(0, HALF), (HALF, CHUNK), (HALF + CHUNK, CHUNK)]
         FIRST, MIDDLE, LAST = range(len(spans))
@@ -407,13 +421,11 @@ def tile_picked_opening_relu_po_kernel(
         fetch_far1(1, 1)
         fetch_far1(2, 0)
         fetch_far2(FIRST, 2)
-        make_high(0, slice(0, 3))
-        make_high(1, slice(0, 2))
-        make_z(FIRST, slice(0, 3))
         fetch_far1(3, 0)
         fetch_far2(FIRST, 3)
-        make_high(0, slice(3, 4))
-        make_z(FIRST, slice(3, 4))
+        make_high(0, slice(0, PACK))
+        make_high(1, slice(0, 2))
+        make_z(FIRST)
         weave_z(FIRST, nc.scalar.copy)
         fetch_far1(2, 1)
         fetch_far1(3, 1)

@@ -348,7 +348,7 @@ def tile_picked_opening_relu_po_kernel(
             )
 
         def weave_z(span, copy):
-            weave(copy, z_woven[span][:], z_planar[span][:], 8)
+            weave(copy, z_woven[span][:], z_planar[span][:], 4)
 
         def quantise_z(span):
             nc.vector.quantize_mx(out=z_codes[span][:].bitcast(FP8X4), scales=z_scales[span][:], in_=z_woven[span][:])

@@ -25,11 +25,12 @@ P = 128
 PACK = 4
 PASSES = K // (P * PACK)
 QUADS = 4
+BANKS = 8
 HALF = S // 2
 CHUNK = 128
 STRIPE = 16
 ORDER = (0, 1, 3, 2)
-ON_VECTOR = 2
+ON_VECTOR = ORDER[-1]
 
 
 def tile_picked_opening_relu_po_kernel(
@@ -150,7 +151,6 @@ def tile_picked_opening_relu_po_kernel(
         pieces = [(0, 0, HALF), (0, HALF, HALF)] + [(t, 0, S) for t in range(1, PACK)]
         y_ps = [bank_tile([P, count], "y_ps%d" % i, i + 1) for i, (t, first, count) in enumerate(pieces)]
         y_piece = {t: i for i, (t, first, count) in enumerate(pieces)}
-        y_bank = {t: y_piece[t] + 1 for t in range(PACK)}
 
         def first_product(i, g, start):
             t, first, count = pieces[i]
@@ -179,15 +179,13 @@ def tile_picked_opening_relu_po_kernel(
         diff1 = [tile([P, S], F32, "diff1_%d" % t) for t in range(PACK)]
         diff2 = [tile([P, S], F32, "diff2_%d" % t) for t in range(PACK)]
         stage = [tile([P, S], F32, "stage%d" % t) for t in range(PACK - 1)]
-        turned = {t: tile([P, S], F32, "turned%d" % t) for t in ORDER[:-1]}
+        low_turned = {t: tile([P, S], F32, "low_turned%d" % t) for t in ORDER[:-1]}
         over2_turned = {t: tile([P, S], F32, "over2_turned%d" % t) for t in ORDER[:-1]}
         stage.append(tile([P, S], F32, "stage3", tag="over2_turned0"))
         h = [tile([P, S], F32, "h%d" % t, tag="over2_turned0" if t == ON_VECTOR else None) for t in range(PACK)]
-        h_bf = tile([P, PACK, S], BF16, "h_bf")
-        far1_first = tile([P, PACK, HALF], BF16, "far1_first", tag="far1")
-        far1_second = [
-            tile([P, 2, HALF], BF16, "far1_second0"),
-        ]
+        h_bf = tile([P, PACK, S], BF16, "h_bf", tag="over2_turned3")
+        far1_first = tile([P, PACK, HALF], BF16, "far1_first")
+        far1_second = [tile([P, 2, HALF], BF16, "far1_second0")]
         high = [tile([P, PACK, HALF], BF16, "high%d" % half) for half in range(2)]
         far1_second.append(tile([P, 2, HALF], BF16, "far1_second1", tag="high0"))
 
@@ -229,8 +227,11 @@ def tile_picked_opening_relu_po_kernel(
                     )
             return acc
 
-        def h_bank(t):
-            return len(pieces) + 1 + t % 2
+        low_bank = {0: 1, 1: y_piece[1] + 1, 3: y_piece[1] + 1}
+        near2_bank = y_piece[0] + 1
+
+        def h_bank(turn):
+            return (len(pieces) + 1 + turn) % BANKS
 
         sums = {}
 
@@ -238,19 +239,19 @@ def tile_picked_opening_relu_po_kernel(
             nc.scalar.activation(stage[t][:], diff1[t][:], RELU, scale=-1.0)
 
         def sum_minus_low(t):
-            sums["low", t] = turned_sum([own[t], stage[t]], "minus_low_ps%d" % t, {0: 1, 1: 3, 3: 3}[t])
+            sums["low", t] = turned_sum([own[t], stage[t]], "minus_low_ps%d" % t, low_bank[t])
 
         def sum_near2_less_low(t):
-            sums["near2", t] = turned_sum([stage[t], diff2[t]], "near2_less_low_ps%d" % t, 2)
+            sums["near2", t] = turned_sum([stage[t], diff2[t]], "near2_less_low_ps%d" % t, near2_bank)
 
         def empty_low(t):
-            nc.scalar.copy(out=turned[t][:], in_=sums["low", t][:])
+            nc.scalar.copy(out=low_turned[t][:], in_=sums["low", t][:])
 
         def make_over2(t):
             nc.scalar.activation(over2_turned[t][:], sums["near2", t][:], RELU, scale=-1.0)
 
         def sum_minus_h(t):
-            sums["h", t] = turned_sum([turned[t], over2_turned[t]], "minus_h_ps%d" % t, h_bank(ORDER.index(t)))
+            sums["h", t] = turned_sum([low_turned[t], over2_turned[t]], "minus_h_ps%d" % t, h_bank(ORDER.index(t)))
 
         def empty_h(t):
             nc.scalar.activation(h[t][:], sums["h", t][:], RELU, scale=-1.0)
@@ -295,13 +296,11 @@ def tile_picked_opening_relu_po_kernel(
         fetch_diff(diff1[3], 3, "p1")
         empty_h(0)
         make_over1(3)
-        round_h(0)
         make_over2(1)
         sum_minus_low(3)
         sum_minus_h(1)
         empty_h(1)
         empty_low(3)
-        round_h(1)
         fetch_diff(diff2[3], 3, "p2")
         sum_near2_less_low(3)
         make_over2(3)
@@ -309,9 +308,10 @@ def tile_picked_opening_relu_po_kernel(
         fetch_diff(diff1[2], 2, "p1")
         fetch_diff(diff2[2], 2, "p2")
         fetch_far1(0, 0)
-        h_with_vector(2)
         empty_h(3)
-        round_h(3)
+        for t in ORDER[:-1]:
+            round_h(t)
+        h_with_vector(2)
 
         spans = [(0, HALF), (HALF, CHUNK), (HALF + CHUNK, CHUNK)]
         FIRST, MIDDLE, LAST = range(len(spans))
@@ -330,25 +330,23 @@ def tile_picked_opening_relu_po_kernel(
         out_rows = out_0.rearrange("(p t) j -> p t j", t=PACK)
         out_words = out_1[0].rearrange("p c r -> p (c r)").bitcast(I32)
 
-        def weave(copy, dst, src, run):
+        def weave(copy, dst, src):
             copy(
-                out=dst.rearrange("p (n i t) -> p n t i", i=run, t=PACK),
-                in_=src.rearrange("p t (n i) -> p n t i", i=run),
+                out=dst.rearrange("p (n i t) -> p n t i", i=4, t=PACK),
+                in_=src.rearrange("p t (n i) -> p n t i", i=4),
             )
 
         def fetch_far2(span, t):
             first, count = spans[span]
             fetch_h(far2[span][:, t, :], t, "q2", first, count)
 
-        def make_z(span, quarters=slice(0, PACK)):
+        def make_z(span):
             first, count = spans[span]
             half, lo = divmod(first, HALF)
-            nc.vector.tensor_tensor(
-                z_planar[span][:, quarters], far2[span][:, quarters], high[half][:, quarters, lo : lo + count], MAX
-            )
+            nc.vector.tensor_tensor(z_planar[span][:], far2[span][:], high[half][:, :, lo : lo + count], MAX)
 
         def weave_z(span, copy):
-            weave(copy, z_woven[span][:], z_planar[span][:], 4)
+            weave(copy, z_woven[span][:], z_planar[span][:])
 
         def quantise_z(span):
             nc.vector.quantize_mx(out=z_codes[span][:].bitcast(FP8X4), scales=z_scales[span][:], in_=z_woven[span][:])
@@ -372,7 +370,7 @@ def tile_picked_opening_relu_po_kernel(
             return acc
 
         def round_chunk(copy, span, lo, acc):
-            weave(copy, out_woven[span][:, PACK * lo : PACK * (lo + CHUNK)], acc[:], 4)
+            weave(copy, out_woven[span][:, PACK * lo : PACK * (lo + CHUNK)], acc[:])
 
         def store_pair(span, pair, bank, queue):
             first, count = spans[span]

@@ -1,7 +1,6 @@
 from contextlib import ExitStack
 
 import concourse.mybir as mybir
-from concourse.masks import make_identity
 
 F32 = mybir.dt.float32
 BF16 = mybir.dt.bfloat16
@@ -13,9 +12,6 @@ FP8X4 = mybir.dt.float8_e4m3fn_x4
 FP4X4 = mybir.dt.float4_e2m1fn_x4
 MAX = mybir.AluOpType.max
 MIN = mybir.AluOpType.min
-ADD = mybir.AluOpType.add
-MULT = mybir.AluOpType.mult
-SUB = mybir.AluOpType.subtract
 RELU = mybir.ActivationFunctionType.Relu
 COPY = mybir.ActivationFunctionType.Copy
 
@@ -25,12 +21,9 @@ P = 128
 PACK = 4
 PASSES = K // (P * PACK)
 QUADS = 4
-BANKS = 8
 HALF = S // 2
 CHUNK = 128
 STRIPE = 16
-ORDER = (0, 1, 3, 2)
-ON_VECTOR = ORDER[-1]
 
 
 def tile_picked_opening_relu_po_kernel(
@@ -59,8 +52,6 @@ def tile_picked_opening_relu_po_kernel(
 
         nc.gpsimd.memset(x_scale_table[:].bitcast(I32), 0)
         nc.vector.memset(w2_scale_raw[:].bitcast(I32), 0)
-        ident = tile([P, P], F32, "ident")
-        make_identity(nc, ident[:])
 
         def w1_rows(g):
             return w1[P * PACK * g : P * PACK * (g + 1), :].rearrange("(p j) c -> p j c", j=PACK)
@@ -168,158 +159,46 @@ def tile_picked_opening_relu_po_kernel(
         for g in range(PASSES):
             for i in range(y_piece[2]):
                 first_product(i, g, g == 0)
-        for t in ORDER[2:]:
+        for t in range(2, PACK):
             first_product(y_piece[t], 1, True)
             first_product(y_piece[t], 0, False)
 
-        y_window = [tile([P, S if t == 0 else 2 * S], F32, "y_window%d" % t) for t in range(PACK)]
+        y_window = [tile([P, 2 * S], F32, "y_window%d" % t) for t in range(PACK)]
         y = [y_window[t][:, 0:S] for t in range(PACK)]
-        own = {ORDER[i]: y_window[ORDER[i + 1]][:, S : 2 * S] for i in range(PACK - 1)}
-        own[ORDER[-1]] = tile([P, S], F32, "own_last")[:]
-        diff1 = [tile([P, S], F32, "diff1_%d" % t) for t in range(PACK)]
-        diff2 = [tile([P, S], F32, "diff2_%d" % t) for t in range(PACK)]
-        stage = [tile([P, S], F32, "stage%d" % t) for t in range(PACK - 1)]
-        low_turned = {t: tile([P, S], F32, "low_turned%d" % t) for t in ORDER[:-1]}
-        over2_turned = {t: tile([P, S], F32, "over2_turned%d" % t) for t in ORDER[:-1]}
-        stage.append(tile([P, S], F32, "stage3", tag="over2_turned0"))
-        h = [tile([P, S], F32, "h%d" % t, tag="over2_turned0" if t == ON_VECTOR else None) for t in range(PACK)]
-        h_bf = tile([P, PACK, S], BF16, "h_bf", tag="over2_turned3")
-        far1_first = tile([P, PACK, HALF], BF16, "far1_first")
-        far1_second = [tile([P, 2, HALF], BF16, "far1_second0")]
-        high = [tile([P, PACK, HALF], BF16, "high%d" % half) for half in range(2)]
-        far1_second.append(tile([P, 2, HALF], BF16, "far1_second1", tag="high0"))
+        for t in range(PACK):
+            nc.gpsimd.memset(y_window[t][:, S : 2 * S], 0.0)
+        near = {(name, t): tile([P, S], F32, "near_%s_%d" % (name, t)) for name in ("p1", "p2") for t in range(PACK)}
+        h = [tile([P, S], F32, "h%d" % t) for t in range(PACK)]
 
-        nc.scalar.copy(out=y[0][:, 0:HALF], in_=y_ps[0][:])
-        nc.scalar.activation(own[0][:, 0:HALF], y_ps[0][:], COPY, scale=-1.0)
-        nc.vector.tensor_copy(y[0][:, HALF:S], y_ps[1][:])
-        nc.scalar.activation(own[0][:, HALF:S], y_ps[1][:], COPY, scale=-1.0)
+        def gather_vector(dst, window):
+            nc.vector.tensor_copy(dst, window)
+
+        def gather_scalar(dst, window):
+            nc.scalar.activation(dst, window, COPY)
 
         def empty_y(t):
-            if t != ON_VECTOR:
-                nc.scalar.copy(out=y[t], in_=y_ps[y_piece[t]][:])
-                nc.scalar.activation(own[t], y_ps[y_piece[t]][:], COPY, scale=-1.0)
-            else:
-                nc.scalar.activation(y[t], y_ps[y_piece[t]][:], RELU)
-                nc.sync.dma_start(out=own[t], in_=y[t])
+            nc.scalar.activation(y[t], y_ps[y_piece[t]][:], RELU)
 
-        def fetch_diff(dst, t, name):
-            step = y_window[t].shape[1] // 2
-            for first in range(0, S, step):
-                cols = slice(first, first + step)
-                nc.vector.tensor_tensor(
-                    dst[:, cols],
-                    y_window[t][:].indirect(entries(name, first, step)),
-                    own[t][:, cols],
-                    SUB if t == ON_VECTOR else ADD,
-                )
+        def fetch_near(gather, name, t):
+            gather(near[name, t][:], y_window[t][:].indirect(lists[name][:]))
 
-        def turned_sum(terms, name, bank):
-            acc = bank_tile([P, S], name, bank)
-            for i, term in enumerate(terms):
-                for lo in range(0, S, P):
-                    nc.tensor.matmul(
-                        out=acc[:, lo : lo + P],
-                        lhsT=term[:, lo : lo + P],
-                        rhs=ident[:],
-                        start=(i == 0 and lo == 0),
-                        stop=(i == len(terms) - 1 and lo == S - P),
-                        is_transpose=True,
-                    )
-            return acc
+        def min_with_own(name, t):
+            nc.vector.tensor_tensor(near[name, t][:], near[name, t][:], y[t], MIN)
 
-        low_bank = {0: 1, 1: y_piece[1] + 1, 3: y_piece[1] + 1}
-        near2_bank = y_piece[0] + 1
-
-        def h_bank(turn):
-            return (len(pieces) + 1 + turn) % BANKS
-
-        sums = {}
-
-        def make_over1(t):
-            nc.scalar.activation(stage[t][:], diff1[t][:], RELU, scale=-1.0)
-
-        def sum_minus_low(t):
-            sums["low", t] = turned_sum([own[t], stage[t]], "minus_low_ps%d" % t, low_bank[t])
-
-        def sum_near2_less_low(t):
-            sums["near2", t] = turned_sum([stage[t], diff2[t]], "near2_less_low_ps%d" % t, near2_bank)
-
-        def empty_low(t):
-            nc.scalar.copy(out=low_turned[t][:], in_=sums["low", t][:])
-
-        def make_over2(t):
-            nc.scalar.activation(over2_turned[t][:], sums["near2", t][:], RELU, scale=-1.0)
-
-        def sum_minus_h(t):
-            sums["h", t] = turned_sum([low_turned[t], over2_turned[t]], "minus_h_ps%d" % t, h_bank(ORDER.index(t)))
-
-        def empty_h(t):
-            nc.scalar.activation(h[t][:], sums["h", t][:], RELU, scale=-1.0)
-
-        def round_h(t):
-            nc.scalar.activation(h_bf[:, t, :], sums["h", t][:], RELU, scale=-1.0)
-
-        def h_with_vector(t):
-            nc.vector.scalar_tensor_tensor(out=stage[t][:], in0=diff1[t][:], scalar=0.0, in1=diff2[t][:], op0=MIN, op1=MIN)
-            nc.gpsimd.tensor_tensor(h[t][:], y[t], stage[t][:], ADD)
-            nc.gpsimd.tensor_scalar(h_bf[:, t, :], h[t][:], 1.0, 0.0, MULT, ADD)
-
-        def fetch_h(dst, t, name, first, count):
-            nc.vector.tensor_copy(dst, h[t][:].indirect(entries(name, first, count)))
-
-        def fetch_far1(t, half):
-            dst = far1_second[t // 2][:, t % 2, :] if half else far1_first[:, t, :]
-            fetch_h(dst, t, "q1", half * HALF, HALF)
-
-        def make_high(half, quarters):
-            cols = slice(half * HALF, (half + 1) * HALF)
-            far = far1_second[quarters.start // 2][:] if half else far1_first[:, quarters]
-            nc.vector.tensor_tensor(high[half][:, quarters], far, h_bf[:, quarters, cols], MAX)
-
-        empty_y(1)
-        fetch_diff(diff1[0], 0, "p1")
-        make_over1(0)
-        empty_y(3)
-        sum_minus_low(0)
-        empty_low(0)
-        empty_y(2)
-        fetch_diff(diff2[0], 0, "p2")
-        sum_near2_less_low(0)
-        fetch_diff(diff1[1], 1, "p1")
-        make_over1(1)
-        make_over2(0)
-        sum_minus_low(1)
-        sum_minus_h(0)
-        empty_low(1)
-        fetch_diff(diff2[1], 1, "p2")
-        sum_near2_less_low(1)
-        fetch_diff(diff1[3], 3, "p1")
-        empty_h(0)
-        make_over1(3)
-        make_over2(1)
-        sum_minus_low(3)
-        sum_minus_h(1)
-        empty_h(1)
-        empty_low(3)
-        fetch_diff(diff2[3], 3, "p2")
-        sum_near2_less_low(3)
-        make_over2(3)
-        sum_minus_h(3)
-        fetch_diff(diff1[2], 2, "p1")
-        fetch_diff(diff2[2], 2, "p2")
-        fetch_far1(0, 0)
-        empty_h(3)
-        for t in ORDER[:-1]:
-            round_h(t)
-        h_with_vector(2)
+        def make_h(t):
+            nc.vector.tensor_tensor(h[t][:], near["p1", t][:], near["p2", t][:], MIN)
 
         spans = [(0, HALF), (HALF, CHUNK), (HALF + CHUNK, CHUNK)]
         FIRST, MIDDLE, LAST = range(len(spans))
-        z_planar = [
-            tile([P, PACK, count], BF16, "z_planar%d" % first, tag="held" if first == 0 else None) for first, count in spans
-        ]
-        far2_late = tile([P, 2, PACK, CHUNK], BF16, "far2_late", tag="held")
-        far2 = [tile([P, PACK, HALF], BF16, "far2_first"), far2_late[:, 0], far2_late[:, 1]]
+        far1_first = [tile([P, HALF], F32, "far1_first%d" % t) for t in range(PACK)]
+        far1_second = tile([P, PACK, HALF], F32, "far1_second", tag="near_p1_3")
+        high = [tile([P, PACK, HALF], F32, "high_first"), far1_second]
+        far2_tags = [None, "far1_first2", "near_p2_3"]
+        far2 = [tile([P, PACK, count], F32, "far2_%d" % first, tag=far2_tags[i]) for i, (first, count) in enumerate(spans)]
+
+        def far1(half, t):
+            return far1_second[:, t, :] if half else far1_first[t][:]
+
         z_woven = [tile([P, PACK * count], BF16, "z_woven%d" % first) for first, count in spans]
         out_woven = [tile([P, PACK * count], BF16, "out_woven%d" % first) for first, count in spans]
         z_codes = [tile([P, count], U32, "z_codes%d" % first) for first, count in spans]
@@ -330,76 +209,55 @@ def tile_picked_opening_relu_po_kernel(
         out_rows = out_0.rearrange("(p t) j -> p t j", t=PACK)
         out_words = out_1[0].rearrange("p c r -> p (c r)").bitcast(I32)
 
-        def weave(copy, dst, src):
-            copy(
-                out=dst.rearrange("p (n i t) -> p n t i", i=4, t=PACK),
-                in_=src.rearrange("p t (n i) -> p n t i", i=4),
-            )
+        def fetch_far1(gather, half, t):
+            gather(far1(half, t), h[t][:].indirect(entries("q1", half * HALF, HALF)))
 
-        def fetch_far2(span, t):
+        def fetch_far2(gather, span, t):
             first, count = spans[span]
-            fetch_h(far2[span][:, t, :], t, "q2", first, count)
+            gather(far2[span][:, t, :], h[t][:].indirect(entries("q2", first, count)))
+
+        def max_with_own(half, t):
+            nc.vector.tensor_tensor(high[half][:, t, :], far1(half, t), h[t][:, half * HALF : (half + 1) * HALF], MAX)
+
+        def woven(dst, run):
+            return dst.rearrange("p (n i t) -> p n t i", i=run, t=PACK)
+
+        def planar(src, run):
+            return src.rearrange("p t (n i) -> p n t i", i=run)
 
         def make_z(span):
             first, count = spans[span]
             half, lo = divmod(first, HALF)
-            nc.vector.tensor_tensor(z_planar[span][:], far2[span][:], high[half][:, :, lo : lo + count], MAX)
-
-        def weave_z(span, copy):
-            weave(copy, z_woven[span][:], z_planar[span][:])
+            nc.vector.tensor_tensor(
+                woven(z_woven[span][:], 2), planar(far2[span][:], 2), planar(high[half][:, :, lo : lo + count], 2), MAX
+            )
 
         def quantise_z(span):
             nc.vector.quantize_mx(out=z_codes[span][:].bitcast(FP8X4), scales=z_scales[span][:], in_=z_woven[span][:])
 
-        def product(out, t, span, lo, count):
-            nc.tensor.matmul_mx(
-                out=out,
-                lhsT=w2_dealt[:, 2 * P * t : 2 * P * (t + 1)].bitcast(FP4X4),
-                lhsT_scale=w2_scale_dealt[:, P * t : P * (t + 1)],
-                rhs=z_codes[span][:, lo : lo + count].bitcast(FP8X4),
-                rhs_scale=z_scales[span][:, lo : lo + count],
-                start=True,
-                stop=True,
-            )
-
-        def chunk_product(span, lo):
-            n = (spans[span][0] + lo) // CHUNK
-            acc = bank_tile([P, PACK, CHUNK], "out_chunk_ps%d" % n, n)
+        def chunk_product(span, lo, bank):
+            acc = bank_tile([P, PACK, CHUNK], "out_ps%d_%d_%d" % (span, lo, bank), bank)
             for t in range(PACK):
-                product(acc[:, t, :], t, span, lo, CHUNK)
+                nc.tensor.matmul_mx(
+                    out=acc[:, t, :],
+                    lhsT=w2_dealt[:, 2 * P * t : 2 * P * (t + 1)].bitcast(FP4X4),
+                    lhsT_scale=w2_scale_dealt[:, P * t : P * (t + 1)],
+                    rhs=z_codes[span][:, lo : lo + CHUNK].bitcast(FP8X4),
+                    rhs_scale=z_scales[span][:, lo : lo + CHUNK],
+                    start=True,
+                    stop=True,
+                )
             return acc
 
         def round_chunk(copy, span, lo, acc):
-            weave(copy, out_woven[span][:, PACK * lo : PACK * (lo + CHUNK)], acc[:])
+            copy(out=woven(out_woven[span][:, PACK * lo : PACK * (lo + CHUNK)], 4), in_=planar(acc[:], 4))
 
-        def store_pair(span, pair, bank, queue):
+        def copy_chunk(span, lo, acc):
+            nc.scalar.copy(out=out_f32[span][:, :, lo : lo + CHUNK], in_=acc[:])
+
+        def store_rows(span, queue):
             first, count = spans[span]
-            quarters = slice(2 * pair, 2 * pair + 2)
-            acc = bank_tile([P, 2, count], "out_pair_ps%d_%d" % (span, pair), bank)
-            for t in range(2):
-                product(acc[:, t, :], 2 * pair + t, span, 0, count)
-            nc.scalar.copy(out=out_f32[span][:, quarters], in_=acc[:])
-            queue.dma_start(out=out_rows[:, quarters, first : first + count], in_=out_f32[span][:, quarters])
-
-        def first_span_out():
-            quantise_z(FIRST)
-            for pair in range(2):
-                round_chunk(nc.scalar.copy, FIRST, pair * CHUNK, chunk_product(FIRST, pair * CHUNK))
-                store_pair(FIRST, pair, h_bank(pair), nc.sync)
-
-        def middle_span_out():
-            first, count = spans[MIDDLE]
-            quantise_z(MIDDLE)
-            acc = chunk_product(MIDDLE, 0)
-            nc.scalar.copy(out=out_f32[MIDDLE][:], in_=acc[:])
-            nc.sync.dma_start(out=out_rows[:, :, first : first + count], in_=out_f32[MIDDLE][:])
-            round_chunk(nc.scalar.copy, MIDDLE, 0, acc)
-
-        def last_span_out():
-            quantise_z(LAST)
-            round_chunk(nc.vector.tensor_copy, LAST, 0, chunk_product(LAST, 0))
-            for pair in range(2):
-                store_pair(LAST, pair, S // CHUNK + pair, nc.scalar)
+            queue.dma_start(out=out_rows[:, :, first : first + count], in_=out_f32[span][:])
 
         def planes(span):
             first, count = spans[span]
@@ -412,37 +270,73 @@ def tile_picked_opening_relu_po_kernel(
             if lo + count == HALF:
                 nc.sync.dma_start(out=out_words[:, half * HALF : (half + 1) * HALF], in_=out_codes[half][:].bitcast(I32))
 
-        fetch_far2(FIRST, 0)
-        fetch_far1(0, 1)
-        fetch_far1(1, 0)
-        fetch_far2(FIRST, 1)
-        fetch_far1(1, 1)
-        fetch_far1(2, 0)
-        fetch_far2(FIRST, 2)
-        fetch_far1(3, 0)
-        fetch_far2(FIRST, 3)
-        make_high(0, slice(0, PACK))
-        make_high(1, slice(0, 2))
+        V, A = gather_vector, gather_scalar
+        nc.scalar.activation(y[0][:, 0:HALF], y_ps[0][:], RELU)
+        nc.vector.tensor_scalar_max(y[0][:, HALF:S], y_ps[1][:], 0.0)
+        empty_y(1)
+        fetch_near(V, "p1", 0)
+        fetch_near(A, "p2", 0)
+        fetch_near(V, "p1", 1)
+        empty_y(2)
+        fetch_near(A, "p2", 1)
+        min_with_own("p1", 0)
+        min_with_own("p1", 1)
+        make_h(0)
+        empty_y(3)
+        fetch_near(A, "p2", 2)
+        make_h(1)
+        fetch_near(V, "p1", 2)
+        fetch_near(A, "p2", 3)
+        min_with_own("p2", 2)
+        fetch_near(A, "p1", 3)
+        fetch_far1(V, 0, 0)
+        make_h(2)
+        min_with_own("p2", 3)
+        fetch_far1(A, 0, 1)
+        fetch_far2(V, FIRST, 0)
+        fetch_far2(A, FIRST, 1)
+        make_h(3)
+        fetch_far1(A, 0, 2)
+        fetch_far2(A, FIRST, 2)
+        max_with_own(0, 0)
+        fetch_far1(V, 0, 3)
+        fetch_far2(A, FIRST, 3)
+        for t in range(1, PACK):
+            max_with_own(0, t)
+        fetch_far2(V, MIDDLE, 0)
         make_z(FIRST)
-        weave_z(FIRST, nc.scalar.copy)
-        fetch_far1(2, 1)
-        fetch_far1(3, 1)
-        first_span_out()
-        make_high(1, slice(2, 4))
         for t in range(PACK):
-            fetch_far2(MIDDLE, t)
-        fetch_far2(LAST, 0)
+            fetch_far1(A, 1, t)
+        fetch_far2(V, MIDDLE, 1)
+        quantise_z(FIRST)
+        first_acc = [chunk_product(FIRST, lo, lo // CHUNK) for lo in (0, CHUNK)]
+        for t in range(2, PACK):
+            fetch_far2(V, MIDDLE, t)
+        fetch_far2(A, LAST, 0)
+        fetch_far2(A, LAST, 1)
+        for n in range(2):
+            round_chunk(nc.scalar.copy, FIRST, n * CHUNK, first_acc[n])
+        for t in range(PACK):
+            max_with_own(1, t)
+        fetch_far2(A, LAST, 2)
+        fetch_far2(A, LAST, 3)
         make_z(MIDDLE)
-        fetch_far2(LAST, 1)
-        weave_z(MIDDLE, nc.vector.tensor_copy)
-        fetch_far2(LAST, 2)
-        middle_span_out()
-        fetch_far2(LAST, 3)
         planes(FIRST)
+        quantise_z(MIDDLE)
+        middle_acc = chunk_product(MIDDLE, 0, 2)
+        for n in range(2):
+            copy_chunk(FIRST, n * CHUNK, first_acc[n])
+        store_rows(FIRST, nc.sync)
         make_z(LAST)
-        weave_z(LAST, nc.vector.tensor_copy)
+        quantise_z(LAST)
+        round_chunk(nc.scalar.copy, MIDDLE, 0, middle_acc)
+        copy_chunk(MIDDLE, 0, middle_acc)
+        store_rows(MIDDLE, nc.sync)
+        last_acc = [chunk_product(LAST, 0, bank) for bank in (3, 4)]
         planes(MIDDLE)
-        last_span_out()
+        round_chunk(nc.vector.tensor_copy, LAST, 0, last_acc[0])
+        copy_chunk(LAST, 0, last_acc[1])
+        store_rows(LAST, nc.scalar)
         planes(LAST)
         for quad in range(QUADS):
             queue = nc.scalar if quad % 2 else nc.sync

@@ -170,6 +170,8 @@ def tile_picked_opening_relu_po_kernel(
         near = {(name, t): tile([P, S], F32, "near_%s_%d" % (name, t)) for name in ("p1", "p2") for t in range(PACK)}
         h = [tile([P, S], F32, "h%d" % t) for t in range(PACK)]
 
+        h_all = tile([P, PACK, S], F32, "h_all")
+
         def gather_vector(dst, window):
             nc.vector.tensor_copy(dst, window)
 
@@ -187,18 +189,15 @@ def tile_picked_opening_relu_po_kernel(
 
         def make_h(t):
             nc.vector.tensor_tensor(h[t][:], near["p1", t][:], near["p2", t][:], MIN)
+            nc.sync.dma_start(out=h_all[:, t, :], in_=h[t][:])
 
         spans = [(0, HALF), (HALF, CHUNK), (HALF + CHUNK, CHUNK)]
         FIRST, MIDDLE, LAST = range(len(spans))
-        far1_first = [tile([P, HALF], F32, "far1_first%d" % t) for t in range(PACK)]
-        far1_second = tile([P, PACK, HALF], F32, "far1_second", tag="near_p1_3")
-        high = [tile([P, PACK, HALF], F32, "high_first"), far1_second]
-        far2_tags = [None, "far1_first2", "near_p2_3"]
-        far2 = [tile([P, PACK, count], F32, "far2_%d" % first, tag=far2_tags[i]) for i, (first, count) in enumerate(spans)]
-
-        def far1(half, t):
-            return far1_second[:, t, :] if half else far1_first[t][:]
-
+        far1 = [tile([P, PACK, HALF], BF16, "far1_first"), tile([P, PACK, HALF], BF16, "far1_second", tag="near_p1_3")]
+        far2_tags = [None, "near_p2_2", "near_p2_3"]
+        far2 = [tile([P, PACK, count], BF16, "far2_%d" % first, tag=far2_tags[i]) for i, (first, count) in enumerate(spans)]
+        high_tags = ["high_first", "high_first", None]
+        high = [tile([P, PACK, count], BF16, "high%d" % first, tag=high_tags[i]) for i, (first, count) in enumerate(spans)]
         z_woven = [tile([P, PACK * count], BF16, "z_woven%d" % first) for first, count in spans]
         out_woven = [tile([P, PACK * count], BF16, "out_woven%d" % first) for first, count in spans]
         z_codes = [tile([P, count], U32, "z_codes%d" % first) for first, count in spans]
@@ -210,14 +209,23 @@ def tile_picked_opening_relu_po_kernel(
         out_words = out_1[0].rearrange("p c r -> p (c r)").bitcast(I32)
 
         def fetch_far1(gather, half, t):
-            gather(far1(half, t), h[t][:].indirect(entries("q1", half * HALF, HALF)))
+            gather(far1[half][:, t, :], h[t][:].indirect(entries("q1", half * HALF, HALF)))
 
         def fetch_far2(gather, span, t):
             first, count = spans[span]
             gather(far2[span][:, t, :], h[t][:].indirect(entries("q2", first, count)))
 
-        def max_with_own(half, t):
-            nc.vector.tensor_tensor(high[half][:, t, :], far1(half, t), h[t][:, half * HALF : (half + 1) * HALF], MAX)
+        def far1_span(span):
+            first, count = spans[span]
+            half, lo = divmod(first, HALF)
+            return far1[half][:, :, lo : lo + count]
+
+        def own_span(span):
+            first, count = spans[span]
+            return h_all[:, :, first : first + count]
+
+        def make_high(span, other):
+            nc.vector.tensor_tensor(high[span][:], far1_span(span), other, MAX)
 
         def woven(dst, run):
             return dst.rearrange("p (n i t) -> p n t i", i=run, t=PACK)
@@ -225,12 +233,8 @@ def tile_picked_opening_relu_po_kernel(
         def planar(src, run):
             return src.rearrange("p t (n i) -> p n t i", i=run)
 
-        def make_z(span):
-            first, count = spans[span]
-            half, lo = divmod(first, HALF)
-            nc.vector.tensor_tensor(
-                woven(z_woven[span][:], 2), planar(far2[span][:], 2), planar(high[half][:, :, lo : lo + count], 2), MAX
-            )
+        def make_z(span, other):
+            nc.vector.tensor_tensor(woven(z_woven[span][:], 4), planar(high[span][:], 4), planar(other, 4), MAX)
 
         def quantise_z(span):
             nc.vector.quantize_mx(out=z_codes[span][:].bitcast(FP8X4), scales=z_scales[span][:], in_=z_woven[span][:])
@@ -249,8 +253,8 @@ def tile_picked_opening_relu_po_kernel(
                 )
             return acc
 
-        def round_chunk(copy, span, lo, acc):
-            copy(out=woven(out_woven[span][:, PACK * lo : PACK * (lo + CHUNK)], 4), in_=planar(acc[:], 4))
+        def round_span(copy, span, src):
+            copy(out=woven(out_woven[span][:], 4), in_=planar(src[:], 4))
 
         def copy_chunk(span, lo, acc):
             nc.scalar.copy(out=out_f32[span][:, :, lo : lo + CHUNK], in_=acc[:])
@@ -289,54 +293,47 @@ def tile_picked_opening_relu_po_kernel(
         fetch_near(A, "p2", 3)
         min_with_own("p2", 2)
         fetch_near(A, "p1", 3)
-        fetch_far1(V, 0, 0)
-        make_h(2)
         min_with_own("p2", 3)
-        fetch_far1(A, 0, 1)
-        fetch_far2(V, FIRST, 0)
-        fetch_far2(A, FIRST, 1)
+        make_h(2)
         make_h(3)
-        fetch_far1(A, 0, 2)
-        fetch_far2(A, FIRST, 2)
-        max_with_own(0, 0)
-        fetch_far1(V, 0, 3)
-        fetch_far2(A, FIRST, 3)
-        for t in range(1, PACK):
-            max_with_own(0, t)
-        fetch_far2(V, MIDDLE, 0)
-        make_z(FIRST)
+        for t in range(2):
+            fetch_far1(A, 0, t)
+            fetch_far2(A, FIRST, t)
+        for t in range(2, PACK):
+            fetch_far1(V, 0, t)
+            fetch_far2(V, FIRST, t)
         for t in range(PACK):
             fetch_far1(A, 1, t)
-        fetch_far2(V, MIDDLE, 1)
+        make_high(FIRST, far2[FIRST][:])
+        fetch_far2(V, MIDDLE, 3)
+        make_z(FIRST, own_span(FIRST))
+        fetch_far2(V, MIDDLE, 2)
         quantise_z(FIRST)
         first_acc = [chunk_product(FIRST, lo, lo // CHUNK) for lo in (0, CHUNK)]
-        for t in range(2, PACK):
-            fetch_far2(V, MIDDLE, t)
-        fetch_far2(A, LAST, 0)
-        fetch_far2(A, LAST, 1)
-        for n in range(2):
-            round_chunk(nc.scalar.copy, FIRST, n * CHUNK, first_acc[n])
+        fetch_far2(A, MIDDLE, 0)
+        fetch_far2(A, MIDDLE, 1)
         for t in range(PACK):
-            max_with_own(1, t)
-        fetch_far2(A, LAST, 2)
-        fetch_far2(A, LAST, 3)
-        make_z(MIDDLE)
-        planes(FIRST)
-        quantise_z(MIDDLE)
-        middle_acc = chunk_product(MIDDLE, 0, 2)
+            fetch_far2(A, LAST, t)
+        make_high(MIDDLE, far2[MIDDLE][:])
+        make_high(LAST, own_span(LAST))
+        make_z(MIDDLE, own_span(MIDDLE))
         for n in range(2):
             copy_chunk(FIRST, n * CHUNK, first_acc[n])
         store_rows(FIRST, nc.sync)
-        make_z(LAST)
+        make_z(LAST, far2[LAST][:])
+        quantise_z(MIDDLE)
+        middle_acc = chunk_product(MIDDLE, 0, 2)
         quantise_z(LAST)
-        round_chunk(nc.scalar.copy, MIDDLE, 0, middle_acc)
+        last_acc = [chunk_product(LAST, 0, bank) for bank in (3, 4)]
+        round_span(nc.vector.tensor_copy, FIRST, out_f32[FIRST])
+        round_span(nc.scalar.copy, MIDDLE, middle_acc)
         copy_chunk(MIDDLE, 0, middle_acc)
         store_rows(MIDDLE, nc.sync)
-        last_acc = [chunk_product(LAST, 0, bank) for bank in (3, 4)]
-        planes(MIDDLE)
-        round_chunk(nc.vector.tensor_copy, LAST, 0, last_acc[0])
+        planes(FIRST)
+        round_span(nc.vector.tensor_copy, LAST, last_acc[0])
         copy_chunk(LAST, 0, last_acc[1])
         store_rows(LAST, nc.scalar)
+        planes(MIDDLE)
         planes(LAST)
         for quad in range(QUADS):
             queue = nc.scalar if quad % 2 else nc.sync

@@ -324,15 +324,15 @@ def tile_picked_opening_relu_po_kernel(
         quantise_z(MIDDLE)
         middle_acc = chunk_product(MIDDLE, 0, 2)
         quantise_z(LAST)
-        last_acc = [chunk_product(LAST, 0, bank) for bank in (3, 4)]
+        last_acc = chunk_product(LAST, 0, 3)
         round_span(nc.vector.tensor_copy, FIRST, out_f32[FIRST])
-        round_span(nc.scalar.copy, MIDDLE, middle_acc)
         copy_chunk(MIDDLE, 0, middle_acc)
         store_rows(MIDDLE, nc.sync)
         planes(FIRST)
-        round_span(nc.vector.tensor_copy, LAST, last_acc[0])
-        copy_chunk(LAST, 0, last_acc[1])
+        round_span(nc.scalar.copy, LAST, last_acc)
+        copy_chunk(LAST, 0, last_acc)
         store_rows(LAST, nc.scalar)
+        round_span(nc.vector.tensor_copy, MIDDLE, out_f32[MIDDLE])
         planes(MIDDLE)
         planes(LAST)
         for quad in range(QUADS):

@@ -194,9 +194,9 @@ def tile_picked_opening_relu_po_kernel(
         spans = [(0, HALF), (HALF, CHUNK), (HALF + CHUNK, CHUNK)]
         FIRST, MIDDLE, LAST = range(len(spans))
         far1 = [tile([P, PACK, HALF], BF16, "far1_first"), tile([P, PACK, HALF], BF16, "far1_second", tag="near_p1_3")]
-        far2_tags = [None, "near_p2_2", "near_p2_3"]
+        far2_tags = [None, "near_p2_3", "near_p2_2"]
         far2 = [tile([P, PACK, count], BF16, "far2_%d" % first, tag=far2_tags[i]) for i, (first, count) in enumerate(spans)]
-        high_tags = ["high_first", "high_first", None]
+        high_tags = ["high_first", None, "high_first"]
         high = [tile([P, PACK, count], BF16, "high%d" % first, tag=high_tags[i]) for i, (first, count) in enumerate(spans)]
         z_woven = [tile([P, PACK * count], BF16, "z_woven%d" % first) for first, count in spans]
         out_woven = [tile([P, PACK * count], BF16, "out_woven%d" % first) for first, count in spans]
@@ -233,11 +233,22 @@ def tile_picked_opening_relu_po_kernel(
         def planar(src, run):
             return src.rearrange("p t (n i) -> p n t i", i=run)
 
-        def make_z(span, other):
-            nc.vector.tensor_tensor(woven(z_woven[span][:], 4), planar(high[span][:], 4), planar(other, 4), MAX)
+        def make_z(span, other, lo=0):
+            cols = slice(lo, lo + CHUNK)
+            nc.vector.tensor_tensor(
+                woven(z_woven[span][:, PACK * lo : PACK * (lo + CHUNK)], 4),
+                planar(high[span][:, :, cols], 4),
+                planar(other[:, :, cols], 4),
+                MAX,
+            )
 
-        def quantise_z(span):
-            nc.vector.quantize_mx(out=z_codes[span][:].bitcast(FP8X4), scales=z_scales[span][:], in_=z_woven[span][:])
+        def quantise_z(span, lo=0):
+            cols = slice(lo, lo + CHUNK)
+            nc.vector.quantize_mx(
+                out=z_codes[span][:, cols].bitcast(FP8X4),
+                scales=z_scales[span][:, cols],
+                in_=z_woven[span][:, PACK * lo : PACK * (lo + CHUNK)],
+            )
 
         def chunk_product(span, lo, bank):
             acc = bank_tile([P, PACK, CHUNK], "out_ps%d_%d_%d" % (span, lo, bank), bank)
@@ -253,8 +264,8 @@ def tile_picked_opening_relu_po_kernel(
                 )
             return acc
 
-        def round_span(copy, span, src):
-            copy(out=woven(out_woven[span][:], 4), in_=planar(src[:], 4))
+        def round_chunk(copy, span, lo, src):
+            copy(out=woven(out_woven[span][:, PACK * lo : PACK * (lo + CHUNK)], 4), in_=planar(src, 4))
 
         def copy_chunk(span, lo, acc):
             nc.scalar.copy(out=out_f32[span][:, :, lo : lo + CHUNK], in_=acc[:])
@@ -305,34 +316,38 @@ def tile_picked_opening_relu_po_kernel(
         for t in range(PACK):
             fetch_far1(A, 1, t)
         make_high(FIRST, far2[FIRST][:])
-        fetch_far2(V, MIDDLE, 3)
-        make_z(FIRST, own_span(FIRST))
-        fetch_far2(V, MIDDLE, 2)
-        quantise_z(FIRST)
+        fetch_far2(V, LAST, 3)
+        for lo in (0, CHUNK):
+            make_z(FIRST, own_span(FIRST), lo)
+        for lo in (0, CHUNK):
+            quantise_z(FIRST, lo)
+        fetch_far2(V, LAST, 2)
         first_acc = [chunk_product(FIRST, lo, lo // CHUNK) for lo in (0, CHUNK)]
-        fetch_far2(A, MIDDLE, 0)
-        fetch_far2(A, MIDDLE, 1)
+        again_acc = chunk_product(FIRST, CHUNK, 4)
+        fetch_far2(A, LAST, 0)
+        fetch_far2(A, LAST, 1)
         for t in range(PACK):
-            fetch_far2(A, LAST, t)
-        make_high(MIDDLE, far2[MIDDLE][:])
-        make_high(LAST, own_span(LAST))
-        make_z(MIDDLE, own_span(MIDDLE))
+            fetch_far2(A, MIDDLE, t)
+        make_high(MIDDLE, own_span(MIDDLE))
+        make_high(LAST, far2[LAST][:])
+        make_z(MIDDLE, far2[MIDDLE][:])
         for n in range(2):
             copy_chunk(FIRST, n * CHUNK, first_acc[n])
         store_rows(FIRST, nc.sync)
-        make_z(LAST, far2[LAST][:])
+        round_chunk(nc.scalar.copy, FIRST, CHUNK, again_acc[:])
+        make_z(LAST, own_span(LAST))
         quantise_z(MIDDLE)
         middle_acc = chunk_product(MIDDLE, 0, 2)
         quantise_z(LAST)
         last_acc = chunk_product(LAST, 0, 3)
-        round_span(nc.vector.tensor_copy, FIRST, out_f32[FIRST])
+        round_chunk(nc.vector.tensor_copy, FIRST, 0, out_f32[FIRST][:, :, 0:CHUNK])
         copy_chunk(MIDDLE, 0, middle_acc)
         store_rows(MIDDLE, nc.sync)
         planes(FIRST)
-        round_span(nc.scalar.copy, LAST, last_acc)
+        round_chunk(nc.scalar.copy, LAST, 0, last_acc[:])
         copy_chunk(LAST, 0, last_acc)
         store_rows(LAST, nc.scalar)
-        round_span(nc.vector.tensor_copy, MIDDLE, out_f32[MIDDLE])
+        round_chunk(nc.vector.tensor_copy, MIDDLE, 0, out_f32[MIDDLE][:])
         planes(MIDDLE)
         planes(LAST)
         for quad in range(QUADS):

@@ -44,7 +44,7 @@ def tile_picked_opening_relu_po_kernel(
         w1_late = [tile([P, 2, H], F32, "w1_late%d" % pair) for pair in range(2)]
         x_table = [tile([P, T], I32, "x_table%d" % g) for g in range(PASSES)]
         x_scale_table = tile([P, T], U8, "x_scale_table")
-        w2_raw = tile([P, 2 * N], U8, "w2_raw")
+        w2_raw = tile([P, 2 * N], U8, "w2_raw", tag="near_p2_0")
         w2_scale_raw = tile([P, N], U8, "w2_scale_raw")
         lists = {}
         for name in ("offs", "p1", "p2", "q1", "q2"):
@@ -59,15 +59,14 @@ def tile_picked_opening_relu_po_kernel(
         def load_x(g):
             nc.sync.dma_start(out=x_table[g][:], in_=x_words[g].rearrange("p c r -> p (c r)").bitcast(I32))
 
-        nc.sync.dma_start(out=lists["offs"][:], in_=offs)
         nc.sync.dma_start(out=w1_early[:], in_=w1_rows(0))
+        nc.sync.dma_start(out=lists["offs"][:], in_=offs)
         for quad in range(QUADS):
             nc.sync.dma_start(
                 out=x_scale_table[32 * quad : 32 * quad + 4 * PASSES, :].bitcast(I32),
                 in_=x_scales[:, 4 * quad : 4 * quad + 4, :].bitcast(I32),
             )
         load_x(1)
-        nc.sync.dma_start(out=w2_raw[:].bitcast(I32), in_=w2_words[0].bitcast(I32))
         for quad in range(QUADS):
             nc.sync.dma_start(
                 out=w2_scale_raw[32 * quad : 32 * quad + 4, :].bitcast(I32),
@@ -76,6 +75,7 @@ def tile_picked_opening_relu_po_kernel(
         load_x(0)
         for pair in range(2):
             nc.sync.dma_start(out=w1_late[pair][:], in_=w1_rows(1)[:, 2 * pair : 2 * pair + 2, :])
+        nc.sync.dma_start(out=w2_raw[:].bitcast(I32), in_=w2_words[0].bitcast(I32))
         nc.sync.dma_start(out=lists["p1"][:], in_=p1)
         nc.sync.dma_start(out=lists["p2"][:], in_=p2)
         nc.sync.dma_start(out=lists["q1"][:], in_=q1)
@@ -91,10 +91,10 @@ def tile_picked_opening_relu_po_kernel(
             nc.scalar.copy(out=dst[:, 0 : P // 2], in_=src[:, 0 : P // 2])
             nc.vector.tensor_copy(out=dst[:, P // 2 : P], in_=src[:, P // 2 : P])
 
-        def round_late(copy, pair, first, count):
+        def round_late(copy, pair, first, count, m=slice(0, P)):
             dst = w1_bf[1][:].rearrange("p (t m j) -> p m t j", t=PACK, j=PACK)
             src = w1_late[pair][:].rearrange("p j (m t) -> p m t j", t=PACK)
-            copy(out=dst[:, :, first : first + count, 2 * pair : 2 * pair + 2], in_=src[:, :, first : first + count, :])
+            copy(out=dst[:, m, first : first + count, 2 * pair : 2 * pair + 2], in_=src[:, m, first : first + count, :])
 
         def quantise_w1(g, first, count):
             cols = slice(P * first, P * (first + count))
@@ -122,19 +122,20 @@ def tile_picked_opening_relu_po_kernel(
         w2_dealt = tile([P, 2 * N], U8, "w2_dealt")
         w2_scale_dealt = tile([P, N], U8, "w2_scale_dealt")
         nc.vector.tensor_copy(
-            out=w2_dealt[:].rearrange("p (t m b) -> p m t b", t=PACK, b=2),
-            in_=w2_raw[:].rearrange("p (m t b) -> p m t b", t=PACK, b=2),
-        )
-        nc.vector.tensor_copy(
             out=w2_scale_dealt[:].rearrange("p (t m) -> p m t", t=PACK),
             in_=w2_scale_raw[:].rearrange("p (m t) -> p m t", t=PACK),
         )
         gather_words(0, 0, S)
         round_late(nc.scalar.copy, 0, 2, 2)
         round_late(nc.vector.tensor_copy, 0, 0, 2)
+        round_late(nc.scalar.copy, 1, 0, 1, slice(P // 2, P))
+        round_late(nc.vector.tensor_copy, 1, 0, 1, slice(0, P // 2))
         round_late(nc.scalar.copy, 1, 2, 2)
-        round_late(nc.vector.tensor_copy, 1, 0, 1)
         round_late(nc.vector.tensor_copy, 1, 1, 1)
+        nc.scalar.copy(
+            out=w2_dealt[:].bitcast(U16).rearrange("p (t m) -> p t m", t=PACK),
+            in_=w2_raw[:].bitcast(U16).rearrange("p (m t) -> p t m", t=PACK),
+        )
         quantise_w1(1, 0, 1)
         quantise_w1(1, 1, 1)
         quantise_w1(1, 2, 2)

@@ -60,24 +60,30 @@ def tile_picked_opening_relu_po_kernel(
             nc.sync.dma_start(out=x_table[g][:], in_=x_words[g].rearrange("p c r -> p (c r)").bitcast(I32))
 
         nc.sync.dma_start(out=w1_early[:], in_=w1_rows(0))
+        def load_x_scales(i):
+            for g in range(PASSES):
+                nc.sync.dma_start(
+                    out=x_scale_table[4 * g + i : P : 32, :].bitcast(I32),
+                    in_=x_scales[g, i : 4 * QUADS : 4, :].bitcast(I32),
+                )
+
+        load_x_scales(0)
+        load_x_scales(1)
         nc.sync.dma_start(out=lists["offs"][:], in_=offs)
-        for quad in range(QUADS):
-            nc.sync.dma_start(
-                out=x_scale_table[32 * quad : 32 * quad + 4 * PASSES, :].bitcast(I32),
-                in_=x_scales[:, 4 * quad : 4 * quad + 4, :].bitcast(I32),
-            )
         load_x(1)
-        for quad in range(QUADS):
-            nc.sync.dma_start(
-                out=w2_scale_raw[32 * quad : 32 * quad + 4, :].bitcast(I32),
-                in_=w2_scales[0, 4 * quad : 4 * quad + 4, :].bitcast(I32),
-            )
+        load_x_scales(2)
+        load_x_scales(3)
         load_x(0)
         for pair in range(2):
             nc.sync.dma_start(out=w1_late[pair][:], in_=w1_rows(1)[:, 2 * pair : 2 * pair + 2, :])
         nc.sync.dma_start(out=w2_raw[:].bitcast(I32), in_=w2_words[0].bitcast(I32))
         nc.sync.dma_start(out=lists["p1"][:], in_=p1)
         nc.sync.dma_start(out=lists["p2"][:], in_=p2)
+        for quad in range(QUADS):
+            nc.sync.dma_start(
+                out=w2_scale_raw[32 * quad : 32 * quad + 4, :].bitcast(I32),
+                in_=w2_scales[0, 4 * quad : 4 * quad + 4, :].bitcast(I32),
+            )
         nc.sync.dma_start(out=lists["q1"][:], in_=q1)
         nc.sync.dma_start(out=lists["q2"][:], in_=q2)
 
@@ -116,15 +122,11 @@ def tile_picked_opening_relu_po_kernel(
             )
 
         round_early()
-        nc.vector.tensor_copy(x_picked_scales[:], x_scale_table[:].indirect(lists["offs"][:]))
         quantise_w1(0, 0, PACK)
         gather_words(1, 0, S)
+        nc.vector.tensor_copy(x_picked_scales[:], x_scale_table[:].indirect(lists["offs"][:]))
         w2_dealt = tile([P, 2 * N], U8, "w2_dealt")
         w2_scale_dealt = tile([P, N], U8, "w2_scale_dealt")
-        nc.vector.tensor_copy(
-            out=w2_scale_dealt[:].rearrange("p (t m) -> p m t", t=PACK),
-            in_=w2_scale_raw[:].rearrange("p (m t) -> p m t", t=PACK),
-        )
         gather_words(0, 0, S)
         round_late(nc.scalar.copy, 0, 2, 2)
         round_late(nc.vector.tensor_copy, 0, 0, 2)
@@ -139,6 +141,10 @@ def tile_picked_opening_relu_po_kernel(
         quantise_w1(1, 0, 1)
         quantise_w1(1, 1, 1)
         quantise_w1(1, 2, 2)
+        nc.vector.tensor_copy(
+            out=w2_scale_dealt[:].rearrange("p (t m) -> p m t", t=PACK),
+            in_=w2_scale_raw[:].rearrange("p (m t) -> p m t", t=PACK),
+        )
 
         pieces = [(0, 0, HALF), (0, HALF, HALF)] + [(t, 0, S) for t in range(1, PACK)]
         y_ps = [bank_tile([P, count], "y_ps%d" % i, i + 1) for i, (t, first, count) in enumerate(pieces)]
@@ -318,6 +324,7 @@ def tile_picked_opening_relu_po_kernel(
             fetch_far1(A, 1, t)
         make_high(FIRST, far2[FIRST][:])
         fetch_far2(V, LAST, 3)
+        fetch_far2(V, LAST, 1)
         for lo in (0, CHUNK):
             make_z(FIRST, own_span(FIRST), lo)
         for lo in (0, CHUNK):
@@ -326,7 +333,6 @@ def tile_picked_opening_relu_po_kernel(
         first_acc = [chunk_product(FIRST, lo, lo // CHUNK) for lo in (0, CHUNK)]
         again_acc = chunk_product(FIRST, CHUNK, 4)
         fetch_far2(A, LAST, 0)
-        fetch_far2(A, LAST, 1)
         for t in range(PACK):
             fetch_far2(A, MIDDLE, t)
         make_high(MIDDLE, own_span(MIDDLE))

@@ -56,8 +56,9 @@ def tile_picked_opening_relu_po_kernel(
         def w1_rows(g):
             return w1[P * PACK * g : P * PACK * (g + 1), :].rearrange("(p j) c -> p j c", j=PACK)
 
-        def load_x(g):
-            nc.sync.dma_start(out=x_table[g][:], in_=x_words[g].rearrange("p c r -> p (c r)").bitcast(I32))
+        def load_x(g, first=0, count=T):
+            cols = slice(first, first + count)
+            nc.sync.dma_start(out=x_table[g][:, cols], in_=x_words[g].rearrange("p c r -> p (c r)").bitcast(I32)[:, cols])
 
         nc.sync.dma_start(out=w1_early[:], in_=w1_rows(0))
         def load_x_scales(i):
@@ -71,9 +72,10 @@ def tile_picked_opening_relu_po_kernel(
         load_x_scales(1)
         nc.sync.dma_start(out=lists["offs"][:], in_=offs)
         load_x(1)
+        load_x(0, 0, T // 2)
         load_x_scales(2)
         load_x_scales(3)
-        load_x(0)
+        load_x(0, T // 2, T // 2)
         for pair in range(2):
             nc.sync.dma_start(out=w1_late[pair][:], in_=w1_rows(1)[:, 2 * pair : 2 * pair + 2, :])
         nc.sync.dma_start(out=w2_raw[:].bitcast(I32), in_=w2_words[0].bitcast(I32))

@@ -212,7 +212,7 @@ def tile_picked_opening_relu_po_kernel(
         z_codes = [tile([P, count], U32, "z_codes%d" % first) for first, count in spans]
         z_scales = [tile([P, count], U8, "z_scales%d" % first) for first, count in spans]
         out_f32 = [tile([P, PACK, count], F32, "out_f32_%d" % first) for first, count in spans]
-        out_codes = [tile([P, HALF], U32, "out_codes%d" % half) for half in range(2)]
+        out_codes = tile([P, S], U32, "out_codes")
         out_scales = tile([P, S], U8, "out_scales")
         out_rows = out_0.rearrange("(p t) j -> p t j", t=PACK)
         out_words = out_1[0].rearrange("p c r -> p (c r)").bitcast(I32)
@@ -285,14 +285,12 @@ def tile_picked_opening_relu_po_kernel(
 
         def planes(span):
             first, count = spans[span]
-            half, lo = divmod(first, HALF)
-            nc.vector.quantize_mx(
-                out=out_codes[half][:, lo : lo + count].bitcast(FP8X4),
-                scales=out_scales[:, first : first + count],
-                in_=out_woven[span][:],
-            )
-            if lo + count == HALF:
-                nc.sync.dma_start(out=out_words[:, half * HALF : (half + 1) * HALF], in_=out_codes[half][:].bitcast(I32))
+            cols = slice(first, first + count)
+            nc.vector.quantize_mx(out=out_codes[:, cols].bitcast(FP8X4), scales=out_scales[:, cols], in_=out_woven[span][:])
+
+        def store_words(first, count):
+            cols = slice(first, first + count)
+            nc.sync.dma_start(out=out_words[:, cols], in_=out_codes[:, cols].bitcast(I32))
 
         V, A = gather_vector, gather_scalar
         nc.scalar.activation(y[0][:, 0:HALF], y_ps[0][:], RELU)
@@ -353,12 +351,14 @@ def tile_picked_opening_relu_po_kernel(
         copy_chunk(MIDDLE, 0, middle_acc)
         store_rows(MIDDLE, nc.sync)
         planes(FIRST)
-        round_chunk(nc.scalar.copy, LAST, 0, last_acc[:])
         copy_chunk(LAST, 0, last_acc)
-        store_rows(LAST, nc.scalar)
+        store_rows(LAST, nc.sync)
+        round_chunk(nc.scalar.copy, LAST, 0, last_acc[:])
         round_chunk(nc.vector.tensor_copy, MIDDLE, 0, out_f32[MIDDLE][:])
         planes(MIDDLE)
+        store_words(0, spans[LAST][0])
         planes(LAST)
+        store_words(*spans[LAST])
         for quad in range(QUADS):
             queue = nc.scalar if quad % 2 else nc.sync
             queue.dma_start(

@@ -71,11 +71,11 @@ def tile_picked_opening_relu_po_kernel(
         load_x_scales(0)
         load_x_scales(1)
         nc.sync.dma_start(out=lists["offs"][:], in_=offs)
-        load_x(1)
-        load_x(0, 0, T // 2)
+        load_x(0)
+        load_x(1, 0, T // 2)
         load_x_scales(2)
         load_x_scales(3)
-        load_x(0, T // 2, T // 2)
+        load_x(1, T // 2, T // 2)
         for pair in range(2):
             nc.sync.dma_start(out=w1_late[pair][:], in_=w1_rows(1)[:, 2 * pair : 2 * pair + 2, :])
         nc.sync.dma_start(out=w2_raw[:].bitcast(I32), in_=w2_words[0].bitcast(I32))
@@ -125,11 +125,11 @@ def tile_picked_opening_relu_po_kernel(
 
         round_early()
         quantise_w1(0, 0, PACK)
-        gather_words(1, 0, S)
+        gather_words(0, 0, S)
         nc.vector.tensor_copy(x_picked_scales[:], x_scale_table[:].indirect(lists["offs"][:]))
         w2_dealt = tile([P, 2 * N], U8, "w2_dealt")
         w2_scale_dealt = tile([P, N], U8, "w2_scale_dealt")
-        gather_words(0, 0, S)
+        gather_words(1, 0, S)
         round_late(nc.scalar.copy, 0, 2, 2)
         round_late(nc.vector.tensor_copy, 0, 0, 2)
         round_late(nc.scalar.copy, 1, 0, 1, slice(P // 2, P))
@@ -166,11 +166,8 @@ def tile_picked_opening_relu_po_kernel(
             )
 
         for g in range(PASSES):
-            for i in range(y_piece[2]):
+            for i in range(len(pieces)):
                 first_product(i, g, g == 0)
-        for t in range(2, PACK):
-            first_product(y_piece[t], 1, True)
-            first_product(y_piece[t], 0, False)
 
         y_window = [tile([P, 2 * S], F32, "y_window%d" % t) for t in range(PACK)]
         y = [y_window[t][:, 0:S] for t in range(PACK)]

@@ -276,9 +276,9 @@ def tile_picked_opening_relu_po_kernel(
         def copy_chunk(span, lo, acc):
             nc.scalar.copy(out=out_f32[span][:, :, lo : lo + CHUNK], in_=acc[:])
 
-        def store_rows(span, queue):
-            first, count = spans[span]
-            queue.dma_start(out=out_rows[:, :, first : first + count], in_=out_f32[span][:])
+        def store_rows(span, lo):
+            first = spans[span][0] + lo
+            nc.sync.dma_start(out=out_rows[:, :, first : first + CHUNK], in_=out_f32[span][:, :, lo : lo + CHUNK])
 
         def planes(span):
             first, count = spans[span]
@@ -337,7 +337,7 @@ def tile_picked_opening_relu_po_kernel(
         make_z(MIDDLE, far2[MIDDLE][:])
         for n in range(2):
             copy_chunk(FIRST, n * CHUNK, first_acc[n])
-        store_rows(FIRST, nc.sync)
+            store_rows(FIRST, n * CHUNK)
         round_chunk(nc.scalar.copy, FIRST, CHUNK, again_acc[:])
         make_z(LAST, own_span(LAST))
         quantise_z(MIDDLE)
@@ -346,10 +346,10 @@ def tile_picked_opening_relu_po_kernel(
         last_acc = chunk_product(LAST, 0, 3)
         round_chunk(nc.vector.tensor_copy, FIRST, 0, out_f32[FIRST][:, :, 0:CHUNK])
         copy_chunk(MIDDLE, 0, middle_acc)
-        store_rows(MIDDLE, nc.sync)
+        store_rows(MIDDLE, 0)
         planes(FIRST)
         copy_chunk(LAST, 0, last_acc)
-        store_rows(LAST, nc.sync)
+        store_rows(LAST, 0)
         round_chunk(nc.scalar.copy, LAST, 0, last_acc[:])
         round_chunk(nc.vector.tensor_copy, MIDDLE, 0, out_f32[MIDDLE][:])
         planes(MIDDLE)

@@ -44,7 +44,7 @@ def tile_picked_opening_relu_po_kernel(
         w1_late = [tile([P, 2, H], F32, "w1_late%d" % pair) for pair in range(2)]
         x_table = [tile([P, T], I32, "x_table%d" % g) for g in range(PASSES)]
         x_scale_table = tile([P, T], U8, "x_scale_table")
-        w2_raw = tile([P, 2 * N], U8, "w2_raw", tag="near_p2_0")
+        w2_raw = tile([P, 2 * N], U8, "w2_raw")
         w2_scale_raw = tile([P, N], U8, "w2_scale_raw")
         lists = {}
         for name in ("offs", "p1", "p2", "q1", "q2"):
@@ -127,8 +127,10 @@ def tile_picked_opening_relu_po_kernel(
         quantise_w1(0, 0, PACK)
         gather_words(0, 0, S)
         nc.vector.tensor_copy(x_picked_scales[:], x_scale_table[:].indirect(lists["offs"][:]))
-        w2_dealt = tile([P, 2 * N], U8, "w2_dealt")
-        w2_scale_dealt = tile([P, N], U8, "w2_scale_dealt")
+        w2_dealt_first = tile([P, 2 * P], U8, "w2_dealt_first")
+        w2_dealt_rest = tile([P, PACK - 1, 2 * P], U8, "w2_dealt_rest", tag="near_p1_2")
+        w2_dealt = [w2_dealt_first[:]] + [w2_dealt_rest[:, t, :] for t in range(PACK - 1)]
+        w2_scale_dealt = tile([P, N], U8, "w2_scale_dealt", tag="w1_bf1")
         gather_words(1, 0, S)
         round_late(nc.scalar.copy, 0, 2, 2)
         round_late(nc.vector.tensor_copy, 0, 0, 2)
@@ -136,16 +138,13 @@ def tile_picked_opening_relu_po_kernel(
         round_late(nc.vector.tensor_copy, 1, 0, 1, slice(0, P // 2))
         round_late(nc.scalar.copy, 1, 2, 2)
         round_late(nc.vector.tensor_copy, 1, 1, 1)
-        nc.scalar.copy(
-            out=w2_dealt[:].bitcast(U16).rearrange("p (t m) -> p t m", t=PACK),
-            in_=w2_raw[:].bitcast(U16).rearrange("p (m t) -> p t m", t=PACK),
-        )
+        nc.scalar.copy(out=w2_dealt_first[:].bitcast(U16), in_=w2_raw[:].bitcast(U16).rearrange("p (m t) -> p t m", t=PACK)[:, 0])
         quantise_w1(1, 0, 1)
         quantise_w1(1, 1, 1)
         quantise_w1(1, 2, 2)
-        nc.vector.tensor_copy(
-            out=w2_scale_dealt[:].rearrange("p (t m) -> p m t", t=PACK),
-            in_=w2_scale_raw[:].rearrange("p (m t) -> p m t", t=PACK),
+        nc.gpsimd.tensor_copy(
+            out=w2_scale_dealt[:].rearrange("p (t m) -> p t m", t=PACK),
+            in_=w2_scale_raw[:].rearrange("p (m t) -> p t m", t=PACK),
         )
 
         pieces = [(0, 0, HALF), (0, HALF, HALF)] + [(t, 0, S) for t in range(1, PACK)]
@@ -261,7 +260,7 @@ def tile_picked_opening_relu_po_kernel(
             for t in range(PACK):
                 nc.tensor.matmul_mx(
                     out=acc[:, t, :],
-                    lhsT=w2_dealt[:, 2 * P * t : 2 * P * (t + 1)].bitcast(FP4X4),
+                    lhsT=w2_dealt[t].bitcast(FP4X4),
                     lhsT_scale=w2_scale_dealt[:, P * t : P * (t + 1)],
                     rhs=z_codes[span][:, lo : lo + CHUNK].bitcast(FP8X4),
                     rhs_scale=z_scales[span][:, lo : lo + CHUNK],
@@ -311,6 +310,10 @@ def tile_picked_opening_relu_po_kernel(
         min_with_own("p2", 3)
         make_h(2)
         make_h(3)
+        nc.gpsimd.tensor_copy(
+            out=w2_dealt_rest[:].rearrange("p t (m b) -> p t m b", b=2),
+            in_=w2_raw[:].rearrange("p (m t b) -> p t m b", t=PACK, b=2)[:, 1:PACK],
+        )
         for t in range(2):
             fetch_far1(A, 0, t)
             fetch_far2(A, FIRST, t)

from contextlib import ExitStack

import concourse.mybir as mybir

F32 = mybir.dt.float32
BF16 = mybir.dt.bfloat16
I32 = mybir.dt.int32
U32 = mybir.dt.uint32
U16 = mybir.dt.uint16
U8 = mybir.dt.uint8
FP8X4 = mybir.dt.float8_e4m3fn_x4
FP4X4 = mybir.dt.float4_e2m1fn_x4
MAX = mybir.AluOpType.max
MIN = mybir.AluOpType.min
RELU = mybir.ActivationFunctionType.Relu
COPY = mybir.ActivationFunctionType.Copy

K, T, S, H, N = 1024, 2048, 512, 512, 512
FLOPS = 2 * K * H * S + 2 * H * N * S
P = 128
PACK = 4
PASSES = K // (P * PACK)
QUADS = 4
HALF = S // 2
CHUNK = 128
STRIPE = 16


def tile_picked_opening_relu_po_kernel(
    tc, x_words, x_scales, w1, w2_words, w2_scales, offs, p1, p2, q1, q2, out_0, out_1, out_2
):
    nc = tc.nc
    with ExitStack() as ctx:
        sb = ctx.enter_context(tc.tile_pool(name="sb", bufs=1))
        ps = ctx.enter_context(tc.psum_pool(name="ps", bufs=1))

        def tile(shape, dtype, name, tag=None):
            return sb.tile(shape, dtype, name=name, tag=tag or name, align_bytes=64)

        def bank_tile(shape, name, bank):
            return ps.tile(shape, F32, name=name, tag="bank%d" % bank)

        w1_early = tile([P, PACK, H], F32, "w1_early")
        w1_late = [tile([P, 2, H], F32, "w1_late%d" % pair) for pair in range(2)]
        x_table = [tile([P, T], I32, "x_table%d" % g) for g in range(PASSES)]
        x_scale_table = tile([P, T], U8, "x_scale_table")
        w2_raw = tile([P, 2 * N], U8, "w2_raw")
        w2_scale_raw = tile([P, N], U8, "w2_scale_raw")
        lists = {}
        for name in ("offs", "p1", "p2", "q1", "q2"):
            lists[name] = tile([P, S // STRIPE], U16, "list_" + name)

        nc.gpsimd.memset(x_scale_table[:].bitcast(I32), 0)
        nc.vector.memset(w2_scale_raw[:].bitcast(I32), 0)

        def w1_rows(g):
            return w1[P * PACK * g : P * PACK * (g + 1), :].rearrange("(p j) c -> p j c", j=PACK)

        def load_x(g, first=0, count=T):
            cols = slice(first, first + count)
            nc.sync.dma_start(out=x_table[g][:, cols], in_=x_words[g].rearrange("p c r -> p (c r)").bitcast(I32)[:, cols])

        nc.sync.dma_start(out=w1_early[:], in_=w1_rows(0))
        def load_x_scales(i):
            for g in range(PASSES):
                nc.sync.dma_start(
                    out=x_scale_table[4 * g + i : P : 32, :].bitcast(I32),
                    in_=x_scales[g, i : 4 * QUADS : 4, :].bitcast(I32),
                )

        load_x_scales(0)
        load_x_scales(1)
        nc.sync.dma_start(out=lists["offs"][:], in_=offs)
        load_x(0)
        load_x(1, 0, T // 2)
        load_x_scales(2)
        load_x_scales(3)
        load_x(1, T // 2, T // 2)
        for pair in range(2):
            nc.sync.dma_start(out=w1_late[pair][:], in_=w1_rows(1)[:, 2 * pair : 2 * pair + 2, :])
        nc.sync.dma_start(out=w2_raw[:].bitcast(I32), in_=w2_words[0].bitcast(I32))
        nc.sync.dma_start(out=lists["p1"][:], in_=p1)
        nc.sync.dma_start(out=lists["p2"][:], in_=p2)
        for quad in range(QUADS):
            nc.sync.dma_start(
                out=w2_scale_raw[32 * quad : 32 * quad + 4, :].bitcast(I32),
                in_=w2_scales[0, 4 * quad : 4 * quad + 4, :].bitcast(I32),
            )
        nc.sync.dma_start(out=lists["q1"][:], in_=q1)
        nc.sync.dma_start(out=lists["q2"][:], in_=q2)

        w1_bf = [tile([P, PACK * H], BF16, "w1_bf%d" % g) for g in range(PASSES)]
        w1_codes = [tile([P, H], U32, "w1_codes%d" % g) for g in range(PASSES)]
        w1_scales = [tile([P, H], U8, "w1_scales%d" % g) for g in range(PASSES)]

        def round_early():
            dst = w1_bf[0][:].rearrange("p (t m j) -> p m j t", t=PACK, j=PACK)
            src = w1_early[:].rearrange("p j (m t) -> p m j t", t=PACK)
            nc.scalar.copy(out=dst[:, 0 : P // 2], in_=src[:, 0 : P // 2])
            nc.vector.tensor_copy(out=dst[:, P // 2 : P], in_=src[:, P // 2 : P])

        def round_late(copy, pair, first, count, m=slice(0, P)):
            dst = w1_bf[1][:].rearrange("p (t m j) -> p m t j", t=PACK, j=PACK)
            src = w1_late[pair][:].rearrange("p j (m t) -> p m t j", t=PACK)
            copy(out=dst[:, m, first : first + count, 2 * pair : 2 * pair + 2], in_=src[:, m, first : first + count, :])

        def quantise_w1(g, first, count):
            cols = slice(P * first, P * (first + count))
            nc.vector.quantize_mx(
                out=w1_codes[g][:, cols].bitcast(FP8X4),
                scales=w1_scales[g][:, cols],
                in_=w1_bf[g][:, PACK * P * first : PACK * P * (first + count)],
            )

        x_codes = [tile([P, S], U32, "x_codes%d" % g) for g in range(PASSES)]
        x_picked_scales = tile([P, S], U8, "x_picked_scales")

        def entries(name, first, count):
            return lists[name][:, first // STRIPE : (first + count) // STRIPE]

        def gather_words(g, first, count):
            nc.vector.tensor_copy(
                x_codes[g][:, first : first + count], x_table[g][:].bitcast(U32).indirect(entries("offs", first, count))
            )

        round_early()
        quantise_w1(0, 0, PACK)
        gather_words(0, 0, S)
        nc.vector.tensor_copy(x_picked_scales[:], x_scale_table[:].indirect(lists["offs"][:]))
        w2_dealt_first = tile([P, 2 * P], U8, "w2_dealt_first")
        w2_dealt_rest = tile([P, PACK - 1, 2 * P], U8, "w2_dealt_rest", tag="near_p1_2")
        w2_dealt = [w2_dealt_first[:]] + [w2_dealt_rest[:, t, :] for t in range(PACK - 1)]
        w2_scale_dealt = tile([P, N], U8, "w2_scale_dealt", tag="w1_bf1")
        gather_words(1, 0, S)
        round_late(nc.scalar.copy, 0, 2, 2)
        round_late(nc.vector.tensor_copy, 0, 0, 2)
        round_late(nc.scalar.copy, 1, 0, 1, slice(P // 2, P))
        round_late(nc.vector.tensor_copy, 1, 0, 1, slice(0, P // 2))
        round_late(nc.scalar.copy, 1, 2, 2)
        round_late(nc.vector.tensor_copy, 1, 1, 1)
        nc.scalar.copy(out=w2_dealt_first[:].bitcast(U16), in_=w2_raw[:].bitcast(U16).rearrange("p (m t) -> p t m", t=PACK)[:, 0])
        quantise_w1(1, 0, 1)
        quantise_w1(1, 1, 1)
        quantise_w1(1, 2, 2)
        nc.gpsimd.tensor_copy(
            out=w2_scale_dealt[:].rearrange("p (t m) -> p t m", t=PACK),
            in_=w2_scale_raw[:].rearrange("p (m t) -> p t m", t=PACK),
        )

        pieces = [(0, 0, HALF), (0, HALF, HALF)] + [(t, 0, S) for t in range(1, PACK)]
        y_ps = [bank_tile([P, count], "y_ps%d" % i, i + 1) for i, (t, first, count) in enumerate(pieces)]
        y_piece = {t: i for i, (t, first, count) in enumerate(pieces)}

        def first_product(i, g, start):
            t, first, count = pieces[i]
            cols = slice(P * t, P * (t + 1))
            nc.tensor.matmul_mx(
                out=y_ps[i][:],
                lhsT=w1_codes[g][:, cols].bitcast(FP8X4),
                lhsT_scale=w1_scales[g][:, cols],
                rhs=x_codes[g][:, first : first + count].bitcast(FP8X4),
                rhs_scale=x_picked_scales[4 * g : P, first : first + count],
                start=start,
                stop=not start,
            )

        for g in range(PASSES):
            for i in range(len(pieces)):
                first_product(i, g, g == 0)

        y_window = [tile([P, 2 * S], F32, "y_window%d" % t) for t in range(PACK)]
        y = [y_window[t][:, 0:S] for t in range(PACK)]
        for t in range(PACK):
            nc.gpsimd.memset(y_window[t][:, S : 2 * S], 0.0)
        near = {(name, t): tile([P, S], F32, "near_%s_%d" % (name, t)) for name in ("p1", "p2") for t in range(PACK)}
        h = [tile([P, S], F32, "h%d" % t) for t in range(PACK)]

        h_all = tile([P, PACK, S], F32, "h_all")

        def gather_vector(dst, window):
            nc.vector.tensor_copy(dst, window)

        def gather_scalar(dst, window):
            nc.scalar.activation(dst, window, COPY)

        def empty_y(t):
            nc.scalar.activation(y[t], y_ps[y_piece[t]][:], RELU)

        def fetch_near(gather, name, t):
            gather(near[name, t][:], y_window[t][:].indirect(lists[name][:]))

        def min_with_own(name, t):
            nc.vector.tensor_tensor(near[name, t][:], near[name, t][:], y[t], MIN)

        def make_h(t):
            nc.vector.tensor_tensor(h[t][:], near["p1", t][:], near["p2", t][:], MIN)
            nc.sync.dma_start(out=h_all[:, t, :], in_=h[t][:])

        spans = [(0, HALF), (HALF, CHUNK), (HALF + CHUNK, CHUNK)]
        FIRST, MIDDLE, LAST = range(len(spans))
        far1 = [tile([P, PACK, HALF], BF16, "far1_first"), tile([P, PACK, HALF], BF16, "far1_second", tag="near_p1_3")]
        far2_tags = [None, "near_p2_3", "near_p2_2"]
        far2 = [tile([P, PACK, count], BF16, "far2_%d" % first, tag=far2_tags[i]) for i, (first, count) in enumerate(spans)]
        high_tags = ["high_first", None, "high_first"]
        high = [tile([P, PACK, count], BF16, "high%d" % first, tag=high_tags[i]) for i, (first, count) in enumerate(spans)]
        z_woven = [tile([P, PACK * count], BF16, "z_woven%d" % first) for first, count in spans]
        out_woven = [tile([P, PACK * count], BF16, "out_woven%d" % first) for first, count in spans]
        z_codes = [tile([P, count], U32, "z_codes%d" % first) for first, count in spans]
        z_scales = [tile([P, count], U8, "z_scales%d" % first) for first, count in spans]
        out_f32 = [tile([P, PACK, count], F32, "out_f32_%d" % first) for first, count in spans]
        out_codes = tile([P, S], U32, "out_codes")
        out_scales = tile([P, S], U8, "out_scales")
        out_rows = out_0.rearrange("(p t) j -> p t j", t=PACK)
        out_words = out_1[0].rearrange("p c r -> p (c r)").bitcast(I32)

        def fetch_far1(gather, half, t):
            gather(far1[half][:, t, :], h[t][:].indirect(entries("q1", half * HALF, HALF)))

        def fetch_far2(gather, span, t):
            first, count = spans[span]
            gather(far2[span][:, t, :], h[t][:].indirect(entries("q2", first, count)))

        def far1_span(span):
            first, count = spans[span]
            half, lo = divmod(first, HALF)
            return far1[half][:, :, lo : lo + count]

        def own_span(span):
            first, count = spans[span]
            return h_all[:, :, first : first + count]

        def make_high(span, other):
            nc.vector.tensor_tensor(high[span][:], far1_span(span), other, MAX)

        def woven(dst, run):
            return dst.rearrange("p (n i t) -> p n t i", i=run, t=PACK)

        def planar(src, run):
            return src.rearrange("p t (n i) -> p n t i", i=run)

        def make_z(span, other, lo=0):
            cols = slice(lo, lo + CHUNK)
            nc.vector.tensor_tensor(
                woven(z_woven[span][:, PACK * lo : PACK * (lo + CHUNK)], 4),
                planar(high[span][:, :, cols], 4),
                planar(other[:, :, cols], 4),
                MAX,
            )

        def quantise_z(span, lo=0):
            cols = slice(lo, lo + CHUNK)
            nc.vector.quantize_mx(
                out=z_codes[span][:, cols].bitcast(FP8X4),
                scales=z_scales[span][:, cols],
                in_=z_woven[span][:, PACK * lo : PACK * (lo + CHUNK)],
            )

        def chunk_product(span, lo, bank):
            acc = bank_tile([P, PACK, CHUNK], "out_ps%d_%d_%d" % (span, lo, bank), bank)
            for t in range(PACK):
                nc.tensor.matmul_mx(
                    out=acc[:, t, :],
                    lhsT=w2_dealt[t].bitcast(FP4X4),
                    lhsT_scale=w2_scale_dealt[:, P * t : P * (t + 1)],
                    rhs=z_codes[span][:, lo : lo + CHUNK].bitcast(FP8X4),
                    rhs_scale=z_scales[span][:, lo : lo + CHUNK],
                    start=True,
                    stop=True,
                )
            return acc

        def round_chunk(copy, span, lo, src):
            copy(out=woven(out_woven[span][:, PACK * lo : PACK * (lo + CHUNK)], 4), in_=planar(src, 4))

        def copy_chunk(span, lo, acc):
            nc.scalar.copy(out=out_f32[span][:, :, lo : lo + CHUNK], in_=acc[:])

        def store_rows(span, lo):
            first = spans[span][0] + lo
            nc.sync.dma_start(out=out_rows[:, :, first : first + CHUNK], in_=out_f32[span][:, :, lo : lo + CHUNK])

        def planes(span):
            first, count = spans[span]
            cols = slice(first, first + count)
            nc.vector.quantize_mx(out=out_codes[:, cols].bitcast(FP8X4), scales=out_scales[:, cols], in_=out_woven[span][:])

        def store_words(first, count):
            cols = slice(first, first + count)
            nc.sync.dma_start(out=out_words[:, cols], in_=out_codes[:, cols].bitcast(I32))

        V, A = gather_vector, gather_scalar
        nc.scalar.activation(y[0][:, 0:HALF], y_ps[0][:], RELU)
        nc.vector.tensor_scalar_max(y[0][:, HALF:S], y_ps[1][:], 0.0)
        empty_y(1)
        fetch_near(V, "p1", 0)
        fetch_near(A, "p2", 0)
        fetch_near(V, "p1", 1)
        empty_y(2)
        fetch_near(A, "p2", 1)
        min_with_own("p1", 0)
        min_with_own("p1", 1)
        make_h(0)
        empty_y(3)
        fetch_near(A, "p2", 2)
        make_h(1)
        fetch_near(V, "p1", 2)
        fetch_near(A, "p2", 3)
        min_with_own("p2", 2)
        fetch_near(A, "p1", 3)
        min_with_own("p2", 3)
        make_h(2)
        make_h(3)
        nc.gpsimd.tensor_copy(
            out=w2_dealt_rest[:].rearrange("p t (m b) -> p t m b", b=2),
            in_=w2_raw[:].rearrange("p (m t b) -> p t m b", t=PACK, b=2)[:, 1:PACK],
        )
        for t in range(2):
            fetch_far1(A, 0, t)
            fetch_far2(A, FIRST, t)
        for t in range(2, PACK):
            fetch_far1(V, 0, t)
            fetch_far2(V, FIRST, t)
        for t in range(PACK):
            fetch_far1(A, 1, t)
        make_high(FIRST, far2[FIRST][:])
        fetch_far2(V, LAST, 3)
        fetch_far2(V, LAST, 1)
        for lo in (0, CHUNK):
            make_z(FIRST, own_span(FIRST), lo)
        for lo in (0, CHUNK):
            quantise_z(FIRST, lo)
        fetch_far2(V, LAST, 2)
        first_acc = [chunk_product(FIRST, lo, lo // CHUNK) for lo in (0, CHUNK)]
        again_acc = chunk_product(FIRST, CHUNK, 4)
        fetch_far2(A, LAST, 0)
        for t in range(PACK):
            fetch_far2(A, MIDDLE, t)
        make_high(MIDDLE, own_span(MIDDLE))
        make_high(LAST, far2[LAST][:])
        make_z(MIDDLE, far2[MIDDLE][:])
        for n in range(2):
            copy_chunk(FIRST, n * CHUNK, first_acc[n])
            store_rows(FIRST, n * CHUNK)
        round_chunk(nc.scalar.copy, FIRST, CHUNK, again_acc[:])
        make_z(LAST, own_span(LAST))
        quantise_z(MIDDLE)
        middle_acc = chunk_product(MIDDLE, 0, 2)
        quantise_z(LAST)
        last_acc = chunk_product(LAST, 0, 3)
        round_chunk(nc.vector.tensor_copy, FIRST, 0, out_f32[FIRST][:, :, 0:CHUNK])
        copy_chunk(MIDDLE, 0, middle_acc)
        store_rows(MIDDLE, 0)
        planes(FIRST)
        copy_chunk(LAST, 0, last_acc)
        store_rows(LAST, 0)
        round_chunk(nc.scalar.copy, LAST, 0, last_acc[:])
        round_chunk(nc.vector.tensor_copy, MIDDLE, 0, out_f32[MIDDLE][:])
        planes(MIDDLE)
        store_words(0, spans[LAST][0])
        planes(LAST)
        store_words(*spans[LAST])
        for quad in range(QUADS):
            queue = nc.scalar if quad % 2 else nc.sync
            queue.dma_start(
                out=out_2[0, 4 * quad : 4 * quad + 4, :].bitcast(I32),
                in_=out_scales[32 * quad : 32 * quad + 4, :].bitcast(I32),
            )
